import numpy as np
import ml_dtypes


def mxq(x, axis, fmt="e4m3"):
    dtype, down = {"e4m3": (ml_dtypes.float8_e4m3fn, 7), "e5m2": (ml_dtypes.float8_e5m2, 14)}[fmt]
    v = np.moveaxis(np.asarray(x, np.float32).astype(ml_dtypes.bfloat16).astype(np.float64), axis, -1)
    blocks = v.reshape(v.shape[:-1] + (-1, 32))
    amax = np.abs(blocks).max(-1, keepdims=True)
    byte = np.maximum(np.where(amax > 0, np.frexp(amax)[1] - 1 + 127, 0) - down, 1)
    scale = np.exp2(byte - 127.0)
    codes = (blocks / scale).astype(np.float32).astype(dtype).astype(np.float64)
    return np.moveaxis((codes * scale).reshape(v.shape), -1, axis)


WIDE = False


def mx_kscale(k):
    if not WIDE:
        return np.ones(k)
    levels = np.array([10, -10, 5, -5, 0])
    if k % 512:
        return np.exp2(np.random.permutation(np.resize(levels, k // 32))).repeat(32)
    a = np.empty((k // 512, 16))
    for p in range(k // 512):
        a[p, :8] = np.random.permutation(np.resize(levels, 8))
        for g in range(8):
            far = levels[np.abs(levels - a[p, g]) >= 10]
            a[p, g + 8] = far[np.random.randint(len(far))]
    return np.exp2(a.ravel()).repeat(32)


def f64(x):
    return np.asarray(x).astype(np.float64)


def striped(idx):
    return np.tile(idx.reshape(-1, 16).T, (8, 1)).astype(np.uint16)


def unstriped(offs):
    return offs[:16].T.reshape(-1).astype(np.int64)


E2M1 = np.array([0.0, 0.5, 1.0, 1.5, 2.0, 3.0, 4.0, 6.0, -0.0, -0.5, -1.0, -1.5, -2.0, -3.0, -4.0, -6.0])


def pack_weight(w, fmt):
    k, n = w.shape
    w = f64(np.asarray(w, np.float32).astype(ml_dtypes.bfloat16)).reshape(k // 32, 32, n)
    amax = np.abs(w).max(1)
    if fmt == "e4m3":
        byte = np.frexp(amax)[1] - 1 + 127 - 7
    else:
        mant, ex = np.frexp(amax / 6.0)
        byte = np.where(mant > 0.5, ex, ex - 1) + 127
    byte = np.clip(np.where(amax > 0, byte, 1), 1, 254)
    scaled = (w * np.exp2(127.0 - byte)[:, None, :]).reshape(k, n).astype(np.float32)
    by_word = np.ascontiguousarray(scaled.reshape(k // 512, 128, 4, n).transpose(0, 1, 3, 2))
    if fmt == "e4m3":
        words = by_word.astype(ml_dtypes.float8_e4m3fn).view(np.uint8)
    else:
        c = by_word.astype(ml_dtypes.float4_e2m1fn).view(np.uint8) & 0xF
        words = (c[..., 0::2] | (c[..., 1::2] << 4)).reshape(k // 512, 128, 2 * n)
    return np.ascontiguousarray(words), np.ascontiguousarray(byte.astype(np.uint8).reshape(k // 512, 16, n))


def unpack_weight(words, scales, fmt):
    g, _, n = scales.shape
    words = np.ascontiguousarray(words).reshape(g, 128, n, -1)
    if fmt == "e4m3":
        vals = words.view(ml_dtypes.float8_e4m3fn).astype(np.float64)
    else:
        nib = np.empty((g, 128, n, 4), np.uint8)
        nib[..., 0::2] = words & 0xF
        nib[..., 1::2] = words >> 4
        vals = E2M1[nib]
    vals = vals * np.repeat(np.exp2(scales.astype(np.float64) - 127.0), 8, axis=1)[..., None]
    return vals.transpose(0, 1, 3, 2).reshape(g * 512, n)


def gelu(v):
    return 0.5 * v * (1.0 + np.tanh(np.sqrt(2.0 / np.pi) * (v + 0.044715 * v**3)))


def often(T, S):
    return np.random.permutation(T)[(T * np.random.uniform(0, 1, S) ** 4).astype(np.int64)]


K, K2, H, N, T, T2, S, P = 1024, 1536, 1024, 768, 4096, 2048, 1024, 512

def setup_inputs():
    n = np.random.standard_normal
    s = mx_kscale(K)[:, None]
    s2 = mx_kscale(K2)[:, None]
    u = mx_kscale(H)[:, None]
    tab_words, tab_scales = pack_weight(n((K, T)) * s, "e4m3")
    tab2_words, tab2_scales = pack_weight(n((K2, T2)) * s2, "e4m3")
    w4_words, w4_scales = pack_weight(n((K2, H)) / np.sqrt(K2) / s2 * u.T, "e2m1")
    w8_words, w8_scales = pack_weight(2.0 * n((H, N)) / np.sqrt(H) / u, "e4m3")
    return {
        "tab_words": tab_words, "tab_scales": tab_scales,
        "offs": striped(np.random.permutation(T)[:S]),
        "pos1": striped(often(S, P)),
        "tab2_words": tab2_words, "tab2_scales": tab2_scales,
        "offs2": striped(np.random.permutation(T2)[:P]),
        "w1": (n((K, H)) / np.sqrt(K) / s).astype(np.float32),
        "w4_words": w4_words, "w4_scales": w4_scales,
        "w8_words": w8_words, "w8_scales": w8_scales,
        "b2": (0.5 * n(H) * u[:, 0]).astype(np.float32),
        "kap": np.random.uniform(0.5, 1.5, H).astype(np.float32),
        "b3": (0.5 * n(N)).astype(np.float32),
    }

def reference(tab_words, tab_scales, offs, pos1, tab2_words, tab2_scales, offs2, w1, w4_words, w4_scales, w8_words, w8_scales, b2, kap, b3):
    v = unpack_weight(tab_words, tab_scales, "e4m3")[:, unstriped(offs)]
    h = mxq(f64(w1), 0, "e4m3").T @ v
    a = h[:, unstriped(pos1)]
    v2 = unpack_weight(tab2_words, tab2_scales, "e4m3")[:, unstriped(offs2)]
    b = unpack_weight(w4_words, w4_scales, "e2m1").T @ v2
    top = np.maximum(b + f64(b2)[:, None], 0.0)
    z = top / (f64(kap)[:, None] + np.square(a))
    y = unpack_weight(w8_words, w8_scales, "e4m3").T @ mxq(z, 0, "e4m3")
    return y + f64(b3)[:, None]

@@ -1,0 +1,286 @@
+from contextlib import ExitStack
+
+import concourse.mybir as mybir
+
+K, K2, H, N, T, T2, S, M = 1024, 1536, 1024, 768, 4096, 2048, 1024, 512
+FLOPS = 2 * (K * H * S + K2 * H * M + H * N * M)
+
+F32 = mybir.dt.float32
+BF16 = mybir.dt.bfloat16
+I32 = mybir.dt.int32
+U32 = mybir.dt.uint32
+U16 = mybir.dt.uint16
+U8 = mybir.dt.uint8
+FP8X4 = mybir.dt.float8_e4m3fn_x4
+FP4X4 = mybir.dt.float4_e2m1fn_x4
+ACT = mybir.ActivationFunctionType
+ALU = mybir.AluOpType
+
+P = 128
+PACK = 4
+PASS = P * PACK
+BANK = 512
+SHIFT_ROWS = 112
+
+
+def tile_list_subcatchment_nitrate_loads_kernel(
+    tc, tab_words, tab_scales, offs, pos1, tab2_words, tab2_scales, offs2, w1,
+    w4_words, w4_scales, w8_words, w8_scales, b2, kap, b3, out
+):
+    nc = tc.nc
+    n1, n2, n3 = K // PASS, K2 // PASS, H // PASS
+    with ExitStack() as ctx:
+        lists = ctx.enter_context(tc.tile_pool(name="lists", bufs=1))
+        keep = ctx.enter_context(tc.tile_pool(name="keep", bufs=1))
+        ring = ctx.enter_context(tc.tile_pool(name="ring", bufs=2))
+        hpool = ctx.enter_context(tc.tile_pool(name="hpool", bufs=6))
+        psum = ctx.enter_context(tc.psum_pool(name="psum", bufs=1))
+
+        def bank(i):
+            return psum.tile([P, BANK], F32, name="bank%d" % i)
+
+        def load_words(name, src):
+            t = keep.tile([P, src.shape[1]], I32, name=name, align_bytes=64)
+            nc.sync.dma_start(out=t[:], in_=src.rearrange("p n t -> p (n t)").bitcast(I32))
+            return t
+
+        def load_scale_rows(queue, dst, src, first):
+            passes = src.shape[0]
+            for q in range(4):
+                queue.dma_start(
+                    out=dst[32 * q + first : 32 * q + first + 4 * passes, :].bitcast(I32),
+                    in_=src[:, 4 * q : 4 * q + 4, :].bitcast(I32),
+                )
+
+        def load_scale_rows_of_pass(dst, src, first, a):
+            for q in range(4):
+                row = 32 * q + first + 4 * a
+                nc.sync.dma_start(out=dst[row : row + 4, :].bitcast(I32), in_=src[a, 4 * q : 4 * q + 4, :].bitcast(I32))
+
+        tab_s = keep.tile([P, T], U8, name="tab_s", align_bytes=64)
+        w4_s_raw = keep.tile([P, H], U8, name="w4_s_raw", align_bytes=64)
+        tab2_s = keep.tile([P, T2], U8, name="tab2_s", align_bytes=64)
+        w8_s = keep.tile([P, N], U8, name="w8_s", align_bytes=64)
+        nc.vector.memset(tab_s[:].bitcast(I32), 0)
+        nc.vector.memset(w4_s_raw[:].bitcast(I32), 0)
+        nc.vector.memset(tab2_s[:].bitcast(I32), 0)
+
+        def load_w1(a, b):
+            raw = keep.tile([P, PACK, PASS], F32, name="w1_raw%d%d" % (a, b))
+            nc.sync.dma_start(
+                out=raw[:],
+                in_=w1[a * PASS : (a + 1) * PASS, b * PASS : (b + 1) * PASS].rearrange("(p j) c -> p j c", j=PACK),
+            )
+            return raw
+
+        offs_t = lists.tile([P, S // 16], U16, name="offs_t")
+        pos_t = lists.tile([P, M // 16], U16, name="pos_t")
+        offs2_t = lists.tile([P, M // 16], U16, name="offs2_t")
+        kap_t = keep.tile([P, n3, PACK], F32, name="kap_t")
+        b2_t = keep.tile([P, n3, PACK], F32, name="b2_t")
+        b3_t = keep.tile([P, N // P], F32, name="b3_t")
+        warm = keep.tile([P, 1], F32, name="warm")
+        w4_raw = keep.tile([P, n2, H // 2], I32, name="w4_raw", align_bytes=64)
+        w8_w = keep.tile([P, n3, N], I32, name="w8_w", align_bytes=64)
+
+        nc.gpsimd.dma_start(out=kap_t[:], in_=kap.rearrange("(b p t) -> p b t", p=P, t=PACK))
+        nc.scalar.activation(warm[:], kap_t[:, 0, 0:1], ACT.Abs_reciprocal_sqrt)
+        nc.gpsimd.dma_start(out=b2_t[:], in_=b2.rearrange("(b p t) -> p b t", p=P, t=PACK))
+        with nc.allow_non_contiguous_dma(reason="one bias value a partition"):
+            nc.gpsimd.dma_start(out=b3_t[:], in_=b3.rearrange("(c p) -> p c", p=P))
+        tab_w = [load_words("tab_w0", tab_words[0])]
+        load_scale_rows_of_pass(tab_s, tab_scales, 8, 0)
+        nc.sync.dma_start(offs_t[:], offs)
+        nc.sync.dma_start(out=w4_raw[:], in_=w4_words.rearrange("a p n -> p a n").bitcast(I32))
+        tab_w.append(load_words("tab_w1", tab_words[1]))
+        load_scale_rows_of_pass(tab_s, tab_scales, 8, 1)
+        w1_raw = {(0, 0): load_w1(0, 0), (1, 0): load_w1(1, 0)}
+        nc.sync.dma_start(pos_t[:], pos1)
+        w1_raw[0, 1] = load_w1(0, 1)
+        load_scale_rows(nc.sync, w4_s_raw, w4_scales, 0)
+        w1_raw[1, 1] = load_w1(1, 1)
+        nc.sync.dma_start(offs2_t[:], offs2)
+        load_scale_rows(nc.sync, tab2_s, tab2_scales, 0)
+        tab2_w = [load_words("tab2_w%d" % a, tab2_words[a]) for a in range(n2)]
+        load_scale_rows(nc.sync, w8_s, w8_scales, 0)
+        nc.sync.dma_start(out=w8_w[:], in_=w8_words.rearrange("a p n t -> p a (n t)").bitcast(I32))
+
+        w4_w = keep.tile([P, n2, 2 * H], U8, name="w4_w", align_bytes=64)
+        nc.vector.tensor_copy(
+            out=w4_w[:].bitcast(U16).rearrange("p a (b t m) -> p (a b) m t", t=PACK, m=P),
+            in_=w4_raw[:].bitcast(U16).rearrange("p a (b m t) -> p (a b) m t", t=PACK, m=P),
+        )
+        w4_s = [keep.tile([P, H], U8, name="w4_s%d" % a, align_bytes=64) for a in range(n2)]
+
+        v_s = keep.tile([P, S], U8, name="v_s", align_bytes=64)
+        v_w = [keep.tile([P, S], U32, name="v_w%d" % a, align_bytes=64) for a in range(n1)]
+        v2_s = [keep.tile([P, M], U8, name="v2_s%d" % a, align_bytes=64) for a in range(n2)]
+        nc.vector.tensor_copy(v_w[0][:], tab_w[0][:].bitcast(U32).indirect(offs_t[:]))
+        nc.vector.tensor_copy(v_s[:], tab_s[:].indirect(offs_t[:]))
+        nc.vector.tensor_copy(v_w[1][:], tab_w[1][:].bitcast(U32).indirect(offs_t[:]))
+
+        def shift_planes(planes):
+            for a in range(1, n2):
+                nc.gpsimd.dma_start(
+                    out=planes[a][0:SHIFT_ROWS, :].bitcast(I32),
+                    in_=planes[0][4 * a : 4 * a + SHIFT_ROWS, :].bitcast(I32),
+                )
+
+        w1_w, w1_s = {}, {}
+
+        def quantise_w1(a, b, vector_share):
+            grouped = ring.tile([P, PACK, P, PACK], BF16, name="w1_grouped", align_bytes=64)
+            src = w1_raw[a, b][:].rearrange("p j (m t) -> p m j t", t=PACK)
+            dst = grouped[:].rearrange("p t m j -> p m j t")
+            if vector_share > 0:
+                nc.vector.tensor_copy(out=dst[:, 0:vector_share], in_=src[:, 0:vector_share])
+            if vector_share < P:
+                nc.scalar.copy(out=dst[:, vector_share:P], in_=src[:, vector_share:P])
+            w1_w[a, b] = keep.tile([P, PASS], U32, name="w1_w%d%d" % (a, b), align_bytes=64)
+            w1_s[a, b] = keep.tile([P, PASS], U8, name="w1_s%d%d" % (a, b), align_bytes=64)
+            nc.vector.quantize_mx(
+                out=w1_w[a, b][:].bitcast(FP8X4), scales=w1_s[a, b][:],
+                in_=grouped[:].rearrange("p t m j -> p (t m j)"),
+            )
+
+        half = M // 2
+        units = [(0, 0, M), (1, 0, half), (1, half, half)]
+        picked = {u: keep.tile([P, PACK, u[2]], F32, name="picked%d_%d" % u[:2]) for u in units}
+        h = {}
+
+        def basin_stage(b, t):
+            h[b, t] = hpool.tile([P, S], F32, name="h")
+            cols = slice(t * P, (t + 1) * P)
+            for u in range(S // BANK):
+                acc = bank((2 * t + u) % 4)
+                run = slice(u * BANK, (u + 1) * BANK)
+                for a in range(n1):
+                    nc.tensor.matmul_mx(
+                        out=acc[:], lhsT=w1_w[a, b][:, cols].bitcast(FP8X4), lhsT_scale=w1_s[a, b][:, cols],
+                        rhs=v_w[a][:, run].bitcast(FP8X4), rhs_scale=v_s[8 + 4 * a : P, run],
+                        start=(a == 0), stop=(a == n1 - 1),
+                    )
+                nc.scalar.copy(out=h[b, t][:, run], in_=acc[:])
+
+        def pick_stage(unit, t):
+            b, m0, width = unit
+            nc.vector.tensor_copy(picked[unit][:, t, :], h[b, t][:].indirect(pos_t[:, m0 // 16 : (m0 + width) // 16]))
+
+        def reciprocal_stage(unit, t):
+            x = picked[unit][:, t, :]
+            nc.scalar.activation(x, x, ACT.Square)
+            nc.scalar.activation(x, x, ACT.Abs_reciprocal_sqrt, bias=kap_t[:, unit[0], t : t + 1])
+            nc.scalar.activation(x, x, ACT.Square)
+
+        v2_w = [keep.tile([P, M], U32, name="v2_w%d" % a, align_bytes=64) for a in range(n2)]
+        own = {}
+
+        def own_stage(b, t):
+            own[b, t] = bank(4 + t)
+            c0 = b * PASS + t * P
+            for a in range(n2):
+                nc.tensor.matmul_mx(
+                    out=own[b, t][:], lhsT=w4_w[:, a, 2 * c0 : 2 * (c0 + P)].bitcast(FP4X4), lhsT_scale=w4_s[a][:, c0 : c0 + P],
+                    rhs=v2_w[a][:].bitcast(FP8X4), rhs_scale=v2_s[a][:],
+                    start=(a == 0), stop=(a == n2 - 1),
+                )
+
+        def ratio_stage(unit, t):
+            b, m0, width = unit
+            x = picked[unit][:, t, :]
+            nc.vector.scalar_tensor_tensor(
+                out=x, in0=own[b, t][:, m0 : m0 + width], scalar=b2_t[:, b, t : t + 1], in1=x, op0=ALU.add, op1=ALU.mult
+            )
+
+        z_w = [keep.tile([P, M], U32, name="z_w%d" % b, align_bytes=64) for b in range(n3)]
+        z_s = [keep.tile([P, M], U8, name="z_s%d" % b, align_bytes=64) for b in range(n3)]
+
+        def quantise_z(unit):
+            b, m0, width = unit
+            grouped = keep.tile([P, width, PACK], BF16, name="z_grouped%d_%d" % unit[:2], align_bytes=64)
+            nc.vector.tensor_scalar_max(
+                out=grouped[:].rearrange("p (c i) t -> p c t i", i=4),
+                in0=picked[unit][:].rearrange("p t (c i) -> p c t i", i=4),
+                scalar1=0.0,
+            )
+            nc.vector.quantize_mx(
+                out=z_w[b][:, m0 : m0 + width].bitcast(FP8X4), scales=z_s[b][:, m0 : m0 + width],
+                in_=grouped[:].rearrange("p m t -> p (m t)"),
+            )
+
+        score = {}
+
+        def score_pass(u, pair, b):
+            if b == 0:
+                score[u, pair] = bank(3 * u + pair)
+            run = slice(u * half, (u + 1) * half)
+            for j in range(2):
+                c = 2 * pair + j
+                cols = slice(c * P, (c + 1) * P)
+                nc.tensor.matmul_mx(
+                    out=score[u, pair][:, j * half : (j + 1) * half],
+                    lhsT=w8_w[:, b, cols].bitcast(FP8X4), lhsT_scale=w8_s[4 * b : P, cols],
+                    rhs=z_w[b][:, run].bitcast(FP8X4), rhs_scale=z_s[b][:, run],
+                    start=(b == 0 and j == 0), stop=(b == n3 - 1 and j == 1),
+                )
+
+        def finish(u, pair, on_scalar):
+            res = keep.tile([P, 2, half], F32, name="res%d_%d" % (u, pair))
+            for j in range(2):
+                c = 2 * pair + j
+                src = score[u, pair][:, j * half : (j + 1) * half]
+                if on_scalar:
+                    nc.scalar.activation(res[:, j, :], src, ACT.Identity, bias=b3_t[:, c : c + 1])
+                else:
+                    nc.vector.tensor_scalar_add(out=res[:, j, :], in0=src, scalar1=b3_t[:, c : c + 1])
+            nc.sync.dma_start(
+                out=out[2 * pair * P : 2 * (pair + 1) * P, u * half : (u + 1) * half].rearrange("(j p) m -> p j m", p=P),
+                in_=res[:],
+            )
+
+        quantise_w1(0, 0, 0)
+        quantise_w1(1, 0, 80)
+        for t in range(PACK):
+            basin_stage(0, t)
+            pick_stage(units[0], t)
+        quantise_w1(0, 1, P)
+        quantise_w1(1, 1, P)
+        nc.vector.tensor_copy(
+            out=w4_s[0][:].rearrange("p (b t m) -> p b m t", t=PACK, m=P),
+            in_=w4_s_raw[:].rearrange("p (b m t) -> p b m t", t=PACK, m=P),
+        )
+        shift_planes(w4_s)
+        nc.vector.tensor_copy(v2_s[0][:], tab2_s[:].indirect(offs2_t[:]))
+        shift_planes(v2_s)
+        for t in range(PACK):
+            reciprocal_stage(units[0], t)
+            basin_stage(1, t)
+            pick_stage(units[1], t)
+        for a in range(n2):
+            nc.vector.tensor_copy(v2_w[a][:], tab2_w[a][:].bitcast(U32).indirect(offs2_t[:]))
+        for t in range(PACK):
+            pick_stage(units[2], t)
+            own_stage(0, t)
+            ratio_stage(units[0], t)
+            reciprocal_stage(units[1], t)
+        quantise_z(units[0])
+        for pair in range(3):
+            score_pass(0, pair, 0)
+        score_pass(1, 0, 0)
+        for t in range(PACK):
+            own_stage(1, t)
+            ratio_stage(units[1], t)
+            reciprocal_stage(units[2], t)
+        quantise_z(units[1])
+        for pair in range(3):
+            score_pass(0, pair, 1)
+        for t in range(PACK):
+            ratio_stage(units[2], t)
+        for pair in range(1, 3):
+            score_pass(1, pair, 0)
+        quantise_z(units[2])
+        for pair in range(3):
+            finish(0, pair, True)
+        for pair in range(3):
+            score_pass(1, pair, 1)
+            finish(1, pair, pair == 1)

@@ -52,18 +52,13 @@ def tile_list_subcatchment_nitrate_loads_kernel(
                     in_=src[:, 4 * q : 4 * q + 4, :].bitcast(I32),
                 )
 
-        def load_scale_rows_of_pass(dst, src, first, a):
-            for q in range(4):
-                row = 32 * q + first + 4 * a
-                nc.sync.dma_start(out=dst[row : row + 4, :].bitcast(I32), in_=src[a, 4 * q : 4 * q + 4, :].bitcast(I32))
-
         tab_s = keep.tile([P, T], U8, name="tab_s", align_bytes=64)
         w4_s_raw = keep.tile([P, H], U8, name="w4_s_raw", align_bytes=64)
         tab2_s = keep.tile([P, T2], U8, name="tab2_s", align_bytes=64)
         w8_s = keep.tile([P, N], U8, name="w8_s", align_bytes=64)
         nc.vector.memset(tab_s[:].bitcast(I32), 0)
-        nc.vector.memset(w4_s_raw[:].bitcast(I32), 0)
         nc.vector.memset(tab2_s[:].bitcast(I32), 0)
+        nc.vector.memset(w4_s_raw[:].bitcast(I32), 0)
 
         def load_w1(a, b):
             raw = keep.tile([P, PACK, PASS], F32, name="w1_raw%d%d" % (a, b))
@@ -83,27 +78,26 @@ def tile_list_subcatchment_nitrate_loads_kernel(
         w4_raw = keep.tile([P, n2, H // 2], I32, name="w4_raw", align_bytes=64)
         w8_w = keep.tile([P, n3, N], I32, name="w8_w", align_bytes=64)
 
-        nc.gpsimd.dma_start(out=kap_t[:], in_=kap.rearrange("(b p t) -> p b t", p=P, t=PACK))
+        load_scale_rows(nc.gpsimd, tab_s, tab_scales, 8)
+        load_scale_rows(nc.gpsimd, tab2_s, tab2_scales, 0)
+        load_scale_rows(nc.gpsimd, w4_s_raw, w4_scales, 0)
+        nc.scalar.dma_start(out=kap_t[:], in_=kap.rearrange("(b p t) -> p b t", p=P, t=PACK))
         nc.scalar.activation(warm[:], kap_t[:, 0, 0:1], ACT.Abs_reciprocal_sqrt)
-        nc.gpsimd.dma_start(out=b2_t[:], in_=b2.rearrange("(b p t) -> p b t", p=P, t=PACK))
-        with nc.allow_non_contiguous_dma(reason="one bias value a partition"):
-            nc.gpsimd.dma_start(out=b3_t[:], in_=b3.rearrange("(c p) -> p c", p=P))
         tab_w = [load_words("tab_w0", tab_words[0])]
-        load_scale_rows_of_pass(tab_s, tab_scales, 8, 0)
         nc.sync.dma_start(offs_t[:], offs)
+        nc.sync.dma_start(offs2_t[:], offs2)
         nc.sync.dma_start(out=w4_raw[:], in_=w4_words.rearrange("a p n -> p a n").bitcast(I32))
         tab_w.append(load_words("tab_w1", tab_words[1]))
-        load_scale_rows_of_pass(tab_s, tab_scales, 8, 1)
         w1_raw = {(0, 0): load_w1(0, 0), (1, 0): load_w1(1, 0)}
         nc.sync.dma_start(pos_t[:], pos1)
         w1_raw[0, 1] = load_w1(0, 1)
-        load_scale_rows(nc.sync, w4_s_raw, w4_scales, 0)
         w1_raw[1, 1] = load_w1(1, 1)
-        nc.sync.dma_start(offs2_t[:], offs2)
-        load_scale_rows(nc.sync, tab2_s, tab2_scales, 0)
+        nc.sync.dma_start(out=b2_t[:], in_=b2.rearrange("(b p t) -> p b t", p=P, t=PACK))
         tab2_w = [load_words("tab2_w%d" % a, tab2_words[a]) for a in range(n2)]
-        load_scale_rows(nc.sync, w8_s, w8_scales, 0)
+        with nc.allow_non_contiguous_dma(reason="one bias value a partition"):
+            nc.sync.dma_start(out=b3_t[:], in_=b3.rearrange("(c p) -> p c", p=P))
         nc.sync.dma_start(out=w8_w[:], in_=w8_words.rearrange("a p n t -> p a (n t)").bitcast(I32))
+        load_scale_rows(nc.sync, w8_s, w8_scales, 0)
 
         w4_w = keep.tile([P, n2, 2 * H], U8, name="w4_w", align_bytes=64)
         nc.vector.tensor_copy(
@@ -152,7 +146,7 @@ def tile_list_subcatchment_nitrate_loads_kernel(
             h[b, t] = hpool.tile([P, S], F32, name="h")
             cols = slice(t * P, (t + 1) * P)
             for u in range(S // BANK):
-                acc = bank((2 * t + u) % 4)
+                acc = bank((2 * t + u) % (8 if b == 0 else 4))
                 run = slice(u * BANK, (u + 1) * BANK)
                 for a in range(n1):
                     nc.tensor.matmul_mx(
@@ -160,7 +154,10 @@ def tile_list_subcatchment_nitrate_loads_kernel(
                         rhs=v_w[a][:, run].bitcast(FP8X4), rhs_scale=v_s[8 + 4 * a : P, run],
                         start=(a == 0), stop=(a == n1 - 1),
                     )
-                nc.scalar.copy(out=h[b, t][:, run], in_=acc[:])
+                if (b, t, u) == (0, 0, 1):
+                    nc.vector.tensor_copy(out=h[b, t][:, run], in_=acc[:])
+                else:
+                    nc.scalar.copy(out=h[b, t][:, run], in_=acc[:])
 
         def pick_stage(unit, t):
             b, m0, width = unit
@@ -245,13 +242,13 @@ def tile_list_subcatchment_nitrate_loads_kernel(
             pick_stage(units[0], t)
         quantise_w1(0, 1, P)
         quantise_w1(1, 1, P)
+        nc.vector.tensor_copy(v2_s[0][:], tab2_s[:].indirect(offs2_t[:]))
+        shift_planes(v2_s)
         nc.vector.tensor_copy(
             out=w4_s[0][:].rearrange("p (b t m) -> p b m t", t=PACK, m=P),
             in_=w4_s_raw[:].rearrange("p (b m t) -> p b m t", t=PACK, m=P),
         )
         shift_planes(w4_s)
-        nc.vector.tensor_copy(v2_s[0][:], tab2_s[:].indirect(offs2_t[:]))
-        shift_planes(v2_s)
         for t in range(PACK):
             reciprocal_stage(units[0], t)
             basin_stage(1, t)

@@ -21,6 +21,12 @@ PACK = 4
 PASS = P * PACK
 BANK = 512
 SHIFT_ROWS = 112
+KIB = 1024
+AT_W1_10, AT_W1_00, AT_TAB2_S, AT_W4_S_RAW, AT_TAB1 = 0, 4 * KIB, 8 * KIB, 10 * KIB, 11 * KIB
+AT_TAB2 = (0, 11 * KIB, 21 * KIB)
+AT_V2_S, AT_W4_S = 19 * KIB, 20 * KIB
+AT_W1_01, AT_TAB0, AT_W1_11, AT_V_S, AT_W4 = 29 * KIB, 35 * KIB, 37 * KIB, 45 * KIB, 46 * KIB
+AT_TAB_S = 52 * KIB
 
 
 def tile_list_subcatchment_nitrate_loads_kernel(
@@ -33,14 +39,15 @@ def tile_list_subcatchment_nitrate_loads_kernel(
         lists = ctx.enter_context(tc.tile_pool(name="lists", bufs=1))
         keep = ctx.enter_context(tc.tile_pool(name="keep", bufs=1))
         ring = ctx.enter_context(tc.tile_pool(name="ring", bufs=2))
-        hpool = ctx.enter_context(tc.tile_pool(name="hpool", bufs=6))
+        hpool = ctx.enter_context(tc.tile_pool(name="hpool", bufs=8))
+        stage = ctx.enter_context(tc.tile_pool(name="stage", bufs=1))
         psum = ctx.enter_context(tc.psum_pool(name="psum", bufs=1))
 
         def bank(i):
             return psum.tile([P, BANK], F32, name="bank%d" % i)
 
-        def load_words(name, src):
-            t = keep.tile([P, src.shape[1]], I32, name=name, align_bytes=64)
+        def load_words(name, src, offset):
+            t = stage.tile([P, src.shape[1]], I32, name=name, align_bytes=64, offset=offset)
             nc.sync.dma_start(out=t[:], in_=src.rearrange("p n t -> p (n t)").bitcast(I32))
             return t
 
@@ -52,16 +59,11 @@ def tile_list_subcatchment_nitrate_loads_kernel(
                     in_=src[:, 4 * q : 4 * q + 4, :].bitcast(I32),
                 )
 
-        tab_s = keep.tile([P, T], U8, name="tab_s", align_bytes=64)
-        w4_s_raw = keep.tile([P, H], U8, name="w4_s_raw", align_bytes=64)
-        tab2_s = keep.tile([P, T2], U8, name="tab2_s", align_bytes=64)
-        w8_s = keep.tile([P, N], U8, name="w8_s", align_bytes=64)
+        tab_s = stage.tile([P, T], U8, name="tab_s", align_bytes=64, offset=AT_TAB_S)
         nc.vector.memset(tab_s[:].bitcast(I32), 0)
-        nc.vector.memset(tab2_s[:].bitcast(I32), 0)
-        nc.vector.memset(w4_s_raw[:].bitcast(I32), 0)
 
-        def load_w1(a, b):
-            raw = keep.tile([P, PACK, PASS], F32, name="w1_raw%d%d" % (a, b))
+        def load_w1(a, b, offset):
+            raw = stage.tile([P, PACK, PASS], F32, name="w1_raw%d%d" % (a, b), align_bytes=64, offset=offset)
             nc.sync.dma_start(
                 out=raw[:],
                 in_=w1[a * PASS : (a + 1) * PASS, b * PASS : (b + 1) * PASS].rearrange("(p j) c -> p j c", j=PACK),
@@ -75,43 +77,26 @@ def tile_list_subcatchment_nitrate_loads_kernel(
         b2_t = keep.tile([P, n3, PACK], F32, name="b2_t")
         b3_t = keep.tile([P, N // P], F32, name="b3_t")
         warm = keep.tile([P, 1], F32, name="warm")
-        w4_raw = keep.tile([P, n2, H // 2], I32, name="w4_raw", align_bytes=64)
-        w8_w = keep.tile([P, n3, N], I32, name="w8_w", align_bytes=64)
 
         load_scale_rows(nc.gpsimd, tab_s, tab_scales, 8)
-        load_scale_rows(nc.gpsimd, tab2_s, tab2_scales, 0)
-        load_scale_rows(nc.gpsimd, w4_s_raw, w4_scales, 0)
         nc.scalar.dma_start(out=kap_t[:], in_=kap.rearrange("(b p t) -> p b t", p=P, t=PACK))
         nc.scalar.activation(warm[:], kap_t[:, 0, 0:1], ACT.Abs_reciprocal_sqrt)
-        tab_w = [load_words("tab_w0", tab_words[0])]
         nc.sync.dma_start(offs_t[:], offs)
-        nc.sync.dma_start(offs2_t[:], offs2)
-        nc.sync.dma_start(out=w4_raw[:], in_=w4_words.rearrange("a p n -> p a n").bitcast(I32))
-        tab_w.append(load_words("tab_w1", tab_words[1]))
-        w1_raw = {(0, 0): load_w1(0, 0), (1, 0): load_w1(1, 0)}
+        w1_raw = {(0, 0): load_w1(0, 0, AT_W1_00)}
+        tab_w = [load_words("tab_w0", tab_words[0], AT_TAB0)]
         nc.sync.dma_start(pos_t[:], pos1)
-        w1_raw[0, 1] = load_w1(0, 1)
-        w1_raw[1, 1] = load_w1(1, 1)
+        nc.sync.dma_start(offs2_t[:], offs2)
         nc.sync.dma_start(out=b2_t[:], in_=b2.rearrange("(b p t) -> p b t", p=P, t=PACK))
-        tab2_w = [load_words("tab2_w%d" % a, tab2_words[a]) for a in range(n2)]
         with nc.allow_non_contiguous_dma(reason="one bias value a partition"):
             nc.sync.dma_start(out=b3_t[:], in_=b3.rearrange("(c p) -> p c", p=P))
-        nc.sync.dma_start(out=w8_w[:], in_=w8_words.rearrange("a p n t -> p a (n t)").bitcast(I32))
-        load_scale_rows(nc.sync, w8_s, w8_scales, 0)
 
         w4_w = keep.tile([P, n2, 2 * H], U8, name="w4_w", align_bytes=64)
-        nc.vector.tensor_copy(
-            out=w4_w[:].bitcast(U16).rearrange("p a (b t m) -> p (a b) m t", t=PACK, m=P),
-            in_=w4_raw[:].bitcast(U16).rearrange("p a (b m t) -> p (a b) m t", t=PACK, m=P),
-        )
-        w4_s = [keep.tile([P, H], U8, name="w4_s%d" % a, align_bytes=64) for a in range(n2)]
-
-        v_s = keep.tile([P, S], U8, name="v_s", align_bytes=64)
+        w4_s = [stage.tile([P, H], U8, name="w4_s0", align_bytes=64, offset=AT_W4_S)]
+        w4_s.extend(keep.tile([P, H], U8, name="w4_s%d" % a, align_bytes=64) for a in range(1, n2))
+        v_s = stage.tile([P, S], U8, name="v_s", align_bytes=64, offset=AT_V_S)
         v_w = [keep.tile([P, S], U32, name="v_w%d" % a, align_bytes=64) for a in range(n1)]
-        v2_s = [keep.tile([P, M], U8, name="v2_s%d" % a, align_bytes=64) for a in range(n2)]
-        nc.vector.tensor_copy(v_w[0][:], tab_w[0][:].bitcast(U32).indirect(offs_t[:]))
-        nc.vector.tensor_copy(v_s[:], tab_s[:].indirect(offs_t[:]))
-        nc.vector.tensor_copy(v_w[1][:], tab_w[1][:].bitcast(U32).indirect(offs_t[:]))
+        v2_s = [stage.tile([P, M], U8, name="v2_s0", align_bytes=64, offset=AT_V2_S)]
+        v2_s.extend(keep.tile([P, M], U8, name="v2_s%d" % a, align_bytes=64) for a in range(1, n2))
 
         def shift_planes(planes):
             for a in range(1, n2):
@@ -154,10 +139,7 @@ def tile_list_subcatchment_nitrate_loads_kernel(
                         rhs=v_w[a][:, run].bitcast(FP8X4), rhs_scale=v_s[8 + 4 * a : P, run],
                         start=(a == 0), stop=(a == n1 - 1),
                     )
-                if (b, t, u) == (0, 0, 1):
-                    nc.vector.tensor_copy(out=h[b, t][:, run], in_=acc[:])
-                else:
-                    nc.scalar.copy(out=h[b, t][:, run], in_=acc[:])
+                nc.scalar.copy(out=h[b, t][:, run], in_=acc[:])
 
         def pick_stage(unit, t):
             b, m0, width = unit
@@ -236,12 +218,43 @@ def tile_list_subcatchment_nitrate_loads_kernel(
             )
 
         quantise_w1(0, 0, 0)
-        quantise_w1(1, 0, 80)
+        w1_raw[1, 0] = load_w1(1, 0, AT_W1_10)
+        tab_w.append(load_words("tab_w1", tab_words[1], AT_TAB1))
+        tab2_s = stage.tile([P, T2], U8, name="tab2_s", align_bytes=64, offset=AT_TAB2_S)
+        w4_s_raw = stage.tile([P, H], U8, name="w4_s_raw", align_bytes=64, offset=AT_W4_S_RAW)
+        nc.vector.memset(tab2_s[:].bitcast(I32), 0)
+        nc.vector.memset(w4_s_raw[:].bitcast(I32), 0)
+        load_scale_rows(nc.gpsimd, tab2_s, tab2_scales, 0)
+        load_scale_rows(nc.gpsimd, w4_s_raw, w4_scales, 0)
+        nc.vector.tensor_copy(v_w[0][:], tab_w[0][:].bitcast(U32).indirect(offs_t[:]))
+        nc.vector.tensor_copy(v_s[:], tab_s[:].indirect(offs_t[:]))
+        w1_raw[0, 1] = load_w1(0, 1, AT_W1_01)
+        w1_raw[1, 1] = load_w1(1, 1, AT_W1_11)
+        w4_raw = stage.tile([P, n2, H // 2], I32, name="w4_raw", align_bytes=64, offset=AT_W4)
+        nc.sync.dma_start(out=w4_raw[:], in_=w4_words.rearrange("a p n -> p a n").bitcast(I32))
+        w8_s = stage.tile([P, N], U8, name="w8_s", align_bytes=64, offset=AT_TAB_S)
+        load_scale_rows(nc.gpsimd, w8_s, w8_scales, 0)
+        quantise_w1(1, 0, 0)
+        tab2_w = [load_words("tab2_w0", tab2_words[0], AT_TAB2[0])]
+        for u in range(S // BANK):
+            nc.vector.tensor_copy(
+                v_w[1][:, u * BANK : (u + 1) * BANK],
+                tab_w[1][:].bitcast(U32).indirect(offs_t[:, u * BANK // 16 : (u + 1) * BANK // 16]),
+            )
+        for a in range(1, n2):
+            tab2_w.append(load_words("tab2_w%d" % a, tab2_words[a], AT_TAB2[a]))
         for t in range(PACK):
             basin_stage(0, t)
-            pick_stage(units[0], t)
         quantise_w1(0, 1, P)
+        w8_w = stage.tile([P, n3, N], I32, name="w8_w", align_bytes=64, offset=AT_W1_01)
+        nc.sync.dma_start(out=w8_w[:], in_=w8_words.rearrange("a p n t -> p a (n t)").bitcast(I32))
         quantise_w1(1, 1, P)
+        for t in range(PACK):
+            pick_stage(units[0], t)
+        nc.vector.tensor_copy(
+            out=w4_w[:].bitcast(U16).rearrange("p a (b t m) -> p (a b) m t", t=PACK, m=P),
+            in_=w4_raw[:].bitcast(U16).rearrange("p a (b m t) -> p (a b) m t", t=PACK, m=P),
+        )
         nc.vector.tensor_copy(v2_s[0][:], tab2_s[:].indirect(offs2_t[:]))
         shift_planes(v2_s)
         nc.vector.tensor_copy(

@@ -21,12 +21,21 @@ PACK = 4
 PASS = P * PACK
 BANK = 512
 SHIFT_ROWS = 112
+TAB_PLANE = 8
 KIB = 1024
-AT_W1_10, AT_W1_00, AT_TAB2_S, AT_W4_S_RAW, AT_TAB1 = 0, 4 * KIB, 8 * KIB, 10 * KIB, 11 * KIB
-AT_TAB2 = (0, 11 * KIB, 21 * KIB)
-AT_V2_S, AT_W4_S = 19 * KIB, 20 * KIB
-AT_W1_01, AT_TAB0, AT_W1_11, AT_V_S, AT_W4 = 29 * KIB, 35 * KIB, 37 * KIB, 45 * KIB, 46 * KIB
-AT_TAB_S = 52 * KIB
+AT_TAB = (0, 16 * KIB)
+AT_KAP = AT_TAB[1]
+AT_W1 = {(0, 0): 38 * KIB, (1, 0): 32 * KIB, (0, 1): 44 * KIB, (1, 1): 56 * KIB}
+AT_H0 = tuple((76 + 4 * t) * KIB for t in range(4))
+AT_TAB2_S, AT_W4_S_RAW = 92 * KIB, 96 * KIB
+AT_GROUPED = {(0, 0): 54 * KIB, (1, 0): 71 * KIB, (0, 1): AT_TAB2_S, (1, 1): AT_H0[0]}
+AT_V1 = 52 * KIB
+AT_TAB2 = (16 * KIB, 32 * KIB, 64 * KIB)
+AT_W4_RAW, AT_W4, AT_W8 = 24 * KIB, 16 * KIB, 34 * KIB
+AT_V2 = (AT_H0[3], AT_W4_RAW, AT_TAB2[1])
+AT_V2_S, AT_W4_S = 74 * KIB, AT_H0[1]
+VECTOR_SHARE = 88
+CHUNK = 128
 
 
 def tile_list_subcatchment_nitrate_loads_kernel(
@@ -38,8 +47,6 @@ def tile_list_subcatchment_nitrate_loads_kernel(
     with ExitStack() as ctx:
         lists = ctx.enter_context(tc.tile_pool(name="lists", bufs=1))
         keep = ctx.enter_context(tc.tile_pool(name="keep", bufs=1))
-        ring = ctx.enter_context(tc.tile_pool(name="ring", bufs=2))
-        hpool = ctx.enter_context(tc.tile_pool(name="hpool", bufs=8))
         stage = ctx.enter_context(tc.tile_pool(name="stage", bufs=1))
         psum = ctx.enter_context(tc.psum_pool(name="psum", bufs=1))
 
@@ -59,42 +66,192 @@ def tile_list_subcatchment_nitrate_loads_kernel(
                     in_=src[:, 4 * q : 4 * q + 4, :].bitcast(I32),
                 )
 
-        tab_s = stage.tile([P, T], U8, name="tab_s", align_bytes=64, offset=AT_TAB_S)
-        nc.vector.memset(tab_s[:].bitcast(I32), 0)
-
-        def load_w1(a, b, offset):
-            raw = stage.tile([P, PACK, PASS], F32, name="w1_raw%d%d" % (a, b), align_bytes=64, offset=offset)
+        def load_w1(a, b):
+            raw = stage.tile([P, PACK, PASS], F32, name="w1_raw%d%d" % (a, b), align_bytes=64, offset=AT_W1[a, b])
             nc.sync.dma_start(
                 out=raw[:],
                 in_=w1[a * PASS : (a + 1) * PASS, b * PASS : (b + 1) * PASS].rearrange("(p j) c -> p j c", j=PACK),
             )
             return raw
 
+        tab_s = keep.tile([P, T], U8, name="tab_s", align_bytes=64)
+        tab2_s = stage.tile([P, T2], U8, name="tab2_s", align_bytes=64, offset=AT_TAB2_S)
+        w4_s_raw = stage.tile([P, H], U8, name="w4_s_raw", align_bytes=64, offset=AT_W4_S_RAW)
+        nc.vector.memset(tab_s[:].bitcast(I32), 0)
+        nc.vector.memset(tab2_s[:].bitcast(I32), 0)
+        nc.vector.memset(w4_s_raw[:].bitcast(I32), 0)
+
         offs_t = lists.tile([P, S // 16], U16, name="offs_t")
         pos_t = lists.tile([P, M // 16], U16, name="pos_t")
         offs2_t = lists.tile([P, M // 16], U16, name="offs2_t")
-        kap_t = keep.tile([P, n3, PACK], F32, name="kap_t")
+        kap_t = stage.tile([P, n3, PACK], F32, name="kap_t", align_bytes=64, offset=AT_KAP)
         b2_t = keep.tile([P, n3, PACK], F32, name="b2_t")
         b3_t = keep.tile([P, N // P], F32, name="b3_t")
-        warm = keep.tile([P, 1], F32, name="warm")
 
-        load_scale_rows(nc.gpsimd, tab_s, tab_scales, 8)
-        nc.scalar.dma_start(out=kap_t[:], in_=kap.rearrange("(b p t) -> p b t", p=P, t=PACK))
-        nc.scalar.activation(warm[:], kap_t[:, 0, 0:1], ACT.Abs_reciprocal_sqrt)
+        load_scale_rows(nc.gpsimd, tab_s, tab_scales, TAB_PLANE)
+        load_scale_rows(nc.gpsimd, tab2_s, tab2_scales, 0)
+        load_scale_rows(nc.gpsimd, w4_s_raw, w4_scales, 0)
         nc.sync.dma_start(offs_t[:], offs)
-        w1_raw = {(0, 0): load_w1(0, 0, AT_W1_00)}
-        tab_w = [load_words("tab_w0", tab_words[0], AT_TAB0)]
-        nc.sync.dma_start(pos_t[:], pos1)
+        tab_w = [load_words("tab_w0", tab_words[0], AT_TAB[0])]
+        nc.sync.dma_start(out=kap_t[:], in_=kap.rearrange("(b p t) -> p b t", p=P, t=PACK))
+        w1_raw = {(0, 0): load_w1(0, 0)}
         nc.sync.dma_start(offs2_t[:], offs2)
         nc.sync.dma_start(out=b2_t[:], in_=b2.rearrange("(b p t) -> p b t", p=P, t=PACK))
+        nc.sync.dma_start(pos_t[:], pos1)
         with nc.allow_non_contiguous_dma(reason="one bias value a partition"):
             nc.sync.dma_start(out=b3_t[:], in_=b3.rearrange("(c p) -> p c", p=P))
 
-        w4_w = keep.tile([P, n2, 2 * H], U8, name="w4_w", align_bytes=64)
-        w4_s = [stage.tile([P, H], U8, name="w4_s0", align_bytes=64, offset=AT_W4_S)]
-        w4_s.extend(keep.tile([P, H], U8, name="w4_s%d" % a, align_bytes=64) for a in range(1, n2))
-        v_s = stage.tile([P, S], U8, name="v_s", align_bytes=64, offset=AT_V_S)
-        v_w = [keep.tile([P, S], U32, name="v_w%d" % a, align_bytes=64) for a in range(n1)]
+        root = keep.tile([P, n3, PACK], F32, name="root")
+        nc.scalar.activation(root[:], kap_t[:], ACT.Abs_reciprocal_sqrt)
+
+        grouped, w1_w, w1_s = {}, {}, {}
+
+        def cast_w1(a, b, vector_share):
+            grouped[a, b] = stage.tile(
+                [P, PACK, P, PACK], BF16, name="w1_grouped%d%d" % (a, b), align_bytes=64, offset=AT_GROUPED[a, b]
+            )
+            src = w1_raw[a, b][:].rearrange("p j (m t) -> p m j t", t=PACK)
+            dst = grouped[a, b][:].rearrange("p t m j -> p m j t")
+            if vector_share > 0:
+                nc.vector.tensor_copy(out=dst[:, 0:vector_share], in_=src[:, 0:vector_share])
+            if vector_share < P:
+                nc.scalar.copy(out=dst[:, vector_share:P], in_=src[:, vector_share:P])
+
+        def quantise_w1(a, b, pieces):
+            w1_w[a, b] = keep.tile([P, PASS], U32, name="w1_w%d%d" % (a, b), align_bytes=64)
+            w1_s[a, b] = keep.tile([P, PASS], U8, name="w1_s%d%d" % (a, b), align_bytes=64)
+            flat = grouped[a, b][:].rearrange("p t m j -> p (t m j)")
+            width = PASS // pieces
+            for i in range(pieces):
+                nc.vector.quantize_mx(
+                    out=w1_w[a, b][:, i * width : (i + 1) * width].bitcast(FP8X4),
+                    scales=w1_s[a, b][:, i * width : (i + 1) * width],
+                    in_=flat[:, PACK * i * width : PACK * (i + 1) * width],
+                )
+
+        v_s = keep.tile([P, S], U8, name="v_s", align_bytes=64)
+        v_w = [keep.tile([P, S], U32, name="v_w0", align_bytes=64)]
+        h = {}
+
+        def basin_pass(acc, b, t, u, a):
+            cols = slice(t * P, (t + 1) * P)
+            run = slice(u * BANK, (u + 1) * BANK)
+            nc.tensor.matmul_mx(
+                out=acc[:], lhsT=w1_w[a, b][:, cols].bitcast(FP8X4), lhsT_scale=w1_s[a, b][:, cols],
+                rhs=v_w[a][:, run].bitcast(FP8X4), rhs_scale=v_s[TAB_PLANE + 4 * a : P, run],
+                start=(a == 0), stop=(a == n1 - 1),
+            )
+
+        def empty_basin(acc, b, t, u, on_vector):
+            if u == 0:
+                if b == 0:
+                    h[b, t] = stage.tile([P, S], F32, name="h0%d" % t, align_bytes=64, offset=AT_H0[t])
+                else:
+                    h[b, t] = keep.tile([P, S], F32, name="h1%d" % t)
+            run = slice(u * BANK, (u + 1) * BANK)
+            if on_vector:
+                nc.vector.tensor_copy(out=h[b, t][:, run], in_=acc[:])
+            else:
+                nc.scalar.copy(out=h[b, t][:, run], in_=acc[:])
+
+        units = [(0, 0, M), (1, 0, 2 * CHUNK), (1, 2 * CHUNK, CHUNK), (1, 3 * CHUNK, CHUNK)]
+        picked = {u: keep.tile([P, PACK, u[2]], F32, name="picked%d_%d" % u[:2]) for u in units}
+
+        def pick(unit, t):
+            b, m0, width = unit
+            nc.vector.tensor_copy(picked[unit][:, t, :], h[b, t][:].indirect(pos_t[:, m0 // 16 : (m0 + width) // 16]))
+
+        def reciprocal(unit, ts):
+            for t in ts:
+                x = picked[unit][:, t, :]
+                nc.scalar.activation(x, x, ACT.Square, scale=root[:, unit[0], t : t + 1])
+            for t in ts:
+                x = picked[unit][:, t, :]
+                nc.scalar.activation(x, x, ACT.Abs_reciprocal_sqrt, bias=1.0)
+            for t in ts:
+                x = picked[unit][:, t, :]
+                nc.scalar.activation(x, x, ACT.Square, scale=root[:, unit[0], t : t + 1])
+
+        v2_w = {}
+        own = {}
+
+        def gather_v2(a):
+            v2_w[a] = stage.tile([P, M], U32, name="v2_w%d" % a, align_bytes=64, offset=AT_V2[a])
+            nc.vector.tensor_copy(v2_w[a][:], tab2_w[a][:].bitcast(U32).indirect(offs2_t[:]))
+
+        def own_passes(acc, b, t, run):
+            c0 = b * PASS + t * P
+            for a in range(n2):
+                nc.tensor.matmul_mx(
+                    out=acc, lhsT=w4_w[:, a, 2 * c0 : 2 * (c0 + P)].bitcast(FP4X4), lhsT_scale=w4_s[a][:, c0 : c0 + P],
+                    rhs=v2_w[a][:, run].bitcast(FP8X4), rhs_scale=v2_s[a][:, run],
+                    start=(a == 0), stop=(a == n2 - 1),
+                )
+
+        def ratio(unit, t, acc, m0, width):
+            x = picked[unit][:, t, m0 - unit[1] : m0 - unit[1] + width]
+            nc.vector.scalar_tensor_tensor(
+                out=x, in0=acc, scalar=b2_t[:, unit[0], t : t + 1], in1=x, op0=ALU.add, op1=ALU.mult
+            )
+
+        z_w = [keep.tile([P, M], U32, name="z_w%d" % b, align_bytes=64) for b in range(n3)]
+        z_s = [keep.tile([P, M], U8, name="z_s%d" % b, align_bytes=64) for b in range(n3)]
+        z_grouped = {}
+
+        def group_z(unit):
+            z_grouped[unit] = keep.tile([P, unit[2], PACK], BF16, name="z_grouped%d_%d" % unit[:2], align_bytes=64)
+            nc.vector.tensor_scalar_max(
+                out=z_grouped[unit][:].rearrange("p (c i) t -> p c t i", i=4),
+                in0=picked[unit][:].rearrange("p t (c i) -> p c t i", i=4),
+                scalar1=0.0,
+            )
+
+        def quantise_z(unit):
+            b, m0, width = unit
+            nc.vector.quantize_mx(
+                out=z_w[b][:, m0 : m0 + width].bitcast(FP8X4), scales=z_s[b][:, m0 : m0 + width],
+                in_=z_grouped[unit][:].rearrange("p m t -> p (m t)"),
+            )
+
+        def score_pass(acc, unit, c, b, start, stop):
+            run = slice(unit[1], unit[1] + unit[2])
+            cols = slice(c * P, (c + 1) * P)
+            nc.tensor.matmul_mx(
+                out=acc, lhsT=w8_w[:, b, cols].bitcast(FP8X4), lhsT_scale=w8_s[4 * b : P, cols],
+                rhs=z_w[b][:, run].bitcast(FP8X4), rhs_scale=z_s[b][:, run], start=start, stop=stop,
+            )
+
+        def add_bias(res, acc, c, on_vector):
+            if on_vector:
+                nc.vector.tensor_scalar_add(out=res, in0=acc, scalar1=b3_t[:, c : c + 1])
+            else:
+                nc.scalar.activation(res, acc, ACT.Identity, bias=b3_t[:, c : c + 1])
+
+        tab_w.append(load_words("tab_w1", tab_words[1], AT_TAB[1]))
+        nc.vector.tensor_copy(v_w[0][:], tab_w[0][:].bitcast(U32).indirect(offs_t[:]))
+        nc.vector.tensor_copy(v_s[:], tab_s[:].indirect(offs_t[:]))
+        cast_w1(0, 0, 0)
+        w1_raw[1, 0] = load_w1(1, 0)
+        w1_raw[0, 1] = load_w1(0, 1)
+        quantise_w1(0, 0, 1)
+        w1_raw[1, 1] = load_w1(1, 1)
+        slots = [(t, u) for t in range(PACK) for u in range(S // BANK)]
+        acc0 = {(t, u): bank(2 * t + u) for t, u in slots}
+        for t, u in slots:
+            basin_pass(acc0[t, u], 0, t, u, 0)
+        v_w.append(stage.tile([P, S], U32, name="v_w1", align_bytes=64, offset=AT_V1))
+        nc.vector.tensor_copy(v_w[1][:], tab_w[1][:].bitcast(U32).indirect(offs_t[:]))
+        tab2_w = {0: load_words("tab2_w0", tab2_words[0], AT_TAB2[0])}
+        w4_raw = stage.tile([P, n2, H // 2], I32, name="w4_raw", align_bytes=64, offset=AT_W4_RAW)
+        nc.sync.dma_start(out=w4_raw[:], in_=w4_words.rearrange("a p n -> p a n").bitcast(I32))
+        cast_w1(1, 0, VECTOR_SHARE)
+        tab2_w[1] = load_words("tab2_w1", tab2_words[1], AT_TAB2[1])
+        quantise_w1(1, 0, PACK)
+        tab2_w[2] = load_words("tab2_w2", tab2_words[2], AT_TAB2[2])
+        for t, u in slots:
+            basin_pass(acc0[t, u], 0, t, u, 1)
+            empty_basin(acc0[t, u], 0, t, u, False)
+
         v2_s = [stage.tile([P, M], U8, name="v2_s0", align_bytes=64, offset=AT_V2_S)]
         v2_s.extend(keep.tile([P, M], U8, name="v2_s%d" % a, align_bytes=64) for a in range(1, n2))
 
@@ -105,192 +262,92 @@ def tile_list_subcatchment_nitrate_loads_kernel(
                     in_=planes[0][4 * a : 4 * a + SHIFT_ROWS, :].bitcast(I32),
                 )
 
-        w1_w, w1_s = {}, {}
+        nc.vector.tensor_copy(v2_s[0][:], tab2_s[:].indirect(offs2_t[:]))
+        shift_planes(v2_s)
+        cast_w1(0, 1, P)
+        pick(units[0], 0)
+        quantise_w1(0, 1, 1)
+        cast_w1(1, 1, 0)
+        pick(units[0], 1)
+        w4_s = [stage.tile([P, H], U8, name="w4_s0", align_bytes=64, offset=AT_W4_S)]
+        w4_s.extend(keep.tile([P, H], U8, name="w4_s%d" % a, align_bytes=64) for a in range(1, n2))
+        pick(units[0], 2)
+        nc.vector.tensor_copy(
+            out=w4_s[0][:].rearrange("p (b t c i) -> p b c t i", t=PACK, c=8, i=16),
+            in_=w4_s_raw[:].rearrange("p (b c i t) -> p b c t i", t=PACK, c=8, i=16),
+        )
+        shift_planes(w4_s)
+        w8_s = stage.tile([P, N], U8, name="w8_s", align_bytes=64, offset=AT_W4_S_RAW)
+        load_scale_rows(nc.gpsimd, w8_s, w8_scales, 0)
+        quantise_w1(1, 1, 1)
+        pick(units[0], 3)
+        for t, u in slots:
+            acc = bank((2 * t + u) % 4)
+            for a in range(n1):
+                basin_pass(acc, 1, t, u, a)
+            empty_basin(acc, 1, t, u, False)
+        gather_v2(0)
+        w4_w = stage.tile([P, n2, 2 * H], U8, name="w4_w", align_bytes=64, offset=AT_W4)
+        nc.vector.tensor_copy(
+            out=w4_w[:].bitcast(U16).rearrange("p a (b t c i) -> p (a b) c t i", t=PACK, c=16, i=8),
+            in_=w4_raw[:].bitcast(U16).rearrange("p a (b c i t) -> p (a b) c t i", t=PACK, c=16, i=8),
+        )
+        gather_v2(1)
+        w8_w = stage.tile([P, n3, N], I32, name="w8_w", align_bytes=64, offset=AT_W8)
+        nc.sync.dma_start(out=w8_w[:], in_=w8_words.rearrange("a p n t -> p a (n t)").bitcast(I32))
+        reciprocal(units[0], (0, 1))
+        reciprocal(units[0], (2, 3))
+        pick(units[1], 0)
+        pick(units[1], 1)
+        gather_v2(2)
+        pick(units[1], 2)
+        pick(units[1], 3)
+        for unit in units[2:]:
+            for t in range(PACK):
+                pick(unit, t)
+        for t in range(PACK):
+            acc = bank(4 + t)
+            own_passes(acc[:], 0, t, slice(0, M))
+            ratio(units[0], t, acc[:], 0, M)
+        group_z(units[0])
+        quantise_z(units[0])
+        for i in range(M // CHUNK):
+            own[i] = bank(i)
+            for t in range(PACK):
+                own_passes(own[i][:, t * CHUNK : (t + 1) * CHUNK], 1, t, slice(i * CHUNK, (i + 1) * CHUNK))
 
-        def quantise_w1(a, b, vector_share):
-            grouped = ring.tile([P, PACK, P, PACK], BF16, name="w1_grouped", align_bytes=64)
-            src = w1_raw[a, b][:].rearrange("p j (m t) -> p m j t", t=PACK)
-            dst = grouped[:].rearrange("p t m j -> p m j t")
-            if vector_share > 0:
-                nc.vector.tensor_copy(out=dst[:, 0:vector_share], in_=src[:, 0:vector_share])
-            if vector_share < P:
-                nc.scalar.copy(out=dst[:, vector_share:P], in_=src[:, vector_share:P])
-            w1_w[a, b] = keep.tile([P, PASS], U32, name="w1_w%d%d" % (a, b), align_bytes=64)
-            w1_s[a, b] = keep.tile([P, PASS], U8, name="w1_s%d%d" % (a, b), align_bytes=64)
-            nc.vector.quantize_mx(
-                out=w1_w[a, b][:].bitcast(FP8X4), scales=w1_s[a, b][:],
-                in_=grouped[:].rearrange("p t m j -> p (t m j)"),
-            )
+        def places(unit, banks):
+            per_bank = N // P // len(banks)
+            tiles = [bank(i) for i in banks]
+            return [
+                (tiles[c // per_bank][:, (c % per_bank) * unit[2] : (c % per_bank + 1) * unit[2]], c % per_bank == 0, c % per_bank == per_bank - 1)
+                for c in range(N // P)
+            ]
 
-        half = M // 2
-        units = [(0, 0, M), (1, 0, half), (1, half, half)]
-        picked = {u: keep.tile([P, PACK, u[2]], F32, name="picked%d_%d" % u[:2]) for u in units}
-        h = {}
-
-        def basin_stage(b, t):
-            h[b, t] = hpool.tile([P, S], F32, name="h")
-            cols = slice(t * P, (t + 1) * P)
-            for u in range(S // BANK):
-                acc = bank((2 * t + u) % (8 if b == 0 else 4))
-                run = slice(u * BANK, (u + 1) * BANK)
-                for a in range(n1):
-                    nc.tensor.matmul_mx(
-                        out=acc[:], lhsT=w1_w[a, b][:, cols].bitcast(FP8X4), lhsT_scale=w1_s[a, b][:, cols],
-                        rhs=v_w[a][:, run].bitcast(FP8X4), rhs_scale=v_s[8 + 4 * a : P, run],
-                        start=(a == 0), stop=(a == n1 - 1),
-                    )
-                nc.scalar.copy(out=h[b, t][:, run], in_=acc[:])
-
-        def pick_stage(unit, t):
-            b, m0, width = unit
-            nc.vector.tensor_copy(picked[unit][:, t, :], h[b, t][:].indirect(pos_t[:, m0 // 16 : (m0 + width) // 16]))
-
-        def reciprocal_stage(unit, t):
-            x = picked[unit][:, t, :]
-            nc.scalar.activation(x, x, ACT.Square)
-            nc.scalar.activation(x, x, ACT.Abs_reciprocal_sqrt, bias=kap_t[:, unit[0], t : t + 1])
-            nc.scalar.activation(x, x, ACT.Square)
-
-        v2_w = [keep.tile([P, M], U32, name="v2_w%d" % a, align_bytes=64) for a in range(n2)]
-        own = {}
-
-        def own_stage(b, t):
-            own[b, t] = bank(4 + t)
-            c0 = b * PASS + t * P
-            for a in range(n2):
-                nc.tensor.matmul_mx(
-                    out=own[b, t][:], lhsT=w4_w[:, a, 2 * c0 : 2 * (c0 + P)].bitcast(FP4X4), lhsT_scale=w4_s[a][:, c0 : c0 + P],
-                    rhs=v2_w[a][:].bitcast(FP8X4), rhs_scale=v2_s[a][:],
-                    start=(a == 0), stop=(a == n2 - 1),
-                )
-
-        def ratio_stage(unit, t):
-            b, m0, width = unit
-            x = picked[unit][:, t, :]
-            nc.vector.scalar_tensor_tensor(
-                out=x, in0=own[b, t][:, m0 : m0 + width], scalar=b2_t[:, b, t : t + 1], in1=x, op0=ALU.add, op1=ALU.mult
-            )
-
-        z_w = [keep.tile([P, M], U32, name="z_w%d" % b, align_bytes=64) for b in range(n3)]
-        z_s = [keep.tile([P, M], U8, name="z_s%d" % b, align_bytes=64) for b in range(n3)]
-
-        def quantise_z(unit):
-            b, m0, width = unit
-            grouped = keep.tile([P, width, PACK], BF16, name="z_grouped%d_%d" % unit[:2], align_bytes=64)
-            nc.vector.tensor_scalar_max(
-                out=grouped[:].rearrange("p (c i) t -> p c t i", i=4),
-                in0=picked[unit][:].rearrange("p t (c i) -> p c t i", i=4),
-                scalar1=0.0,
-            )
-            nc.vector.quantize_mx(
-                out=z_w[b][:, m0 : m0 + width].bitcast(FP8X4), scales=z_s[b][:, m0 : m0 + width],
-                in_=grouped[:].rearrange("p m t -> p (m t)"),
+        def finish(unit, place, cs, on_vector):
+            res = keep.tile([P, len(cs), unit[2]], F32, name="res%d_%d" % (unit[1], cs[0]))
+            for j, c in enumerate(cs):
+                add_bias(res[:, j, :], place[c][0], c, on_vector)
+            nc.sync.dma_start(
+                out=out[cs[0] * P : (cs[-1] + 1) * P, unit[1] : unit[1] + unit[2]].rearrange("(j p) m -> p j m", p=P), in_=res[:]
             )
 
         score = {}
-
-        def score_pass(u, pair, b):
-            if b == 0:
-                score[u, pair] = bank(3 * u + pair)
-            run = slice(u * half, (u + 1) * half)
-            for j in range(2):
-                c = 2 * pair + j
-                cols = slice(c * P, (c + 1) * P)
-                nc.tensor.matmul_mx(
-                    out=score[u, pair][:, j * half : (j + 1) * half],
-                    lhsT=w8_w[:, b, cols].bitcast(FP8X4), lhsT_scale=w8_s[4 * b : P, cols],
-                    rhs=z_w[b][:, run].bitcast(FP8X4), rhs_scale=z_s[b][:, run],
-                    start=(b == 0 and j == 0), stop=(b == n3 - 1 and j == 1),
-                )
-
-        def finish(u, pair, on_scalar):
-            res = keep.tile([P, 2, half], F32, name="res%d_%d" % (u, pair))
-            for j in range(2):
-                c = 2 * pair + j
-                src = score[u, pair][:, j * half : (j + 1) * half]
-                if on_scalar:
-                    nc.scalar.activation(res[:, j, :], src, ACT.Identity, bias=b3_t[:, c : c + 1])
-                else:
-                    nc.vector.tensor_scalar_add(out=res[:, j, :], in0=src, scalar1=b3_t[:, c : c + 1])
-            nc.sync.dma_start(
-                out=out[2 * pair * P : 2 * (pair + 1) * P, u * half : (u + 1) * half].rearrange("(j p) m -> p j m", p=P),
-                in_=res[:],
-            )
-
-        quantise_w1(0, 0, 0)
-        w1_raw[1, 0] = load_w1(1, 0, AT_W1_10)
-        tab_w.append(load_words("tab_w1", tab_words[1], AT_TAB1))
-        tab2_s = stage.tile([P, T2], U8, name="tab2_s", align_bytes=64, offset=AT_TAB2_S)
-        w4_s_raw = stage.tile([P, H], U8, name="w4_s_raw", align_bytes=64, offset=AT_W4_S_RAW)
-        nc.vector.memset(tab2_s[:].bitcast(I32), 0)
-        nc.vector.memset(w4_s_raw[:].bitcast(I32), 0)
-        load_scale_rows(nc.gpsimd, tab2_s, tab2_scales, 0)
-        load_scale_rows(nc.gpsimd, w4_s_raw, w4_scales, 0)
-        nc.vector.tensor_copy(v_w[0][:], tab_w[0][:].bitcast(U32).indirect(offs_t[:]))
-        nc.vector.tensor_copy(v_s[:], tab_s[:].indirect(offs_t[:]))
-        w1_raw[0, 1] = load_w1(0, 1, AT_W1_01)
-        w1_raw[1, 1] = load_w1(1, 1, AT_W1_11)
-        w4_raw = stage.tile([P, n2, H // 2], I32, name="w4_raw", align_bytes=64, offset=AT_W4)
-        nc.sync.dma_start(out=w4_raw[:], in_=w4_words.rearrange("a p n -> p a n").bitcast(I32))
-        w8_s = stage.tile([P, N], U8, name="w8_s", align_bytes=64, offset=AT_TAB_S)
-        load_scale_rows(nc.gpsimd, w8_s, w8_scales, 0)
-        quantise_w1(1, 0, 0)
-        tab2_w = [load_words("tab2_w0", tab2_words[0], AT_TAB2[0])]
-        for u in range(S // BANK):
-            nc.vector.tensor_copy(
-                v_w[1][:, u * BANK : (u + 1) * BANK],
-                tab_w[1][:].bitcast(U32).indirect(offs_t[:, u * BANK // 16 : (u + 1) * BANK // 16]),
-            )
-        for a in range(1, n2):
-            tab2_w.append(load_words("tab2_w%d" % a, tab2_words[a], AT_TAB2[a]))
-        for t in range(PACK):
-            basin_stage(0, t)
-        quantise_w1(0, 1, P)
-        w8_w = stage.tile([P, n3, N], I32, name="w8_w", align_bytes=64, offset=AT_W1_01)
-        nc.sync.dma_start(out=w8_w[:], in_=w8_words.rearrange("a p n t -> p a (n t)").bitcast(I32))
-        quantise_w1(1, 1, P)
-        for t in range(PACK):
-            pick_stage(units[0], t)
-        nc.vector.tensor_copy(
-            out=w4_w[:].bitcast(U16).rearrange("p a (b t m) -> p (a b) m t", t=PACK, m=P),
-            in_=w4_raw[:].bitcast(U16).rearrange("p a (b m t) -> p (a b) m t", t=PACK, m=P),
-        )
-        nc.vector.tensor_copy(v2_s[0][:], tab2_s[:].indirect(offs2_t[:]))
-        shift_planes(v2_s)
-        nc.vector.tensor_copy(
-            out=w4_s[0][:].rearrange("p (b t m) -> p b m t", t=PACK, m=P),
-            in_=w4_s_raw[:].rearrange("p (b m t) -> p b m t", t=PACK, m=P),
-        )
-        shift_planes(w4_s)
-        for t in range(PACK):
-            reciprocal_stage(units[0], t)
-            basin_stage(1, t)
-            pick_stage(units[1], t)
-        for a in range(n2):
-            nc.vector.tensor_copy(v2_w[a][:], tab2_w[a][:].bitcast(U32).indirect(offs2_t[:]))
-        for t in range(PACK):
-            pick_stage(units[2], t)
-            own_stage(0, t)
-            ratio_stage(units[0], t)
-            reciprocal_stage(units[1], t)
-        quantise_z(units[0])
+        for unit, banks in zip(units[1:], ((4, 5, 6), (7, 0), (1, 2))):
+            score[unit] = places(unit, banks)
+            for c, (acc, first, last) in enumerate(score[unit]):
+                score_pass(acc, unit, c, 0, first, False)
+            reciprocal(unit, range(PACK))
+            for i in range(unit[1] // CHUNK, (unit[1] + unit[2]) // CHUNK):
+                for t in range(PACK):
+                    ratio(unit, t, own[i][:, t * CHUNK : (t + 1) * CHUNK], i * CHUNK, CHUNK)
+            group_z(unit)
+            quantise_z(unit)
+            for c, (acc, first, last) in enumerate(score[unit]):
+                score_pass(acc, unit, c, 1, False, last)
         for pair in range(3):
-            score_pass(0, pair, 0)
-        score_pass(1, 0, 0)
-        for t in range(PACK):
-            own_stage(1, t)
-            ratio_stage(units[1], t)
-            reciprocal_stage(units[2], t)
-        quantise_z(units[1])
-        for pair in range(3):
-            score_pass(0, pair, 1)
-        for t in range(PACK):
-            ratio_stage(units[2], t)
-        for pair in range(1, 3):
-            score_pass(1, pair, 0)
-        quantise_z(units[2])
-        for pair in range(3):
-            finish(0, pair, True)
-        for pair in range(3):
-            score_pass(1, pair, 1)
-            finish(1, pair, pair == 1)
+            finish(units[1], score[units[1]], (2 * pair, 2 * pair + 1), False)
+        finish(units[2], score[units[2]], (0, 1, 2), False)
+        finish(units[2], score[units[2]], (3, 4, 5), False)
+        finish(units[3], score[units[3]], (0, 1, 2), True)
+        finish(units[3], score[units[3]], (3, 4, 5), False)

@@ -24,16 +24,17 @@ SHIFT_ROWS = 112
 TAB_PLANE = 8
 KIB = 1024
 AT_TAB = (0, 16 * KIB)
-AT_KAP = AT_TAB[1]
+AT_KAP = AT_TAB[1] - 32
 AT_W1 = {(0, 0): 38 * KIB, (1, 0): 32 * KIB, (0, 1): 44 * KIB, (1, 1): 56 * KIB}
 AT_H0 = tuple((76 + 4 * t) * KIB for t in range(4))
-AT_TAB2_S, AT_W4_S_RAW = 92 * KIB, 96 * KIB
-AT_GROUPED = {(0, 0): 54 * KIB, (1, 0): 71 * KIB, (0, 1): AT_TAB2_S, (1, 1): AT_H0[0]}
+AT_TAB2_S, AT_W4_S_RAW = 40 * KIB, 42 * KIB
+AT_GROUPED = {(0, 0): 54 * KIB, (1, 0): 71 * KIB, (0, 1): 72 * KIB, (1, 1): AT_H0[0]}
 AT_V1 = 52 * KIB
 AT_TAB2 = (16 * KIB, 32 * KIB, 64 * KIB)
-AT_W4_RAW, AT_W4, AT_W8 = 24 * KIB, 16 * KIB, 34 * KIB
+AT_W4_RAW, AT_W4, AT_W8 = 25 * KIB, 16 * KIB, 34 * KIB
 AT_V2 = (AT_H0[3], AT_W4_RAW, AT_TAB2[1])
-AT_V2_S, AT_W4_S = 74 * KIB, AT_H0[1]
+AT_V2_S, AT_W4_S, AT_W8_S = AT_H0[1], AT_H0[2], 30 * KIB
+AT_B2, AT_B3 = 0, 64
 VECTOR_SHARE = 88
 CHUNK = 128
 
@@ -75,34 +76,22 @@ def tile_list_subcatchment_nitrate_loads_kernel(
             return raw
 
         tab_s = keep.tile([P, T], U8, name="tab_s", align_bytes=64)
-        tab2_s = stage.tile([P, T2], U8, name="tab2_s", align_bytes=64, offset=AT_TAB2_S)
-        w4_s_raw = stage.tile([P, H], U8, name="w4_s_raw", align_bytes=64, offset=AT_W4_S_RAW)
         nc.vector.memset(tab_s[:].bitcast(I32), 0)
-        nc.vector.memset(tab2_s[:].bitcast(I32), 0)
-        nc.vector.memset(w4_s_raw[:].bitcast(I32), 0)
 
         offs_t = lists.tile([P, S // 16], U16, name="offs_t")
         pos_t = lists.tile([P, M // 16], U16, name="pos_t")
         offs2_t = lists.tile([P, M // 16], U16, name="offs2_t")
-        kap_t = stage.tile([P, n3, PACK], F32, name="kap_t", align_bytes=64, offset=AT_KAP)
-        b2_t = keep.tile([P, n3, PACK], F32, name="b2_t")
-        b3_t = keep.tile([P, N // P], F32, name="b3_t")
+        kap_t = stage.tile([P, n3, 2 * PACK], F32, name="kap_t", offset=AT_KAP)
 
-        load_scale_rows(nc.gpsimd, tab_s, tab_scales, TAB_PLANE)
-        load_scale_rows(nc.gpsimd, tab2_s, tab2_scales, 0)
-        load_scale_rows(nc.gpsimd, w4_s_raw, w4_scales, 0)
+        nc.sync.dma_start(out=kap_t[:, :, 0:PACK], in_=kap.rearrange("(b p t) -> p b t", p=P, t=PACK))
         nc.sync.dma_start(offs_t[:], offs)
-        tab_w = [load_words("tab_w0", tab_words[0], AT_TAB[0])]
-        nc.sync.dma_start(out=kap_t[:], in_=kap.rearrange("(b p t) -> p b t", p=P, t=PACK))
         w1_raw = {(0, 0): load_w1(0, 0)}
         nc.sync.dma_start(offs2_t[:], offs2)
-        nc.sync.dma_start(out=b2_t[:], in_=b2.rearrange("(b p t) -> p b t", p=P, t=PACK))
         nc.sync.dma_start(pos_t[:], pos1)
-        with nc.allow_non_contiguous_dma(reason="one bias value a partition"):
-            nc.sync.dma_start(out=b3_t[:], in_=b3.rearrange("(c p) -> p c", p=P))
+        load_scale_rows(nc.sync, tab_s, tab_scales, TAB_PLANE)
 
         root = keep.tile([P, n3, PACK], F32, name="root")
-        nc.scalar.activation(root[:], kap_t[:], ACT.Abs_reciprocal_sqrt)
+        nc.scalar.activation(root[:], kap_t[:, :, 0:PACK], ACT.Abs_reciprocal_sqrt)
 
         grouped, w1_w, w1_s = {}, {}, {}
 
@@ -227,14 +216,25 @@ def tile_list_subcatchment_nitrate_loads_kernel(
             else:
                 nc.scalar.activation(res, acc, ACT.Identity, bias=b3_t[:, c : c + 1])
 
-        tab_w.append(load_words("tab_w1", tab_words[1], AT_TAB[1]))
-        nc.vector.tensor_copy(v_w[0][:], tab_w[0][:].bitcast(U32).indirect(offs_t[:]))
+        tab_w = [load_words("tab_w%d" % a, tab_words[a], AT_TAB[a]) for a in range(n1)]
         nc.vector.tensor_copy(v_s[:], tab_s[:].indirect(offs_t[:]))
         cast_w1(0, 0, 0)
         w1_raw[1, 0] = load_w1(1, 0)
         w1_raw[0, 1] = load_w1(0, 1)
         quantise_w1(0, 0, 1)
         w1_raw[1, 1] = load_w1(1, 1)
+        tab2_s = stage.tile([P, T2], U8, name="tab2_s", align_bytes=64, offset=AT_TAB2_S)
+        w4_s_raw = stage.tile([P, H], U8, name="w4_s_raw", align_bytes=64, offset=AT_W4_S_RAW)
+        nc.vector.memset(tab2_s[:].bitcast(I32), 0)
+        nc.vector.memset(w4_s_raw[:].bitcast(I32), 0)
+        load_scale_rows(nc.sync, tab2_s, tab2_scales, 0)
+        load_scale_rows(nc.sync, w4_s_raw, w4_scales, 0)
+        nc.vector.tensor_copy(v_w[0][:], tab_w[0][:].bitcast(U32).indirect(offs_t[:]))
+        b2_t = stage.tile([P, n3, PACK], F32, name="b2_t", align_bytes=64, offset=AT_B2)
+        b3_t = stage.tile([P, N // P], F32, name="b3_t", align_bytes=64, offset=AT_B3)
+        nc.sync.dma_start(out=b2_t[:], in_=b2.rearrange("(b p t) -> p b t", p=P, t=PACK))
+        with nc.allow_non_contiguous_dma(reason="one bias value a partition"):
+            nc.sync.dma_start(out=b3_t[:], in_=b3.rearrange("(c p) -> p c", p=P))
         slots = [(t, u) for t in range(PACK) for u in range(S // BANK)]
         acc0 = {(t, u): bank(2 * t + u) for t, u in slots}
         for t, u in slots:
@@ -252,33 +252,30 @@ def tile_list_subcatchment_nitrate_loads_kernel(
             basin_pass(acc0[t, u], 0, t, u, 1)
             empty_basin(acc0[t, u], 0, t, u, False)
 
-        v2_s = [stage.tile([P, M], U8, name="v2_s0", align_bytes=64, offset=AT_V2_S)]
-        v2_s.extend(keep.tile([P, M], U8, name="v2_s%d" % a, align_bytes=64) for a in range(1, n2))
-
         def shift_planes(planes):
             for a in range(1, n2):
-                nc.gpsimd.dma_start(
+                nc.sync.dma_start(
                     out=planes[a][0:SHIFT_ROWS, :].bitcast(I32),
                     in_=planes[0][4 * a : 4 * a + SHIFT_ROWS, :].bitcast(I32),
                 )
 
-        nc.vector.tensor_copy(v2_s[0][:], tab2_s[:].indirect(offs2_t[:]))
-        shift_planes(v2_s)
         cast_w1(0, 1, P)
         pick(units[0], 0)
         quantise_w1(0, 1, 1)
         cast_w1(1, 1, 0)
         pick(units[0], 1)
+        pick(units[0], 2)
+        v2_s = [stage.tile([P, M], U8, name="v2_s0", align_bytes=64, offset=AT_V2_S)]
+        v2_s.extend(keep.tile([P, M], U8, name="v2_s%d" % a, align_bytes=64) for a in range(1, n2))
+        nc.vector.tensor_copy(v2_s[0][:], tab2_s[:].indirect(offs2_t[:]))
+        shift_planes(v2_s)
         w4_s = [stage.tile([P, H], U8, name="w4_s0", align_bytes=64, offset=AT_W4_S)]
         w4_s.extend(keep.tile([P, H], U8, name="w4_s%d" % a, align_bytes=64) for a in range(1, n2))
-        pick(units[0], 2)
         nc.vector.tensor_copy(
             out=w4_s[0][:].rearrange("p (b t c i) -> p b c t i", t=PACK, c=8, i=16),
             in_=w4_s_raw[:].rearrange("p (b c i t) -> p b c t i", t=PACK, c=8, i=16),
         )
         shift_planes(w4_s)
-        w8_s = stage.tile([P, N], U8, name="w8_s", align_bytes=64, offset=AT_W4_S_RAW)
-        load_scale_rows(nc.gpsimd, w8_s, w8_scales, 0)
         quantise_w1(1, 1, 1)
         pick(units[0], 3)
         for t, u in slots:
@@ -292,6 +289,8 @@ def tile_list_subcatchment_nitrate_loads_kernel(
             out=w4_w[:].bitcast(U16).rearrange("p a (b t c i) -> p (a b) c t i", t=PACK, c=16, i=8),
             in_=w4_raw[:].bitcast(U16).rearrange("p a (b c i t) -> p (a b) c t i", t=PACK, c=16, i=8),
         )
+        w8_s = stage.tile([P, N], U8, name="w8_s", align_bytes=64, offset=AT_W8_S)
+        load_scale_rows(nc.sync, w8_s, w8_scales, 0)
         gather_v2(1)
         w8_w = stage.tile([P, n3, N], I32, name="w8_w", align_bytes=64, offset=AT_W8)
         nc.sync.dma_start(out=w8_w[:], in_=w8_words.rearrange("a p n t -> p a (n t)").bitcast(I32))

@@ -24,19 +24,18 @@ SHIFT_ROWS = 112
 TAB_PLANE = 8
 KIB = 1024
 AT_TAB = (0, 16 * KIB)
-AT_KAP = AT_TAB[1] - 32
-AT_W1 = {(0, 0): 38 * KIB, (1, 0): 32 * KIB, (0, 1): 44 * KIB, (1, 1): 56 * KIB}
-AT_H0 = tuple((76 + 4 * t) * KIB for t in range(4))
+AT_W1 = {(0, 0): 28 * KIB, (1, 0): 32 * KIB, (0, 1): 48 * KIB, (1, 1): 56 * KIB}
+AT_H = {(b, t): (76 + 16 * b + 4 * t) * KIB for b in range(2) for t in range(4)}
+AT_GROUPED = {(0, 0): 54 * KIB, (1, 0): 71 * KIB, (0, 1): AT_H[0, 0], (1, 1): AT_H[0, 1]}
+AT_V_S = 0
 AT_TAB2_S, AT_W4_S_RAW = 40 * KIB, 42 * KIB
-AT_GROUPED = {(0, 0): 54 * KIB, (1, 0): 71 * KIB, (0, 1): 72 * KIB, (1, 1): AT_H0[0]}
-AT_V1 = 52 * KIB
 AT_TAB2 = (16 * KIB, 32 * KIB, 64 * KIB)
-AT_W4_RAW, AT_W4, AT_W8 = 25 * KIB, 16 * KIB, 34 * KIB
-AT_V2 = (AT_H0[3], AT_W4_RAW, AT_TAB2[1])
-AT_V2_S, AT_W4_S, AT_W8_S = AT_H0[1], AT_H0[2], 30 * KIB
-AT_B2, AT_B3 = 0, 64
+AT_W4_RAW = 24 * KIB
+AT_V2_S, AT_W4_S, AT_W4 = AT_H[0, 2], AT_TAB2_S, AT_TAB2[0]
+AT_V2 = (AT_H[0, 3], AT_W4_RAW, AT_TAB2[1] + 4 * KIB)
+AT_PICKED = (AT_TAB2[1], AT_TAB2[2])
+AT_W8, AT_W8_S = 26 * KIB, 42 * KIB
 VECTOR_SHARE = 88
-CHUNK = 128
 
 
 def tile_list_subcatchment_nitrate_loads_kernel(
@@ -76,22 +75,34 @@ def tile_list_subcatchment_nitrate_loads_kernel(
             return raw
 
         tab_s = keep.tile([P, T], U8, name="tab_s", align_bytes=64)
+        tab2_s = stage.tile([P, T2], U8, name="tab2_s", align_bytes=64, offset=AT_TAB2_S)
+        w4_s_raw = stage.tile([P, H], U8, name="w4_s_raw", align_bytes=64, offset=AT_W4_S_RAW)
         nc.vector.memset(tab_s[:].bitcast(I32), 0)
+        nc.vector.memset(tab2_s[:].bitcast(I32), 0)
+        nc.vector.memset(w4_s_raw[:].bitcast(I32), 0)
 
         offs_t = lists.tile([P, S // 16], U16, name="offs_t")
         pos_t = lists.tile([P, M // 16], U16, name="pos_t")
         offs2_t = lists.tile([P, M // 16], U16, name="offs2_t")
-        kap_t = stage.tile([P, n3, 2 * PACK], F32, name="kap_t", offset=AT_KAP)
+        kap_t = keep.tile([P, n3, PACK], F32, name="kap_t")
+        b2_t = keep.tile([P, n3, PACK], F32, name="b2_t")
+        b3_t = keep.tile([P, N // P], F32, name="b3_t")
 
-        nc.sync.dma_start(out=kap_t[:, :, 0:PACK], in_=kap.rearrange("(b p t) -> p b t", p=P, t=PACK))
-        nc.sync.dma_start(offs_t[:], offs)
+        load_scale_rows(nc.gpsimd, tab_s, tab_scales, TAB_PLANE)
+        load_scale_rows(nc.gpsimd, tab2_s, tab2_scales, 0)
+        load_scale_rows(nc.gpsimd, w4_s_raw, w4_scales, 0)
+        nc.sync.dma_start(out=kap_t[:], in_=kap.rearrange("(b p t) -> p b t", p=P, t=PACK))
         w1_raw = {(0, 0): load_w1(0, 0)}
+        nc.sync.dma_start(offs_t[:], offs)
+        tab_w = [load_words("tab_w0", tab_words[0], AT_TAB[0])]
         nc.sync.dma_start(offs2_t[:], offs2)
         nc.sync.dma_start(pos_t[:], pos1)
-        load_scale_rows(nc.sync, tab_s, tab_scales, TAB_PLANE)
+        nc.sync.dma_start(out=b2_t[:], in_=b2.rearrange("(b p t) -> p b t", p=P, t=PACK))
+        with nc.allow_non_contiguous_dma(reason="one bias value a partition"):
+            nc.sync.dma_start(out=b3_t[:], in_=b3.rearrange("(c p) -> p c", p=P))
 
         root = keep.tile([P, n3, PACK], F32, name="root")
-        nc.scalar.activation(root[:], kap_t[:, :, 0:PACK], ACT.Abs_reciprocal_sqrt)
+        nc.scalar.activation(root[:], kap_t[:], ACT.Abs_reciprocal_sqrt)
 
         grouped, w1_w, w1_s = {}, {}, {}
 
@@ -118,8 +129,7 @@ def tile_list_subcatchment_nitrate_loads_kernel(
                     in_=flat[:, PACK * i * width : PACK * (i + 1) * width],
                 )
 
-        v_s = keep.tile([P, S], U8, name="v_s", align_bytes=64)
-        v_w = [keep.tile([P, S], U32, name="v_w0", align_bytes=64)]
+        v_w = [keep.tile([P, S], U32, name="v_w%d" % a, align_bytes=64) for a in range(n1)]
         h = {}
 
         def basin_pass(acc, b, t, u, a):
@@ -133,18 +143,16 @@ def tile_list_subcatchment_nitrate_loads_kernel(
 
         def empty_basin(acc, b, t, u, on_vector):
             if u == 0:
-                if b == 0:
-                    h[b, t] = stage.tile([P, S], F32, name="h0%d" % t, align_bytes=64, offset=AT_H0[t])
-                else:
-                    h[b, t] = keep.tile([P, S], F32, name="h1%d" % t)
+                h[b, t] = stage.tile([P, S], F32, name="h%d%d" % (b, t), align_bytes=64, offset=AT_H[b, t])
             run = slice(u * BANK, (u + 1) * BANK)
             if on_vector:
                 nc.vector.tensor_copy(out=h[b, t][:, run], in_=acc[:])
             else:
                 nc.scalar.copy(out=h[b, t][:, run], in_=acc[:])
 
-        units = [(0, 0, M), (1, 0, 2 * CHUNK), (1, 2 * CHUNK, CHUNK), (1, 3 * CHUNK, CHUNK)]
-        picked = {u: keep.tile([P, PACK, u[2]], F32, name="picked%d_%d" % u[:2]) for u in units}
+        half = M // 2
+        units = [(0, 0, M), (1, 0, half), (1, half, half)]
+        picked = {units[0]: keep.tile([P, PACK, M], F32, name="picked0")}
 
         def pick(unit, t):
             b, m0, width = unit
@@ -168,19 +176,21 @@ def tile_list_subcatchment_nitrate_loads_kernel(
             v2_w[a] = stage.tile([P, M], U32, name="v2_w%d" % a, align_bytes=64, offset=AT_V2[a])
             nc.vector.tensor_copy(v2_w[a][:], tab2_w[a][:].bitcast(U32).indirect(offs2_t[:]))
 
-        def own_passes(acc, b, t, run):
+        def own_pass(b, t, a):
+            if a == 0:
+                own[b, t] = bank(4 * (1 - b) + t)
             c0 = b * PASS + t * P
-            for a in range(n2):
-                nc.tensor.matmul_mx(
-                    out=acc, lhsT=w4_w[:, a, 2 * c0 : 2 * (c0 + P)].bitcast(FP4X4), lhsT_scale=w4_s[a][:, c0 : c0 + P],
-                    rhs=v2_w[a][:, run].bitcast(FP8X4), rhs_scale=v2_s[a][:, run],
-                    start=(a == 0), stop=(a == n2 - 1),
-                )
+            nc.tensor.matmul_mx(
+                out=own[b, t][:], lhsT=w4_w[:, a, 2 * c0 : 2 * (c0 + P)].bitcast(FP4X4), lhsT_scale=w4_s[a][:, c0 : c0 + P],
+                rhs=v2_w[a][:].bitcast(FP8X4), rhs_scale=v2_s[a][:],
+                start=(a == 0), stop=(a == n2 - 1),
+            )
 
-        def ratio(unit, t, acc, m0, width):
-            x = picked[unit][:, t, m0 - unit[1] : m0 - unit[1] + width]
+        def ratio(unit, t):
+            b, m0, width = unit
+            x = picked[unit][:, t, :]
             nc.vector.scalar_tensor_tensor(
-                out=x, in0=acc, scalar=b2_t[:, unit[0], t : t + 1], in1=x, op0=ALU.add, op1=ALU.mult
+                out=x, in0=own[b, t][:, m0 : m0 + width], scalar=b2_t[:, b, t : t + 1], in1=x, op0=ALU.add, op1=ALU.mult
             )
 
         z_w = [keep.tile([P, M], U32, name="z_w%d" % b, align_bytes=64) for b in range(n3)]
@@ -216,30 +226,19 @@ def tile_list_subcatchment_nitrate_loads_kernel(
             else:
                 nc.scalar.activation(res, acc, ACT.Identity, bias=b3_t[:, c : c + 1])
 
-        tab_w = [load_words("tab_w%d" % a, tab_words[a], AT_TAB[a]) for a in range(n1)]
-        nc.vector.tensor_copy(v_s[:], tab_s[:].indirect(offs_t[:]))
         cast_w1(0, 0, 0)
+        tab_w.append(load_words("tab_w1", tab_words[1], AT_TAB[1]))
         w1_raw[1, 0] = load_w1(1, 0)
-        w1_raw[0, 1] = load_w1(0, 1)
         quantise_w1(0, 0, 1)
+        w1_raw[0, 1] = load_w1(0, 1)
         w1_raw[1, 1] = load_w1(1, 1)
-        tab2_s = stage.tile([P, T2], U8, name="tab2_s", align_bytes=64, offset=AT_TAB2_S)
-        w4_s_raw = stage.tile([P, H], U8, name="w4_s_raw", align_bytes=64, offset=AT_W4_S_RAW)
-        nc.vector.memset(tab2_s[:].bitcast(I32), 0)
-        nc.vector.memset(w4_s_raw[:].bitcast(I32), 0)
-        load_scale_rows(nc.sync, tab2_s, tab2_scales, 0)
-        load_scale_rows(nc.sync, w4_s_raw, w4_scales, 0)
         nc.vector.tensor_copy(v_w[0][:], tab_w[0][:].bitcast(U32).indirect(offs_t[:]))
-        b2_t = stage.tile([P, n3, PACK], F32, name="b2_t", align_bytes=64, offset=AT_B2)
-        b3_t = stage.tile([P, N // P], F32, name="b3_t", align_bytes=64, offset=AT_B3)
-        nc.sync.dma_start(out=b2_t[:], in_=b2.rearrange("(b p t) -> p b t", p=P, t=PACK))
-        with nc.allow_non_contiguous_dma(reason="one bias value a partition"):
-            nc.sync.dma_start(out=b3_t[:], in_=b3.rearrange("(c p) -> p c", p=P))
+        v_s = stage.tile([P, S], U8, name="v_s", align_bytes=64, offset=AT_V_S)
+        nc.vector.tensor_copy(v_s[:], tab_s[:].indirect(offs_t[:]))
         slots = [(t, u) for t in range(PACK) for u in range(S // BANK)]
         acc0 = {(t, u): bank(2 * t + u) for t, u in slots}
         for t, u in slots:
             basin_pass(acc0[t, u], 0, t, u, 0)
-        v_w.append(stage.tile([P, S], U32, name="v_w1", align_bytes=64, offset=AT_V1))
         nc.vector.tensor_copy(v_w[1][:], tab_w[1][:].bitcast(U32).indirect(offs_t[:]))
         tab2_w = {0: load_words("tab2_w0", tab2_words[0], AT_TAB2[0])}
         w4_raw = stage.tile([P, n2, H // 2], I32, name="w4_raw", align_bytes=64, offset=AT_W4_RAW)
@@ -259,12 +258,19 @@ def tile_list_subcatchment_nitrate_loads_kernel(
                     in_=planes[0][4 * a : 4 * a + SHIFT_ROWS, :].bitcast(I32),
                 )
 
-        cast_w1(0, 1, P)
         pick(units[0], 0)
-        quantise_w1(0, 1, 1)
-        cast_w1(1, 1, 0)
+        cast_w1(0, 1, 0)
         pick(units[0], 1)
+        cast_w1(1, 1, 0)
         pick(units[0], 2)
+        pick(units[0], 3)
+        quantise_w1(0, 1, 1)
+        quantise_w1(1, 1, 1)
+        for t, u in slots:
+            acc = bank((2 * t + u) % 4)
+            for a in range(n1):
+                basin_pass(acc, 1, t, u, a)
+            empty_basin(acc, 1, t, u, False)
         v2_s = [stage.tile([P, M], U8, name="v2_s0", align_bytes=64, offset=AT_V2_S)]
         v2_s.extend(keep.tile([P, M], U8, name="v2_s%d" % a, align_bytes=64) for a in range(1, n2))
         nc.vector.tensor_copy(v2_s[0][:], tab2_s[:].indirect(offs2_t[:]))
@@ -276,77 +282,65 @@ def tile_list_subcatchment_nitrate_loads_kernel(
             in_=w4_s_raw[:].rearrange("p (b c i t) -> p b c t i", t=PACK, c=8, i=16),
         )
         shift_planes(w4_s)
-        quantise_w1(1, 1, 1)
-        pick(units[0], 3)
-        for t, u in slots:
-            acc = bank((2 * t + u) % 4)
-            for a in range(n1):
-                basin_pass(acc, 1, t, u, a)
-            empty_basin(acc, 1, t, u, False)
         gather_v2(0)
         w4_w = stage.tile([P, n2, 2 * H], U8, name="w4_w", align_bytes=64, offset=AT_W4)
         nc.vector.tensor_copy(
-            out=w4_w[:].bitcast(U16).rearrange("p a (b t c i) -> p (a b) c t i", t=PACK, c=16, i=8),
-            in_=w4_raw[:].bitcast(U16).rearrange("p a (b c i t) -> p (a b) c t i", t=PACK, c=16, i=8),
+            out=w4_w[:].bitcast(U16).rearrange("p a (b t m) -> p (a b) m t", t=PACK, m=P),
+            in_=w4_raw[:].bitcast(U16).rearrange("p a (b m t) -> p (a b) m t", t=PACK, m=P),
         )
-        w8_s = stage.tile([P, N], U8, name="w8_s", align_bytes=64, offset=AT_W8_S)
-        load_scale_rows(nc.sync, w8_s, w8_scales, 0)
         gather_v2(1)
         w8_w = stage.tile([P, n3, N], I32, name="w8_w", align_bytes=64, offset=AT_W8)
         nc.sync.dma_start(out=w8_w[:], in_=w8_words.rearrange("a p n t -> p a (n t)").bitcast(I32))
+        w8_s = stage.tile([P, N], U8, name="w8_s", align_bytes=64, offset=AT_W8_S)
+        load_scale_rows(nc.sync, w8_s, w8_scales, 0)
         reciprocal(units[0], (0, 1))
         reciprocal(units[0], (2, 3))
-        pick(units[1], 0)
-        pick(units[1], 1)
         gather_v2(2)
-        pick(units[1], 2)
-        pick(units[1], 3)
-        for unit in units[2:]:
+        for i in range(2):
+            picked[units[1 + i]] = stage.tile([P, PACK, half], F32, name="picked1_%d" % i, align_bytes=64, offset=AT_PICKED[i])
             for t in range(PACK):
-                pick(unit, t)
+                pick(units[1 + i], t)
+        for a in range(n2):
+            for t in range(PACK):
+                own_pass(0, t, a)
         for t in range(PACK):
-            acc = bank(4 + t)
-            own_passes(acc[:], 0, t, slice(0, M))
-            ratio(units[0], t, acc[:], 0, M)
+            ratio(units[0], t)
         group_z(units[0])
         quantise_z(units[0])
-        for i in range(M // CHUNK):
-            own[i] = bank(i)
-            for t in range(PACK):
-                own_passes(own[i][:, t * CHUNK : (t + 1) * CHUNK], 1, t, slice(i * CHUNK, (i + 1) * CHUNK))
-
-        def places(unit, banks):
-            per_bank = N // P // len(banks)
-            tiles = [bank(i) for i in banks]
-            return [
-                (tiles[c // per_bank][:, (c % per_bank) * unit[2] : (c % per_bank + 1) * unit[2]], c % per_bank == 0, c % per_bank == per_bank - 1)
-                for c in range(N // P)
-            ]
-
-        def finish(unit, place, cs, on_vector):
-            res = keep.tile([P, len(cs), unit[2]], F32, name="res%d_%d" % (unit[1], cs[0]))
-            for j, c in enumerate(cs):
-                add_bias(res[:, j, :], place[c][0], c, on_vector)
-            nc.sync.dma_start(
-                out=out[cs[0] * P : (cs[-1] + 1) * P, unit[1] : unit[1] + unit[2]].rearrange("(j p) m -> p j m", p=P), in_=res[:]
-            )
-
-        score = {}
-        for unit, banks in zip(units[1:], ((4, 5, 6), (7, 0), (1, 2))):
-            score[unit] = places(unit, banks)
-            for c, (acc, first, last) in enumerate(score[unit]):
-                score_pass(acc, unit, c, 0, first, False)
-            reciprocal(unit, range(PACK))
-            for i in range(unit[1] // CHUNK, (unit[1] + unit[2]) // CHUNK):
-                for t in range(PACK):
-                    ratio(unit, t, own[i][:, t * CHUNK : (t + 1) * CHUNK], i * CHUNK, CHUNK)
-            group_z(unit)
-            quantise_z(unit)
-            for c, (acc, first, last) in enumerate(score[unit]):
-                score_pass(acc, unit, c, 1, False, last)
+        for t in range(PACK):
+            for a in range(n2):
+                own_pass(1, t, a)
+        first = [bank(4 + pair) for pair in range(3)]
+        for c in range(N // P):
+            score_pass(first[c // 2][:, (c % 2) * half : (c % 2 + 1) * half], units[1], c, 0, c % 2 == 0, False)
+        reciprocal(units[1], range(PACK))
+        for t in range(PACK):
+            ratio(units[1], t)
+        group_z(units[1])
+        quantise_z(units[1])
+        for c in range(N // P):
+            score_pass(first[c // 2][:, (c % 2) * half : (c % 2 + 1) * half], units[1], c, 1, False, c % 2 == 1)
+        reciprocal(units[2], range(PACK))
+        for t in range(PACK):
+            ratio(units[2], t)
+        group_z(units[2])
+        quantise_z(units[2])
         for pair in range(3):
-            finish(units[1], score[units[1]], (2 * pair, 2 * pair + 1), False)
-        finish(units[2], score[units[2]], (0, 1, 2), False)
-        finish(units[2], score[units[2]], (3, 4, 5), False)
-        finish(units[3], score[units[3]], (0, 1, 2), True)
-        finish(units[3], score[units[3]], (3, 4, 5), False)
+            res = keep.tile([P, 2, half], F32, name="res_first%d" % pair)
+            for j in range(2):
+                add_bias(res[:, j, :], first[pair][:, j * half : (j + 1) * half], 2 * pair + j, False)
+            nc.sync.dma_start(
+                out=out[2 * pair * P : 2 * (pair + 1) * P, 0:half].rearrange("(j p) m -> p j m", p=P), in_=res[:]
+            )
+        second = [bank((7 + c) % 8) for c in range(N // P)]
+        for c in range(N // P):
+            score_pass(second[c][:, 0:half], units[2], c, 0, True, False)
+        for pair in range(3):
+            res = keep.tile([P, 2, half], F32, name="res_second%d" % pair)
+            for j in range(2):
+                c = 2 * pair + j
+                score_pass(second[c][:, 0:half], units[2], c, 1, False, True)
+                add_bias(res[:, j, :], second[c][:, 0:half], c, j == 0)
+            nc.sync.dma_start(
+                out=out[2 * pair * P : 2 * (pair + 1) * P, half:M].rearrange("(j p) m -> p j m", p=P), in_=res[:]
+            )

@@ -1,6 +1,7 @@
 from contextlib import ExitStack
 
 import concourse.mybir as mybir
+from concourse.masks import make_identity
 
 K, K2, H, N, T, T2, S, M = 1024, 1536, 1024, 768, 4096, 2048, 1024, 512
 FLOPS = 2 * (K * H * S + K2 * H * M + H * N * M)
@@ -78,31 +79,41 @@ def tile_list_subcatchment_nitrate_loads_kernel(
         tab2_s = stage.tile([P, T2], U8, name="tab2_s", align_bytes=64, offset=AT_TAB2_S)
         w4_s_raw = stage.tile([P, H], U8, name="w4_s_raw", align_bytes=64, offset=AT_W4_S_RAW)
         nc.vector.memset(tab_s[:].bitcast(I32), 0)
+        rows = keep.tile([P, PASS], F32, name="rows")
+        nc.vector.memset(rows[:], 0.0)
         nc.vector.memset(tab2_s[:].bitcast(I32), 0)
         nc.vector.memset(w4_s_raw[:].bitcast(I32), 0)
 
         offs_t = lists.tile([P, S // 16], U16, name="offs_t")
         pos_t = lists.tile([P, M // 16], U16, name="pos_t")
         offs2_t = lists.tile([P, M // 16], U16, name="offs2_t")
-        kap_t = keep.tile([P, n3, PACK], F32, name="kap_t")
-        b2_t = keep.tile([P, n3, PACK], F32, name="b2_t")
-        b3_t = keep.tile([P, N // P], F32, name="b3_t")
+        identity = keep.tile([P, P], F32, name="identity")
+        make_identity(nc, identity[:])
 
         load_scale_rows(nc.gpsimd, tab_s, tab_scales, TAB_PLANE)
         load_scale_rows(nc.gpsimd, tab2_s, tab2_scales, 0)
         load_scale_rows(nc.gpsimd, w4_s_raw, w4_scales, 0)
-        nc.sync.dma_start(out=kap_t[:], in_=kap.rearrange("(b p t) -> p b t", p=P, t=PACK))
         w1_raw = {(0, 0): load_w1(0, 0)}
         nc.sync.dma_start(offs_t[:], offs)
         tab_w = [load_words("tab_w0", tab_words[0], AT_TAB[0])]
         nc.sync.dma_start(offs2_t[:], offs2)
         nc.sync.dma_start(pos_t[:], pos1)
-        nc.sync.dma_start(out=b2_t[:], in_=b2.rearrange("(b p t) -> p b t", p=P, t=PACK))
-        with nc.allow_non_contiguous_dma(reason="one bias value a partition"):
-            nc.sync.dma_start(out=b3_t[:], in_=b3.rearrange("(c p) -> p c", p=P))
+        nc.sync.dma_start(out=rows[0:n3, :], in_=kap.rearrange("(b c) -> b c", b=n3))
+        nc.sync.dma_start(out=rows[n3 : 2 * n3, :], in_=b2.rearrange("(b c) -> b c", b=n3))
+        nc.sync.dma_start(out=rows[2 * n3 : 2 * n3 + N // P, 0:P], in_=b3.rearrange("(c p) -> c p", p=P))
 
-        root = keep.tile([P, n3, PACK], F32, name="root")
-        nc.scalar.activation(root[:], kap_t[:], ACT.Abs_reciprocal_sqrt)
+        by_slot = bank(6)
+        for t in range(PACK):
+            nc.tensor.transpose(by_slot[:, t * P : (t + 1) * P], rows[:, t:PASS:PACK], identity[:])
+        by_tile = bank(7)
+        nc.tensor.transpose(by_tile[:, 0:P], rows[:, 0:P], identity[:])
+        slot_rows = by_slot[:].rearrange("p (t r) -> p t r", t=PACK)
+        root = keep.tile([P, PACK, n3], F32, name="root")
+        b2_t = keep.tile([P, PACK, n3], F32, name="b2_t")
+        b3_t = keep.tile([P, N // P], F32, name="b3_t")
+        nc.scalar.activation(root[:], slot_rows[:, :, 0:n3], ACT.Abs_reciprocal_sqrt)
+        nc.scalar.copy(out=b2_t[:], in_=slot_rows[:, :, n3 : 2 * n3])
+        nc.scalar.copy(out=b3_t[:], in_=by_tile[:, 2 * n3 : 2 * n3 + N // P])
 
         grouped, w1_w, w1_s = {}, {}, {}
 
@@ -161,13 +172,13 @@ def tile_list_subcatchment_nitrate_loads_kernel(
         def reciprocal(unit, ts):
             for t in ts:
                 x = picked[unit][:, t, :]
-                nc.scalar.activation(x, x, ACT.Square, scale=root[:, unit[0], t : t + 1])
+                nc.scalar.activation(x, x, ACT.Square, scale=root[:, t, unit[0] : unit[0] + 1])
             for t in ts:
                 x = picked[unit][:, t, :]
                 nc.scalar.activation(x, x, ACT.Abs_reciprocal_sqrt, bias=1.0)
             for t in ts:
                 x = picked[unit][:, t, :]
-                nc.scalar.activation(x, x, ACT.Square, scale=root[:, unit[0], t : t + 1])
+                nc.scalar.activation(x, x, ACT.Square, scale=root[:, t, unit[0] : unit[0] + 1])
 
         v2_w = {}
         own = {}
@@ -190,7 +201,7 @@ def tile_list_subcatchment_nitrate_loads_kernel(
             b, m0, width = unit
             x = picked[unit][:, t, :]
             nc.vector.scalar_tensor_tensor(
-                out=x, in0=own[b, t][:, m0 : m0 + width], scalar=b2_t[:, b, t : t + 1], in1=x, op0=ALU.add, op1=ALU.mult
+                out=x, in0=own[b, t][:, m0 : m0 + width], scalar=b2_t[:, t, b : b + 1], in1=x, op0=ALU.add, op1=ALU.mult
             )
 
         z_w = [keep.tile([P, M], U32, name="z_w%d" % b, align_bytes=64) for b in range(n3)]

@@ -21,22 +21,24 @@ P = 128
 PACK = 4
 PASS = P * PACK
 BANK = 512
+LIST_ROWS = 16
 SHIFT_ROWS = 112
 TAB_PLANE = 8
+VECTOR_SHARE = 88
+
 KIB = 1024
 AT_TAB = (0, 16 * KIB)
 AT_W1 = {(0, 0): 28 * KIB, (1, 0): 32 * KIB, (0, 1): 48 * KIB, (1, 1): 56 * KIB}
-AT_H = {(b, t): (76 + 16 * b + 4 * t) * KIB for b in range(2) for t in range(4)}
-AT_GROUPED = {(0, 0): 54 * KIB, (1, 0): 71 * KIB, (0, 1): AT_H[0, 0], (1, 1): AT_H[0, 1]}
-AT_V_S = 0
+AT_H = {(blk, t): (76 + 16 * blk + 4 * t) * KIB for blk in range(2) for t in range(PACK)}
+AT_GROUPED = {(0, 0): 54 * KIB, (1, 0): 71 * KIB, (0, 1): 72 * KIB, (1, 1): AT_H[0, 0]}
+AT_V_S = AT_TAB[0]
 AT_TAB2_S, AT_W4_S_RAW = 40 * KIB, 42 * KIB
 AT_TAB2 = (16 * KIB, 32 * KIB, 64 * KIB)
 AT_W4_RAW = 24 * KIB
 AT_V2_S, AT_W4_S, AT_W4 = AT_H[0, 2], AT_TAB2_S, AT_TAB2[0]
 AT_V2 = (AT_H[0, 3], AT_W4_RAW, AT_TAB2[1] + 4 * KIB)
 AT_PICKED = (AT_TAB2[1], AT_TAB2[2])
-AT_W8, AT_W8_S = 26 * KIB, 42 * KIB
-VECTOR_SHARE = 88
+AT_W8, AT_W8_S = 26 * KIB, AT_W4_S_RAW
 
 
 def tile_list_subcatchment_nitrate_loads_kernel(
@@ -45,6 +47,7 @@ def tile_list_subcatchment_nitrate_loads_kernel(
 ):
     nc = tc.nc
     n1, n2, n3 = K // PASS, K2 // PASS, H // PASS
+    tiles_n = N // P
     with ExitStack() as ctx:
         lists = ctx.enter_context(tc.tile_pool(name="lists", bufs=1))
         keep = ctx.enter_context(tc.tile_pool(name="keep", bufs=1))
@@ -55,9 +58,9 @@ def tile_list_subcatchment_nitrate_loads_kernel(
             return psum.tile([P, BANK], F32, name="bank%d" % i)
 
         def load_words(name, src, offset):
-            t = stage.tile([P, src.shape[1]], I32, name=name, align_bytes=64, offset=offset)
-            nc.sync.dma_start(out=t[:], in_=src.rearrange("p n t -> p (n t)").bitcast(I32))
-            return t
+            words = stage.tile([P, src.shape[1]], I32, name=name, align_bytes=64, offset=offset)
+            nc.sync.dma_start(out=words[:], in_=src.rearrange("p n t -> p (n t)").bitcast(I32))
+            return words
 
         def load_scale_rows(queue, dst, src, first):
             passes = src.shape[0]
@@ -67,11 +70,11 @@ def tile_list_subcatchment_nitrate_loads_kernel(
                     in_=src[:, 4 * q : 4 * q + 4, :].bitcast(I32),
                 )
 
-        def load_w1(a, b):
-            raw = stage.tile([P, PACK, PASS], F32, name="w1_raw%d%d" % (a, b), align_bytes=64, offset=AT_W1[a, b])
+        def load_w1(a, blk):
+            raw = stage.tile([P, PACK, PASS], F32, name="w1_raw%d%d" % (a, blk), align_bytes=64, offset=AT_W1[a, blk])
             nc.sync.dma_start(
                 out=raw[:],
-                in_=w1[a * PASS : (a + 1) * PASS, b * PASS : (b + 1) * PASS].rearrange("(p j) c -> p j c", j=PACK),
+                in_=w1[a * PASS : (a + 1) * PASS, blk * PASS : (blk + 1) * PASS].rearrange("(p j) c -> p j c", j=PACK),
             )
             return raw
 
@@ -84,9 +87,9 @@ def tile_list_subcatchment_nitrate_loads_kernel(
         nc.vector.memset(tab2_s[:].bitcast(I32), 0)
         nc.vector.memset(w4_s_raw[:].bitcast(I32), 0)
 
-        offs_t = lists.tile([P, S // 16], U16, name="offs_t")
-        pos_t = lists.tile([P, M // 16], U16, name="pos_t")
-        offs2_t = lists.tile([P, M // 16], U16, name="offs2_t")
+        offs_t = lists.tile([P, S // LIST_ROWS], U16, name="offs_t")
+        pos_t = lists.tile([P, M // LIST_ROWS], U16, name="pos_t")
+        offs2_t = lists.tile([P, M // LIST_ROWS], U16, name="offs2_t")
         identity = keep.tile([P, P], F32, name="identity")
         make_identity(nc, identity[:])
 
@@ -98,10 +101,11 @@ def tile_list_subcatchment_nitrate_loads_kernel(
         tab_w = [load_words("tab_w0", tab_words[0], AT_TAB[0])]
         nc.sync.dma_start(offs2_t[:], offs2)
         nc.sync.dma_start(pos_t[:], pos1)
-        nc.sync.dma_start(out=rows[0:n3, :], in_=kap.rearrange("(b c) -> b c", b=n3))
-        nc.sync.dma_start(out=rows[n3 : 2 * n3, :], in_=b2.rearrange("(b c) -> b c", b=n3))
-        nc.sync.dma_start(out=rows[2 * n3 : 2 * n3 + N // P, 0:P], in_=b3.rearrange("(c p) -> c p", p=P))
 
+        b2_row, b3_row = n3, 2 * n3
+        nc.sync.dma_start(out=rows[0:b2_row, :], in_=kap.rearrange("(b c) -> b c", b=n3))
+        nc.sync.dma_start(out=rows[b2_row:b3_row, :], in_=b2.rearrange("(b c) -> b c", b=n3))
+        nc.sync.dma_start(out=rows[b3_row : b3_row + tiles_n, 0:P], in_=b3.rearrange("(c p) -> c p", p=P))
         by_slot = bank(6)
         for t in range(PACK):
             nc.tensor.transpose(by_slot[:, t * P : (t + 1) * P], rows[:, t:PASS:PACK], identity[:])
@@ -110,75 +114,73 @@ def tile_list_subcatchment_nitrate_loads_kernel(
         slot_rows = by_slot[:].rearrange("p (t r) -> p t r", t=PACK)
         root = keep.tile([P, PACK, n3], F32, name="root")
         b2_t = keep.tile([P, PACK, n3], F32, name="b2_t")
-        b3_t = keep.tile([P, N // P], F32, name="b3_t")
-        nc.scalar.activation(root[:], slot_rows[:, :, 0:n3], ACT.Abs_reciprocal_sqrt)
-        nc.scalar.copy(out=b2_t[:], in_=slot_rows[:, :, n3 : 2 * n3])
-        nc.scalar.copy(out=b3_t[:], in_=by_tile[:, 2 * n3 : 2 * n3 + N // P])
+        b3_t = keep.tile([P, tiles_n], F32, name="b3_t")
+        nc.scalar.activation(root[:], slot_rows[:, :, 0:b2_row], ACT.Abs_reciprocal_sqrt)
+        nc.scalar.copy(out=b2_t[:], in_=slot_rows[:, :, b2_row:b3_row])
+        nc.scalar.copy(out=b3_t[:], in_=by_tile[:, b3_row : b3_row + tiles_n])
 
         grouped, w1_w, w1_s = {}, {}, {}
 
-        def cast_w1(a, b, vector_share):
-            grouped[a, b] = stage.tile(
-                [P, PACK, P, PACK], BF16, name="w1_grouped%d%d" % (a, b), align_bytes=64, offset=AT_GROUPED[a, b]
+        def cast_w1(a, blk, vector_share):
+            grouped[a, blk] = stage.tile(
+                [P, PACK, P, PACK], BF16, name="w1_grouped%d%d" % (a, blk), align_bytes=64, offset=AT_GROUPED[a, blk]
             )
-            src = w1_raw[a, b][:].rearrange("p j (m t) -> p m j t", t=PACK)
-            dst = grouped[a, b][:].rearrange("p t m j -> p m j t")
+            src = w1_raw[a, blk][:].rearrange("p j (m t) -> p m j t", t=PACK)
+            dst = grouped[a, blk][:].rearrange("p t m j -> p m j t")
             if vector_share > 0:
                 nc.vector.tensor_copy(out=dst[:, 0:vector_share], in_=src[:, 0:vector_share])
             if vector_share < P:
                 nc.scalar.copy(out=dst[:, vector_share:P], in_=src[:, vector_share:P])
 
-        def quantise_w1(a, b, pieces):
-            w1_w[a, b] = keep.tile([P, PASS], U32, name="w1_w%d%d" % (a, b), align_bytes=64)
-            w1_s[a, b] = keep.tile([P, PASS], U8, name="w1_s%d%d" % (a, b), align_bytes=64)
-            flat = grouped[a, b][:].rearrange("p t m j -> p (t m j)")
+        def quantise_w1(a, blk, pieces):
+            w1_w[a, blk] = keep.tile([P, PASS], U32, name="w1_w%d%d" % (a, blk), align_bytes=64)
+            w1_s[a, blk] = keep.tile([P, PASS], U8, name="w1_s%d%d" % (a, blk), align_bytes=64)
+            flat = grouped[a, blk][:].rearrange("p t m j -> p (t m j)")
             width = PASS // pieces
             for i in range(pieces):
                 nc.vector.quantize_mx(
-                    out=w1_w[a, b][:, i * width : (i + 1) * width].bitcast(FP8X4),
-                    scales=w1_s[a, b][:, i * width : (i + 1) * width],
+                    out=w1_w[a, blk][:, i * width : (i + 1) * width].bitcast(FP8X4),
+                    scales=w1_s[a, blk][:, i * width : (i + 1) * width],
                     in_=flat[:, PACK * i * width : PACK * (i + 1) * width],
                 )
 
         v_w = [keep.tile([P, S], U32, name="v_w%d" % a, align_bytes=64) for a in range(n1)]
         h = {}
 
-        def basin_pass(acc, b, t, u, a):
+        def basin_pass(acc, blk, t, u, a):
             cols = slice(t * P, (t + 1) * P)
             run = slice(u * BANK, (u + 1) * BANK)
             nc.tensor.matmul_mx(
-                out=acc[:], lhsT=w1_w[a, b][:, cols].bitcast(FP8X4), lhsT_scale=w1_s[a, b][:, cols],
+                out=acc[:], lhsT=w1_w[a, blk][:, cols].bitcast(FP8X4), lhsT_scale=w1_s[a, blk][:, cols],
                 rhs=v_w[a][:, run].bitcast(FP8X4), rhs_scale=v_s[TAB_PLANE + 4 * a : P, run],
                 start=(a == 0), stop=(a == n1 - 1),
             )
 
-        def empty_basin(acc, b, t, u, on_vector):
+        def empty_basin(acc, blk, t, u):
             if u == 0:
-                h[b, t] = stage.tile([P, S], F32, name="h%d%d" % (b, t), align_bytes=64, offset=AT_H[b, t])
-            run = slice(u * BANK, (u + 1) * BANK)
-            if on_vector:
-                nc.vector.tensor_copy(out=h[b, t][:, run], in_=acc[:])
-            else:
-                nc.scalar.copy(out=h[b, t][:, run], in_=acc[:])
+                h[blk, t] = stage.tile([P, S], F32, name="h%d%d" % (blk, t), align_bytes=64, offset=AT_H[blk, t])
+            nc.scalar.copy(out=h[blk, t][:, u * BANK : (u + 1) * BANK], in_=acc[:])
 
         half = M // 2
-        units = [(0, 0, M), (1, 0, half), (1, half, half)]
-        picked = {units[0]: keep.tile([P, PACK, M], F32, name="picked0")}
+        parts = [(0, 0, M), (1, 0, half), (1, half, half)]
+        picked = {parts[0]: keep.tile([P, PACK, M], F32, name="picked0")}
 
-        def pick(unit, t):
-            b, m0, width = unit
-            nc.vector.tensor_copy(picked[unit][:, t, :], h[b, t][:].indirect(pos_t[:, m0 // 16 : (m0 + width) // 16]))
+        def pick(part, t):
+            blk, m0, width = part
+            entries = pos_t[:, m0 // LIST_ROWS : (m0 + width) // LIST_ROWS]
+            nc.vector.tensor_copy(picked[part][:, t, :], h[blk, t][:].indirect(entries))
 
-        def reciprocal(unit, ts):
+        def reciprocal(part, ts):
+            blk = part[0]
             for t in ts:
-                x = picked[unit][:, t, :]
-                nc.scalar.activation(x, x, ACT.Square, scale=root[:, t, unit[0] : unit[0] + 1])
+                x = picked[part][:, t, :]
+                nc.scalar.activation(x, x, ACT.Square, scale=root[:, t, blk : blk + 1])
             for t in ts:
-                x = picked[unit][:, t, :]
+                x = picked[part][:, t, :]
                 nc.scalar.activation(x, x, ACT.Abs_reciprocal_sqrt, bias=1.0)
             for t in ts:
-                x = picked[unit][:, t, :]
-                nc.scalar.activation(x, x, ACT.Square, scale=root[:, t, unit[0] : unit[0] + 1])
+                x = picked[part][:, t, :]
+                nc.scalar.activation(x, x, ACT.Square, scale=root[:, t, blk : blk + 1])
 
         v2_w = {}
         own = {}
@@ -187,48 +189,52 @@ def tile_list_subcatchment_nitrate_loads_kernel(
             v2_w[a] = stage.tile([P, M], U32, name="v2_w%d" % a, align_bytes=64, offset=AT_V2[a])
             nc.vector.tensor_copy(v2_w[a][:], tab2_w[a][:].bitcast(U32).indirect(offs2_t[:]))
 
-        def own_pass(b, t, a):
+        def shift_planes(planes):
+            for a in range(1, n2):
+                nc.sync.dma_start(
+                    out=planes[a][0:SHIFT_ROWS, :].bitcast(I32),
+                    in_=planes[0][4 * a : 4 * a + SHIFT_ROWS, :].bitcast(I32),
+                )
+
+        def own_pass(blk, t, a):
             if a == 0:
-                own[b, t] = bank(4 * (1 - b) + t)
-            c0 = b * PASS + t * P
+                own[blk, t] = bank(PACK * (1 - blk) + t)
+            c0 = blk * PASS + t * P
             nc.tensor.matmul_mx(
-                out=own[b, t][:], lhsT=w4_w[:, a, 2 * c0 : 2 * (c0 + P)].bitcast(FP4X4), lhsT_scale=w4_s[a][:, c0 : c0 + P],
+                out=own[blk, t][:], lhsT=w4_w[:, a, 2 * c0 : 2 * (c0 + P)].bitcast(FP4X4), lhsT_scale=w4_s[a][:, c0 : c0 + P],
                 rhs=v2_w[a][:].bitcast(FP8X4), rhs_scale=v2_s[a][:],
                 start=(a == 0), stop=(a == n2 - 1),
             )
 
-        def ratio(unit, t):
-            b, m0, width = unit
-            x = picked[unit][:, t, :]
+        def ratio(part, t):
+            blk, m0, width = part
+            x = picked[part][:, t, :]
             nc.vector.scalar_tensor_tensor(
-                out=x, in0=own[b, t][:, m0 : m0 + width], scalar=b2_t[:, t, b : b + 1], in1=x, op0=ALU.add, op1=ALU.mult
+                out=x, in0=own[blk, t][:, m0 : m0 + width], scalar=b2_t[:, t, blk : blk + 1], in1=x, op0=ALU.add, op1=ALU.mult
             )
 
-        z_w = [keep.tile([P, M], U32, name="z_w%d" % b, align_bytes=64) for b in range(n3)]
-        z_s = [keep.tile([P, M], U8, name="z_s%d" % b, align_bytes=64) for b in range(n3)]
-        z_grouped = {}
+        z_w = [keep.tile([P, M], U32, name="z_w%d" % blk, align_bytes=64) for blk in range(n3)]
+        z_s = [keep.tile([P, M], U8, name="z_s%d" % blk, align_bytes=64) for blk in range(n3)]
 
-        def group_z(unit):
-            z_grouped[unit] = keep.tile([P, unit[2], PACK], BF16, name="z_grouped%d_%d" % unit[:2], align_bytes=64)
+        def quantise_z(part):
+            blk, m0, width = part
+            z_grouped = keep.tile([P, width, PACK], BF16, name="z_grouped%d_%d" % (blk, m0), align_bytes=64)
             nc.vector.tensor_scalar_max(
-                out=z_grouped[unit][:].rearrange("p (c i) t -> p c t i", i=4),
-                in0=picked[unit][:].rearrange("p t (c i) -> p c t i", i=4),
+                out=z_grouped[:].rearrange("p (c i) t -> p c t i", i=4),
+                in0=picked[part][:].rearrange("p t (c i) -> p c t i", i=4),
                 scalar1=0.0,
             )
-
-        def quantise_z(unit):
-            b, m0, width = unit
             nc.vector.quantize_mx(
-                out=z_w[b][:, m0 : m0 + width].bitcast(FP8X4), scales=z_s[b][:, m0 : m0 + width],
-                in_=z_grouped[unit][:].rearrange("p m t -> p (m t)"),
+                out=z_w[blk][:, m0 : m0 + width].bitcast(FP8X4), scales=z_s[blk][:, m0 : m0 + width],
+                in_=z_grouped[:].rearrange("p m t -> p (m t)"),
             )
 
-        def score_pass(acc, unit, c, b, start, stop):
-            run = slice(unit[1], unit[1] + unit[2])
+        def score_pass(acc, m0, c, blk, start, stop):
+            run = slice(m0, m0 + half)
             cols = slice(c * P, (c + 1) * P)
             nc.tensor.matmul_mx(
-                out=acc, lhsT=w8_w[:, b, cols].bitcast(FP8X4), lhsT_scale=w8_s[4 * b : P, cols],
-                rhs=z_w[b][:, run].bitcast(FP8X4), rhs_scale=z_s[b][:, run], start=start, stop=stop,
+                out=acc, lhsT=w8_w[:, blk, cols].bitcast(FP8X4), lhsT_scale=w8_s[4 * blk : P, cols],
+                rhs=z_w[blk][:, run].bitcast(FP8X4), rhs_scale=z_s[blk][:, run], start=start, stop=stop,
             )
 
         def add_bias(res, acc, c, on_vector):
@@ -236,6 +242,11 @@ def tile_list_subcatchment_nitrate_loads_kernel(
                 nc.vector.tensor_scalar_add(out=res, in0=acc, scalar1=b3_t[:, c : c + 1])
             else:
                 nc.scalar.activation(res, acc, ACT.Identity, bias=b3_t[:, c : c + 1])
+
+        def store_pair(res, pair, m0):
+            nc.sync.dma_start(
+                out=out[2 * pair * P : 2 * (pair + 1) * P, m0 : m0 + half].rearrange("(j p) m -> p j m", p=P), in_=res[:]
+            )
 
         cast_w1(0, 0, 0)
         tab_w.append(load_words("tab_w1", tab_words[1], AT_TAB[1]))
@@ -246,9 +257,9 @@ def tile_list_subcatchment_nitrate_loads_kernel(
         nc.vector.tensor_copy(v_w[0][:], tab_w[0][:].bitcast(U32).indirect(offs_t[:]))
         v_s = stage.tile([P, S], U8, name="v_s", align_bytes=64, offset=AT_V_S)
         nc.vector.tensor_copy(v_s[:], tab_s[:].indirect(offs_t[:]))
-        slots = [(t, u) for t in range(PACK) for u in range(S // BANK)]
-        acc0 = {(t, u): bank(2 * t + u) for t, u in slots}
-        for t, u in slots:
+        sums = [(t, u) for t in range(PACK) for u in range(S // BANK)]
+        acc0 = {(t, u): bank(2 * t + u) for t, u in sums}
+        for t, u in sums:
             basin_pass(acc0[t, u], 0, t, u, 0)
         nc.vector.tensor_copy(v_w[1][:], tab_w[1][:].bitcast(U32).indirect(offs_t[:]))
         tab2_w = {0: load_words("tab2_w0", tab2_words[0], AT_TAB2[0])}
@@ -258,30 +269,24 @@ def tile_list_subcatchment_nitrate_loads_kernel(
         tab2_w[1] = load_words("tab2_w1", tab2_words[1], AT_TAB2[1])
         quantise_w1(1, 0, PACK)
         tab2_w[2] = load_words("tab2_w2", tab2_words[2], AT_TAB2[2])
-        for t, u in slots:
+        for t, u in sums:
             basin_pass(acc0[t, u], 0, t, u, 1)
-            empty_basin(acc0[t, u], 0, t, u, False)
+            empty_basin(acc0[t, u], 0, t, u)
 
-        def shift_planes(planes):
-            for a in range(1, n2):
-                nc.sync.dma_start(
-                    out=planes[a][0:SHIFT_ROWS, :].bitcast(I32),
-                    in_=planes[0][4 * a : 4 * a + SHIFT_ROWS, :].bitcast(I32),
-                )
-
-        pick(units[0], 0)
-        cast_w1(0, 1, 0)
-        pick(units[0], 1)
-        cast_w1(1, 1, 0)
-        pick(units[0], 2)
-        pick(units[0], 3)
+        cast_w1(0, 1, P)
+        pick(parts[0], 0)
         quantise_w1(0, 1, 1)
+        cast_w1(1, 1, 0)
+        pick(parts[0], 1)
+        pick(parts[0], 2)
         quantise_w1(1, 1, 1)
-        for t, u in slots:
-            acc = bank((2 * t + u) % 4)
+        pick(parts[0], 3)
+        for t, u in sums:
+            acc = bank((2 * t + u) % PACK)
             for a in range(n1):
                 basin_pass(acc, 1, t, u, a)
-            empty_basin(acc, 1, t, u, False)
+            empty_basin(acc, 1, t, u)
+
         v2_s = [stage.tile([P, M], U8, name="v2_s0", align_bytes=64, offset=AT_V2_S)]
         v2_s.extend(keep.tile([P, M], U8, name="v2_s%d" % a, align_bytes=64) for a in range(1, n2))
         nc.vector.tensor_copy(v2_s[0][:], tab2_s[:].indirect(offs2_t[:]))
@@ -304,54 +309,54 @@ def tile_list_subcatchment_nitrate_loads_kernel(
         nc.sync.dma_start(out=w8_w[:], in_=w8_words.rearrange("a p n t -> p a (n t)").bitcast(I32))
         w8_s = stage.tile([P, N], U8, name="w8_s", align_bytes=64, offset=AT_W8_S)
         load_scale_rows(nc.sync, w8_s, w8_scales, 0)
-        reciprocal(units[0], (0, 1))
-        reciprocal(units[0], (2, 3))
+
+        reciprocal(parts[0], (0, 1))
+        reciprocal(parts[0], (2, 3))
         gather_v2(2)
-        for i in range(2):
-            picked[units[1 + i]] = stage.tile([P, PACK, half], F32, name="picked1_%d" % i, align_bytes=64, offset=AT_PICKED[i])
+        for i, part in enumerate(parts[1:]):
+            picked[part] = stage.tile([P, PACK, half], F32, name="picked1_%d" % i, align_bytes=64, offset=AT_PICKED[i])
             for t in range(PACK):
-                pick(units[1 + i], t)
+                pick(part, t)
         for a in range(n2):
             for t in range(PACK):
                 own_pass(0, t, a)
         for t in range(PACK):
-            ratio(units[0], t)
-        group_z(units[0])
-        quantise_z(units[0])
+            ratio(parts[0], t)
+        quantise_z(parts[0])
         for t in range(PACK):
             for a in range(n2):
                 own_pass(1, t, a)
-        first = [bank(4 + pair) for pair in range(3)]
-        for c in range(N // P):
-            score_pass(first[c // 2][:, (c % 2) * half : (c % 2 + 1) * half], units[1], c, 0, c % 2 == 0, False)
-        reciprocal(units[1], range(PACK))
+
+        first = [bank(PACK + pair) for pair in range(tiles_n // 2)]
+
+        def first_place(c):
+            return first[c // 2][:, (c % 2) * half : (c % 2 + 1) * half]
+
+        for c in range(tiles_n):
+            score_pass(first_place(c), 0, c, 0, c % 2 == 0, False)
+        reciprocal(parts[1], range(PACK))
         for t in range(PACK):
-            ratio(units[1], t)
-        group_z(units[1])
-        quantise_z(units[1])
-        for c in range(N // P):
-            score_pass(first[c // 2][:, (c % 2) * half : (c % 2 + 1) * half], units[1], c, 1, False, c % 2 == 1)
-        reciprocal(units[2], range(PACK))
+            ratio(parts[1], t)
+        quantise_z(parts[1])
+        for c in range(tiles_n):
+            score_pass(first_place(c), 0, c, 1, False, c % 2 == 1)
+        reciprocal(parts[2], range(PACK))
         for t in range(PACK):
-            ratio(units[2], t)
-        group_z(units[2])
-        quantise_z(units[2])
-        for pair in range(3):
+            ratio(parts[2], t)
+        quantise_z(parts[2])
+        for pair in range(tiles_n // 2):
             res = keep.tile([P, 2, half], F32, name="res_first%d" % pair)
             for j in range(2):
-                add_bias(res[:, j, :], first[pair][:, j * half : (j + 1) * half], 2 * pair + j, False)
-            nc.sync.dma_start(
-                out=out[2 * pair * P : 2 * (pair + 1) * P, 0:half].rearrange("(j p) m -> p j m", p=P), in_=res[:]
-            )
-        second = [bank((7 + c) % 8) for c in range(N // P)]
-        for c in range(N // P):
-            score_pass(second[c][:, 0:half], units[2], c, 0, True, False)
-        for pair in range(3):
+                add_bias(res[:, j, :], first_place(2 * pair + j), 2 * pair + j, False)
+            store_pair(res, pair, 0)
+
+        second = [bank((7 + c) % 8) for c in range(tiles_n)]
+        for c in range(tiles_n):
+            score_pass(second[c][:, 0:half], half, c, 0, True, False)
+        for pair in range(tiles_n // 2):
             res = keep.tile([P, 2, half], F32, name="res_second%d" % pair)
             for j in range(2):
                 c = 2 * pair + j
-                score_pass(second[c][:, 0:half], units[2], c, 1, False, True)
+                score_pass(second[c][:, 0:half], half, c, 1, False, True)
                 add_bias(res[:, j, :], second[c][:, 0:half], c, j == 0)
-            nc.sync.dma_start(
-                out=out[2 * pair * P : 2 * (pair + 1) * P, half:M].rearrange("(j p) m -> p j m", p=P), in_=res[:]
-            )
+            store_pair(res, pair, half)

@@ -22,23 +22,15 @@ PACK = 4
 PASS = P * PACK
 BANK = 512
 LIST_ROWS = 16
-SHIFT_ROWS = 112
-TAB_PLANE = 8
-VECTOR_SHARE = 88
-
+SCALE_ROWS = 16
 KIB = 1024
-AT_TAB = (0, 16 * KIB)
-AT_W1 = {(0, 0): 28 * KIB, (1, 0): 32 * KIB, (0, 1): 48 * KIB, (1, 1): 56 * KIB}
-AT_H = {(blk, t): (76 + 16 * blk + 4 * t) * KIB for blk in range(2) for t in range(PACK)}
-AT_GROUPED = {(0, 0): 54 * KIB, (1, 0): 71 * KIB, (0, 1): 72 * KIB, (1, 1): AT_H[0, 0]}
-AT_V_S = AT_TAB[0]
-AT_TAB2_S, AT_W4_S_RAW = 40 * KIB, 42 * KIB
-AT_TAB2 = (16 * KIB, 32 * KIB, 64 * KIB)
-AT_W4_RAW = 24 * KIB
-AT_V2_S, AT_W4_S, AT_W4 = AT_H[0, 2], AT_TAB2_S, AT_TAB2[0]
-AT_V2 = (AT_H[0, 3], AT_W4_RAW, AT_TAB2[1] + 4 * KIB)
-AT_PICKED = (AT_TAB2[1], AT_TAB2[2])
-AT_W8, AT_W8_S = 26 * KIB, AT_W4_S_RAW
+
+AT_W1 = {(0, 0): 0, (1, 0): 8 * KIB, (0, 1): 0, (1, 1): 8 * KIB}
+AT_TAB = (16 * KIB, 32 * KIB)
+AT_TAB_S = AT_TAB[1]
+AT_TAB2 = (AT_TAB[0], AT_TAB[1], AT_TAB[1] + 8 * KIB)
+AT_W4_RAW = AT_TAB[0] + 8 * KIB
+AT_W8 = AT_W1[0, 1]
 
 
 def tile_list_subcatchment_nitrate_loads_kernel(
@@ -62,13 +54,20 @@ def tile_list_subcatchment_nitrate_loads_kernel(
             nc.sync.dma_start(out=words[:], in_=src.rearrange("p n t -> p (n t)").bitcast(I32))
             return words
 
-        def load_scale_rows(queue, dst, src, first):
+        def load_scale_rows(dst, src):
             passes = src.shape[0]
-            for q in range(4):
+            nc.sync.dma_start(
+                out=dst[0 : SCALE_ROWS * passes, :].bitcast(I32), in_=src.rearrange("a q n -> q a n").bitcast(I32)
+            )
+
+        def to_planes(queue, name, src, passes):
+            planes = keep.tile([P, passes, src.shape[1]], U8, name=name, align_bytes=64)
+            for g in range(4):
                 queue.dma_start(
-                    out=dst[32 * q + first : 32 * q + first + 4 * passes, :].bitcast(I32),
-                    in_=src[:, 4 * q : 4 * q + 4, :].bitcast(I32),
+                    out=planes[32 * g : 32 * g + 4].bitcast(I32),
+                    in_=src[4 * passes * g : 4 * passes * (g + 1), :].bitcast(I32),
                 )
+            return planes
 
         def load_w1(a, blk):
             raw = stage.tile([P, PACK, PASS], F32, name="w1_raw%d%d" % (a, blk), align_bytes=64, offset=AT_W1[a, blk])
@@ -78,34 +77,48 @@ def tile_list_subcatchment_nitrate_loads_kernel(
             )
             return raw
 
-        tab_s = keep.tile([P, T], U8, name="tab_s", align_bytes=64)
-        tab2_s = stage.tile([P, T2], U8, name="tab2_s", align_bytes=64, offset=AT_TAB2_S)
-        w4_s_raw = stage.tile([P, H], U8, name="w4_s_raw", align_bytes=64, offset=AT_W4_S_RAW)
-        nc.vector.memset(tab_s[:].bitcast(I32), 0)
+        tab_s = stage.tile([P, T], U8, name="tab_s", align_bytes=64, offset=AT_TAB_S)
+        tab2_s = keep.tile([P, T2], U8, name="tab2_s", align_bytes=64)
+        w4_s_raw = keep.tile([P, H], U8, name="w4_s_raw", align_bytes=64)
         rows = keep.tile([P, PASS], F32, name="rows")
         nc.vector.memset(rows[:], 0.0)
         nc.vector.memset(tab2_s[:].bitcast(I32), 0)
         nc.vector.memset(w4_s_raw[:].bitcast(I32), 0)
+        nc.vector.memset(tab_s[32:64, :].bitcast(I32), 0)
+        nc.vector.memset(tab_s[64:P, :].bitcast(I32), 0)
 
         offs_t = lists.tile([P, S // LIST_ROWS], U16, name="offs_t")
         pos_t = lists.tile([P, M // LIST_ROWS], U16, name="pos_t")
         offs2_t = lists.tile([P, M // LIST_ROWS], U16, name="offs2_t")
-        identity = keep.tile([P, P], F32, name="identity")
-        make_identity(nc, identity[:])
 
-        load_scale_rows(nc.gpsimd, tab_s, tab_scales, TAB_PLANE)
-        load_scale_rows(nc.gpsimd, tab2_s, tab2_scales, 0)
-        load_scale_rows(nc.gpsimd, w4_s_raw, w4_scales, 0)
-        w1_raw = {(0, 0): load_w1(0, 0)}
         nc.sync.dma_start(offs_t[:], offs)
-        tab_w = [load_words("tab_w0", tab_words[0], AT_TAB[0])]
+        load_scale_rows(tab_s, tab_scales)
+        w1_raw = {(0, 0): load_w1(0, 0)}
         nc.sync.dma_start(offs2_t[:], offs2)
         nc.sync.dma_start(pos_t[:], pos1)
+        w1_raw[1, 0] = load_w1(1, 0)
+        tab_w = [load_words("tab_w0", tab_words[0], AT_TAB[0])]
+        load_scale_rows(tab2_s, tab2_scales)
+        load_scale_rows(w4_s_raw, w4_scales)
 
         b2_row, b3_row = n3, 2 * n3
-        nc.sync.dma_start(out=rows[0:b2_row, :], in_=kap.rearrange("(b c) -> b c", b=n3))
-        nc.sync.dma_start(out=rows[b2_row:b3_row, :], in_=b2.rearrange("(b c) -> b c", b=n3))
-        nc.sync.dma_start(out=rows[b3_row : b3_row + tiles_n, 0:P], in_=b3.rearrange("(c p) -> c p", p=P))
+        nc.gpsimd.dma_start(out=rows[0:b2_row, :], in_=kap.rearrange("(b c) -> b c", b=n3))
+        nc.gpsimd.dma_start(out=rows[b2_row:b3_row, :], in_=b2.rearrange("(b c) -> b c", b=n3))
+        nc.gpsimd.dma_start(out=rows[b3_row : b3_row + tiles_n, 0:P], in_=b3.rearrange("(c p) -> c p", p=P))
+        identity = keep.tile([P, P], F32, name="identity")
+        make_identity(nc, identity[:])
+        w8_s = keep.tile([P, n3, N], U8, name="w8_s", align_bytes=64)
+        for g in range(4):
+            nc.gpsimd.dma_start(
+                out=w8_s[32 * g : 32 * g + 4].bitcast(I32),
+                in_=w8_scales[:, 4 * g : 4 * g + 4, :].rearrange("a i n -> i a n").bitcast(I32),
+            )
+
+        v_s_rows = keep.tile([P, S], U8, name="v_s_rows", align_bytes=64)
+        nc.vector.tensor_copy(v_s_rows[:], tab_s[:].indirect(offs_t[:]))
+        v_s = to_planes(nc.sync, "v_s", v_s_rows, n1)
+        tab_w.append(load_words("tab_w1", tab_words[1], AT_TAB[1]))
+
         by_slot = bank(6)
         for t in range(PACK):
             nc.tensor.transpose(by_slot[:, t * P : (t + 1) * P], rows[:, t:PASS:PACK], identity[:])
@@ -115,113 +128,93 @@ def tile_list_subcatchment_nitrate_loads_kernel(
         root = keep.tile([P, PACK, n3], F32, name="root")
         b2_t = keep.tile([P, PACK, n3], F32, name="b2_t")
         b3_t = keep.tile([P, tiles_n], F32, name="b3_t")
-        nc.scalar.activation(root[:], slot_rows[:, :, 0:b2_row], ACT.Abs_reciprocal_sqrt)
-        nc.scalar.copy(out=b2_t[:], in_=slot_rows[:, :, b2_row:b3_row])
-        nc.scalar.copy(out=b3_t[:], in_=by_tile[:, b3_row : b3_row + tiles_n])
 
         grouped, w1_w, w1_s = {}, {}, {}
 
-        def cast_w1(a, blk, vector_share):
-            grouped[a, blk] = stage.tile(
-                [P, PACK, P, PACK], BF16, name="w1_grouped%d%d" % (a, blk), align_bytes=64, offset=AT_GROUPED[a, blk]
-            )
+        def cast_w1(a, blk, engine):
+            grouped[a, blk] = keep.tile([P, PACK, P, PACK], BF16, name="w1_grouped%d%d" % (a, blk), align_bytes=64)
             src = w1_raw[a, blk][:].rearrange("p j (m t) -> p m j t", t=PACK)
             dst = grouped[a, blk][:].rearrange("p t m j -> p m j t")
-            if vector_share > 0:
-                nc.vector.tensor_copy(out=dst[:, 0:vector_share], in_=src[:, 0:vector_share])
-            if vector_share < P:
-                nc.scalar.copy(out=dst[:, vector_share:P], in_=src[:, vector_share:P])
+            if engine == "vector":
+                nc.vector.tensor_copy(out=dst, in_=src)
+            else:
+                nc.scalar.copy(out=dst, in_=src)
 
-        def quantise_w1(a, blk, pieces):
+        def quantise_w1(a, blk):
             w1_w[a, blk] = keep.tile([P, PASS], U32, name="w1_w%d%d" % (a, blk), align_bytes=64)
             w1_s[a, blk] = keep.tile([P, PASS], U8, name="w1_s%d%d" % (a, blk), align_bytes=64)
-            flat = grouped[a, blk][:].rearrange("p t m j -> p (t m j)")
-            width = PASS // pieces
-            for i in range(pieces):
-                nc.vector.quantize_mx(
-                    out=w1_w[a, blk][:, i * width : (i + 1) * width].bitcast(FP8X4),
-                    scales=w1_s[a, blk][:, i * width : (i + 1) * width],
-                    in_=flat[:, PACK * i * width : PACK * (i + 1) * width],
-                )
+            nc.vector.quantize_mx(
+                out=w1_w[a, blk][:].bitcast(FP8X4), scales=w1_s[a, blk][:],
+                in_=grouped[a, blk][:].rearrange("p t m j -> p (t m j)"),
+            )
 
         v_w = [keep.tile([P, S], U32, name="v_w%d" % a, align_bytes=64) for a in range(n1)]
-        h = {}
+        h, acc = {}, {}
 
-        def basin_pass(acc, blk, t, u, a):
+        def basin_pass(blk, t, u, a):
+            if a == 0:
+                acc[blk, t, u] = bank(2 * t + u)
             cols = slice(t * P, (t + 1) * P)
             run = slice(u * BANK, (u + 1) * BANK)
             nc.tensor.matmul_mx(
-                out=acc[:], lhsT=w1_w[a, blk][:, cols].bitcast(FP8X4), lhsT_scale=w1_s[a, blk][:, cols],
-                rhs=v_w[a][:, run].bitcast(FP8X4), rhs_scale=v_s[TAB_PLANE + 4 * a : P, run],
+                out=acc[blk, t, u][:], lhsT=w1_w[a, blk][:, cols].bitcast(FP8X4), lhsT_scale=w1_s[a, blk][:, cols],
+                rhs=v_w[a][:, run].bitcast(FP8X4), rhs_scale=v_s[:, a, run],
                 start=(a == 0), stop=(a == n1 - 1),
             )
 
-        def empty_basin(acc, blk, t, u):
+        def empty_basin(blk, t, u):
             if u == 0:
-                h[blk, t] = stage.tile([P, S], F32, name="h%d%d" % (blk, t), align_bytes=64, offset=AT_H[blk, t])
-            nc.scalar.copy(out=h[blk, t][:, u * BANK : (u + 1) * BANK], in_=acc[:])
+                h[blk, t] = keep.tile([P, S], F32, name="h%d%d" % (blk, t), align_bytes=64)
+            nc.scalar.copy(out=h[blk, t][:, u * BANK : (u + 1) * BANK], in_=acc[blk, t, u][:])
 
         half = M // 2
-        parts = [(0, 0, M), (1, 0, half), (1, half, half)]
-        picked = {parts[0]: keep.tile([P, PACK, M], F32, name="picked0")}
+        picked = [keep.tile([P, PACK, M], F32, name="picked%d" % blk) for blk in range(n3)]
 
-        def pick(part, t):
-            blk, m0, width = part
-            entries = pos_t[:, m0 // LIST_ROWS : (m0 + width) // LIST_ROWS]
-            nc.vector.tensor_copy(picked[part][:, t, :], h[blk, t][:].indirect(entries))
+        def pick(blk, t):
+            nc.vector.tensor_copy(picked[blk][:, t, :], h[blk, t][:].indirect(pos_t[:]))
 
-        def reciprocal(part, ts):
-            blk = part[0]
+        def square(blk, ts, m0, width):
             for t in ts:
-                x = picked[part][:, t, :]
+                x = picked[blk][:, t, m0 : m0 + width]
                 nc.scalar.activation(x, x, ACT.Square, scale=root[:, t, blk : blk + 1])
+
+        def inverse_root(blk, ts, m0, width):
             for t in ts:
-                x = picked[part][:, t, :]
+                x = picked[blk][:, t, m0 : m0 + width]
                 nc.scalar.activation(x, x, ACT.Abs_reciprocal_sqrt, bias=1.0)
-            for t in ts:
-                x = picked[part][:, t, :]
-                nc.scalar.activation(x, x, ACT.Square, scale=root[:, t, blk : blk + 1])
 
-        v2_w = {}
-        own = {}
+        v2_w, own, tab2_w = {}, {}, {}
 
         def gather_v2(a):
-            v2_w[a] = stage.tile([P, M], U32, name="v2_w%d" % a, align_bytes=64, offset=AT_V2[a])
+            v2_w[a] = keep.tile([P, M], U32, name="v2_w%d" % a, align_bytes=64)
             nc.vector.tensor_copy(v2_w[a][:], tab2_w[a][:].bitcast(U32).indirect(offs2_t[:]))
-
-        def shift_planes(planes):
-            for a in range(1, n2):
-                nc.sync.dma_start(
-                    out=planes[a][0:SHIFT_ROWS, :].bitcast(I32),
-                    in_=planes[0][4 * a : 4 * a + SHIFT_ROWS, :].bitcast(I32),
-                )
 
         def own_pass(blk, t, a):
             if a == 0:
-                own[blk, t] = bank(PACK * (1 - blk) + t)
+                own[blk, t] = bank(PACK * blk + t)
             c0 = blk * PASS + t * P
             nc.tensor.matmul_mx(
-                out=own[blk, t][:], lhsT=w4_w[:, a, 2 * c0 : 2 * (c0 + P)].bitcast(FP4X4), lhsT_scale=w4_s[a][:, c0 : c0 + P],
-                rhs=v2_w[a][:].bitcast(FP8X4), rhs_scale=v2_s[a][:],
+                out=own[blk, t][:], lhsT=w4_w[:, a, 2 * c0 : 2 * (c0 + P)].bitcast(FP4X4), lhsT_scale=w4_s[:, a, c0 : c0 + P],
+                rhs=v2_w[a][:].bitcast(FP8X4), rhs_scale=v2_s[:, a, :],
                 start=(a == 0), stop=(a == n2 - 1),
-            )
-
-        def ratio(part, t):
-            blk, m0, width = part
-            x = picked[part][:, t, :]
-            nc.vector.scalar_tensor_tensor(
-                out=x, in0=own[blk, t][:, m0 : m0 + width], scalar=b2_t[:, t, blk : blk + 1], in1=x, op0=ALU.add, op1=ALU.mult
             )
 
         z_w = [keep.tile([P, M], U32, name="z_w%d" % blk, align_bytes=64) for blk in range(n3)]
         z_s = [keep.tile([P, M], U8, name="z_s%d" % blk, align_bytes=64) for blk in range(n3)]
 
-        def quantise_z(part):
-            blk, m0, width = part
+        def ratio(blk, ts, m0, width):
+            for t in ts:
+                x = picked[blk][:, t, m0 : m0 + width]
+                nc.vector.scalar_tensor_tensor(
+                    out=x, in0=own[blk, t][:, m0 : m0 + width], scalar=b2_t[:, t, blk : blk + 1], in1=x,
+                    op0=ALU.add, op1=ALU.mult,
+                )
+
+        def quantise_z(blk, m0, width):
             z_grouped = keep.tile([P, width, PACK], BF16, name="z_grouped%d_%d" % (blk, m0), align_bytes=64)
             nc.vector.tensor_scalar_max(
                 out=z_grouped[:].rearrange("p (c i) t -> p c t i", i=4),
-                in0=picked[part][:].rearrange("p t (c i) -> p c t i", i=4),
+                in0=picked[blk][:, :, m0 : m0 + width].rearrange("p t (c i) -> p c t i", i=4),
                 scalar1=0.0,
             )
             nc.vector.quantize_mx(
@@ -229,128 +222,132 @@ def tile_list_subcatchment_nitrate_loads_kernel(
                 in_=z_grouped[:].rearrange("p m t -> p (m t)"),
             )
 
-        def score_pass(acc, m0, c, blk, start, stop):
+        def score_pass(dst, m0, c, blk, start, stop):
             run = slice(m0, m0 + half)
             cols = slice(c * P, (c + 1) * P)
             nc.tensor.matmul_mx(
-                out=acc, lhsT=w8_w[:, blk, cols].bitcast(FP8X4), lhsT_scale=w8_s[4 * blk : P, cols],
+                out=dst, lhsT=w8_w[:, blk, cols].bitcast(FP8X4), lhsT_scale=w8_s[:, blk, cols],
                 rhs=z_w[blk][:, run].bitcast(FP8X4), rhs_scale=z_s[blk][:, run], start=start, stop=stop,
             )
 
-        def add_bias(res, acc, c, on_vector):
+        def add_bias(res, src, c, on_vector):
             if on_vector:
-                nc.vector.tensor_scalar_add(out=res, in0=acc, scalar1=b3_t[:, c : c + 1])
+                nc.vector.tensor_scalar_add(out=res, in0=src, scalar1=b3_t[:, c : c + 1])
             else:
-                nc.scalar.activation(res, acc, ACT.Identity, bias=b3_t[:, c : c + 1])
+                nc.scalar.activation(res, src, ACT.Identity, bias=b3_t[:, c : c + 1])
 
         def store_pair(res, pair, m0):
             nc.sync.dma_start(
                 out=out[2 * pair * P : 2 * (pair + 1) * P, m0 : m0 + half].rearrange("(j p) m -> p j m", p=P), in_=res[:]
             )
 
-        cast_w1(0, 0, 0)
-        tab_w.append(load_words("tab_w1", tab_words[1], AT_TAB[1]))
-        w1_raw[1, 0] = load_w1(1, 0)
-        quantise_w1(0, 0, 1)
+        cast_w1(0, 0, "scalar")
         w1_raw[0, 1] = load_w1(0, 1)
+        quantise_w1(0, 0)
+        cast_w1(1, 0, "scalar")
         w1_raw[1, 1] = load_w1(1, 1)
+        quantise_w1(1, 0)
+        nc.scalar.activation(root[:], slot_rows[:, :, 0:b2_row], ACT.Abs_reciprocal_sqrt)
+        nc.scalar.copy(out=b2_t[:], in_=slot_rows[:, :, b2_row:b3_row])
+        nc.scalar.copy(out=b3_t[:], in_=by_tile[:, b3_row : b3_row + tiles_n])
         nc.vector.tensor_copy(v_w[0][:], tab_w[0][:].bitcast(U32).indirect(offs_t[:]))
-        v_s = stage.tile([P, S], U8, name="v_s", align_bytes=64, offset=AT_V_S)
-        nc.vector.tensor_copy(v_s[:], tab_s[:].indirect(offs_t[:]))
-        sums = [(t, u) for t in range(PACK) for u in range(S // BANK)]
-        acc0 = {(t, u): bank(2 * t + u) for t, u in sums}
-        for t, u in sums:
-            basin_pass(acc0[t, u], 0, t, u, 0)
-        nc.vector.tensor_copy(v_w[1][:], tab_w[1][:].bitcast(U32).indirect(offs_t[:]))
-        tab2_w = {0: load_words("tab2_w0", tab2_words[0], AT_TAB2[0])}
+        tab2_w[0] = load_words("tab2_w0", tab2_words[0], AT_TAB2[0])
         w4_raw = stage.tile([P, n2, H // 2], I32, name="w4_raw", align_bytes=64, offset=AT_W4_RAW)
         nc.sync.dma_start(out=w4_raw[:], in_=w4_words.rearrange("a p n -> p a n").bitcast(I32))
-        cast_w1(1, 0, VECTOR_SHARE)
-        tab2_w[1] = load_words("tab2_w1", tab2_words[1], AT_TAB2[1])
-        quantise_w1(1, 0, PACK)
-        tab2_w[2] = load_words("tab2_w2", tab2_words[2], AT_TAB2[2])
-        for t, u in sums:
-            basin_pass(acc0[t, u], 0, t, u, 1)
-            empty_basin(acc0[t, u], 0, t, u)
-
-        cast_w1(0, 1, P)
-        pick(parts[0], 0)
-        quantise_w1(0, 1, 1)
-        cast_w1(1, 1, 0)
-        pick(parts[0], 1)
-        pick(parts[0], 2)
-        quantise_w1(1, 1, 1)
-        pick(parts[0], 3)
-        for t, u in sums:
-            acc = bank((2 * t + u) % PACK)
-            for a in range(n1):
-                basin_pass(acc, 1, t, u, a)
-            empty_basin(acc, 1, t, u)
-
-        v2_s = [stage.tile([P, M], U8, name="v2_s0", align_bytes=64, offset=AT_V2_S)]
-        v2_s.extend(keep.tile([P, M], U8, name="v2_s%d" % a, align_bytes=64) for a in range(1, n2))
-        nc.vector.tensor_copy(v2_s[0][:], tab2_s[:].indirect(offs2_t[:]))
-        shift_planes(v2_s)
-        w4_s = [stage.tile([P, H], U8, name="w4_s0", align_bytes=64, offset=AT_W4_S)]
-        w4_s.extend(keep.tile([P, H], U8, name="w4_s%d" % a, align_bytes=64) for a in range(1, n2))
+        for u in range(2):
+            for t in range(PACK):
+                basin_pass(0, t, u, 0)
+        v2_s_rows = keep.tile([P, M], U8, name="v2_s_rows", align_bytes=64)
+        nc.vector.tensor_copy(v2_s_rows[:], tab2_s[:].indirect(offs2_t[:]))
+        v2_s = to_planes(nc.gpsimd, "v2_s", v2_s_rows, n2)
+        w4_s_rows = keep.tile([P, H], U8, name="w4_s_rows", align_bytes=64)
         nc.vector.tensor_copy(
-            out=w4_s[0][:].rearrange("p (b t c i) -> p b c t i", t=PACK, c=8, i=16),
+            out=w4_s_rows[:].rearrange("p (b t c i) -> p b c t i", t=PACK, c=8, i=16),
             in_=w4_s_raw[:].rearrange("p (b c i t) -> p b c t i", t=PACK, c=8, i=16),
         )
-        shift_planes(w4_s)
+        w4_s = to_planes(nc.gpsimd, "w4_s", w4_s_rows, n2)
+        for u in range(2):
+            entries = offs_t[:, u * BANK // LIST_ROWS : (u + 1) * BANK // LIST_ROWS]
+            nc.vector.tensor_copy(v_w[1][:, u * BANK : (u + 1) * BANK], tab_w[1][:].bitcast(U32).indirect(entries))
+            for t in range(PACK):
+                basin_pass(0, t, u, 1)
+        for a in range(1, n2):
+            tab2_w[a] = load_words("tab2_w%d" % a, tab2_words[a], AT_TAB2[a])
+        for t, u in ((0, 0), (1, 0), (0, 1), (1, 1), (2, 0), (2, 1), (3, 0), (3, 1)):
+            empty_basin(0, t, u)
+
+        cast_w1(0, 1, "vector")
+        w8_w = stage.tile([P, n3, N], I32, name="w8_w", align_bytes=64, offset=AT_W8)
+        nc.sync.dma_start(out=w8_w[:], in_=w8_words.rearrange("a p n t -> p a (n t)").bitcast(I32))
+        pick(0, 0)
+        quantise_w1(0, 1)
+        for t in range(PACK):
+            for u in range(2):
+                basin_pass(1, t, u, 0)
+        pick(0, 1)
+        cast_w1(1, 1, "scalar")
+        pick(0, 2)
+        pick(0, 3)
+        quantise_w1(1, 1)
+        for t in range(PACK):
+            for u in range(2):
+                basin_pass(1, t, u, 1)
         gather_v2(0)
-        w4_w = stage.tile([P, n2, 2 * H], U8, name="w4_w", align_bytes=64, offset=AT_W4)
+        w4_w = keep.tile([P, n2, 2 * H], U8, name="w4_w", align_bytes=64)
         nc.vector.tensor_copy(
             out=w4_w[:].bitcast(U16).rearrange("p a (b t m) -> p (a b) m t", t=PACK, m=P),
             in_=w4_raw[:].bitcast(U16).rearrange("p a (b m t) -> p (a b) m t", t=PACK, m=P),
         )
-        gather_v2(1)
-        w8_w = stage.tile([P, n3, N], I32, name="w8_w", align_bytes=64, offset=AT_W8)
-        nc.sync.dma_start(out=w8_w[:], in_=w8_words.rearrange("a p n t -> p a (n t)").bitcast(I32))
-        w8_s = stage.tile([P, N], U8, name="w8_s", align_bytes=64, offset=AT_W8_S)
-        load_scale_rows(nc.sync, w8_s, w8_scales, 0)
 
-        reciprocal(parts[0], (0, 1))
-        reciprocal(parts[0], (2, 3))
+        def empty_slot(t):
+            for u in range(2):
+                empty_basin(1, t, u)
+            pick(1, t)
+
+        square(0, (0, 1), 0, M)
+        inverse_root(0, (0, 1), 0, M)
+        empty_slot(0)
+        gather_v2(1)
+        square(0, (0, 1), 0, M)
+        empty_slot(1)
         gather_v2(2)
-        for i, part in enumerate(parts[1:]):
-            picked[part] = stage.tile([P, PACK, half], F32, name="picked1_%d" % i, align_bytes=64, offset=AT_PICKED[i])
-            for t in range(PACK):
-                pick(part, t)
+        square(0, (2, 3), 0, M)
+        empty_slot(2)
         for a in range(n2):
             for t in range(PACK):
                 own_pass(0, t, a)
-        for t in range(PACK):
-            ratio(parts[0], t)
-        quantise_z(parts[0])
+        inverse_root(0, (2, 3), 0, M)
+        empty_slot(3)
+        square(0, (2, 3), 0, M)
         for t in range(PACK):
             for a in range(n2):
                 own_pass(1, t, a)
+        ratio(0, range(PACK), 0, M)
+        quantise_z(0, 0, M)
 
-        first = [bank(PACK + pair) for pair in range(tiles_n // 2)]
+        first = [bank(pair) for pair in range(tiles_n // 2)]
 
         def first_place(c):
             return first[c // 2][:, (c % 2) * half : (c % 2 + 1) * half]
 
         for c in range(tiles_n):
             score_pass(first_place(c), 0, c, 0, c % 2 == 0, False)
-        reciprocal(parts[1], range(PACK))
-        for t in range(PACK):
-            ratio(parts[1], t)
-        quantise_z(parts[1])
-        for c in range(tiles_n):
-            score_pass(first_place(c), 0, c, 1, False, c % 2 == 1)
-        reciprocal(parts[2], range(PACK))
-        for t in range(PACK):
-            ratio(parts[2], t)
-        quantise_z(parts[2])
+        for m0 in (0, half):
+            square(1, range(PACK), m0, half)
+            inverse_root(1, range(PACK), m0, half)
+            square(1, range(PACK), m0, half)
+            ratio(1, range(PACK), m0, half)
+            quantise_z(1, m0, half)
+            if m0 == 0:
+                for c in range(tiles_n):
+                    score_pass(first_place(c), 0, c, 1, False, c % 2 == 1)
         for pair in range(tiles_n // 2):
             res = keep.tile([P, 2, half], F32, name="res_first%d" % pair)
             for j in range(2):
                 add_bias(res[:, j, :], first_place(2 * pair + j), 2 * pair + j, False)
             store_pair(res, pair, 0)
 
-        second = [bank((7 + c) % 8) for c in range(tiles_n)]
+        second = [bank((3 + c) % 8) for c in range(tiles_n)]
         for c in range(tiles_n):
             score_pass(second[c][:, 0:half], half, c, 0, True, False)
         for pair in range(tiles_n // 2):

@@ -28,7 +28,8 @@ KIB = 1024
 AT_W1 = {(0, 0): 0, (1, 0): 8 * KIB, (0, 1): 0, (1, 1): 8 * KIB}
 AT_TAB = (16 * KIB, 32 * KIB)
 AT_TAB_S = AT_TAB[1]
-AT_TAB2 = (AT_TAB[0], AT_TAB[1], AT_TAB[1] + 8 * KIB)
+AT_TAB2_S = 48 * KIB
+AT_TAB2 = (AT_TAB[0], AT_TAB2_S, AT_TAB[1])
 AT_W4_RAW = AT_TAB[0] + 8 * KIB
 AT_W8 = AT_W1[0, 1]
 
@@ -78,7 +79,7 @@ def tile_list_subcatchment_nitrate_loads_kernel(
             return raw
 
         tab_s = stage.tile([P, T], U8, name="tab_s", align_bytes=64, offset=AT_TAB_S)
-        tab2_s = keep.tile([P, T2], U8, name="tab2_s", align_bytes=64)
+        tab2_s = stage.tile([P, T2], U8, name="tab2_s", align_bytes=64, offset=AT_TAB2_S)
         w4_s_raw = keep.tile([P, H], U8, name="w4_s_raw", align_bytes=64)
         rows = keep.tile([P, PASS], F32, name="rows")
         nc.vector.memset(rows[:], 0.0)
@@ -107,12 +108,6 @@ def tile_list_subcatchment_nitrate_loads_kernel(
         nc.gpsimd.dma_start(out=rows[b3_row : b3_row + tiles_n, 0:P], in_=b3.rearrange("(c p) -> c p", p=P))
         identity = keep.tile([P, P], F32, name="identity")
         make_identity(nc, identity[:])
-        w8_s = keep.tile([P, n3, N], U8, name="w8_s", align_bytes=64)
-        for g in range(4):
-            nc.gpsimd.dma_start(
-                out=w8_s[32 * g : 32 * g + 4].bitcast(I32),
-                in_=w8_scales[:, 4 * g : 4 * g + 4, :].rearrange("a i n -> i a n").bitcast(I32),
-            )
 
         v_s_rows = keep.tile([P, S], U8, name="v_s_rows", align_bytes=64)
         nc.vector.tensor_copy(v_s_rows[:], tab_s[:].indirect(offs_t[:]))
@@ -259,26 +254,32 @@ def tile_list_subcatchment_nitrate_loads_kernel(
                 basin_pass(0, t, u, 0)
         v2_s_rows = keep.tile([P, M], U8, name="v2_s_rows", align_bytes=64)
         nc.vector.tensor_copy(v2_s_rows[:], tab2_s[:].indirect(offs2_t[:]))
-        v2_s = to_planes(nc.gpsimd, "v2_s", v2_s_rows, n2)
+        v2_s = to_planes(nc.sync, "v2_s", v2_s_rows, n2)
+        tab2_w[1] = load_words("tab2_w1", tab2_words[1], AT_TAB2[1])
         w4_s_rows = keep.tile([P, H], U8, name="w4_s_rows", align_bytes=64)
         nc.vector.tensor_copy(
             out=w4_s_rows[:].rearrange("p (b t c i) -> p b c t i", t=PACK, c=8, i=16),
             in_=w4_s_raw[:].rearrange("p (b c i t) -> p b c t i", t=PACK, c=8, i=16),
         )
-        w4_s = to_planes(nc.gpsimd, "w4_s", w4_s_rows, n2)
+        w4_s = to_planes(nc.sync, "w4_s", w4_s_rows, n2)
         for u in range(2):
             entries = offs_t[:, u * BANK // LIST_ROWS : (u + 1) * BANK // LIST_ROWS]
             nc.vector.tensor_copy(v_w[1][:, u * BANK : (u + 1) * BANK], tab_w[1][:].bitcast(U32).indirect(entries))
             for t in range(PACK):
                 basin_pass(0, t, u, 1)
-        for a in range(1, n2):
-            tab2_w[a] = load_words("tab2_w%d" % a, tab2_words[a], AT_TAB2[a])
+        tab2_w[2] = load_words("tab2_w2", tab2_words[2], AT_TAB2[2])
         for t, u in ((0, 0), (1, 0), (0, 1), (1, 1), (2, 0), (2, 1), (3, 0), (3, 1)):
             empty_basin(0, t, u)
 
         cast_w1(0, 1, "vector")
         w8_w = stage.tile([P, n3, N], I32, name="w8_w", align_bytes=64, offset=AT_W8)
         nc.sync.dma_start(out=w8_w[:], in_=w8_words.rearrange("a p n t -> p a (n t)").bitcast(I32))
+        w8_s = stage.tile([P, n3, N], U8, name="w8_s", align_bytes=64, offset=AT_W8 + 6 * KIB)
+        for g in range(4):
+            nc.sync.dma_start(
+                out=w8_s[32 * g : 32 * g + 4].bitcast(I32),
+                in_=w8_scales[:, 4 * g : 4 * g + 4, :].rearrange("a i n -> i a n").bitcast(I32),
+            )
         pick(0, 0)
         quantise_w1(0, 1)
         for t in range(PACK):

@@ -24,6 +24,8 @@ BANK = 512
 LIST_ROWS = 16
 SCALE_ROWS = 16
 KIB = 1024
+TAB_ROWS, LATE_ROWS = 64, 16
+V_PLANE, W8_PLANE = 8, 4
 
 AT_W1 = {(0, 0): 0, (1, 0): 8 * KIB, (0, 1): 0, (1, 1): 8 * KIB}
 AT_TAB = (16 * KIB, 32 * KIB)
@@ -32,6 +34,7 @@ AT_TAB2_S = 48 * KIB
 AT_TAB2 = (AT_TAB[0], AT_TAB2_S, AT_TAB[1])
 AT_W4_RAW = AT_TAB[0] + 8 * KIB
 AT_W8 = AT_W1[0, 1]
+AT_PICKED = {(1, 0): AT_TAB2[1], (1, 1): AT_TAB2[2], (1, 2): AT_TAB2[2] + 2 * KIB, (1, 3): AT_TAB2[2] + 4 * KIB}
 
 
 def tile_list_subcatchment_nitrate_loads_kernel(
@@ -55,18 +58,19 @@ def tile_list_subcatchment_nitrate_loads_kernel(
             nc.sync.dma_start(out=words[:], in_=src.rearrange("p n t -> p (n t)").bitcast(I32))
             return words
 
-        def load_scale_rows(dst, src):
+        def load_scale_rows(dst, src, base):
             passes = src.shape[0]
             nc.sync.dma_start(
-                out=dst[0 : SCALE_ROWS * passes, :].bitcast(I32), in_=src.rearrange("a q n -> q a n").bitcast(I32)
+                out=dst[base : base + SCALE_ROWS * passes, :].bitcast(I32),
+                in_=src.rearrange("a q n -> q a n").bitcast(I32),
             )
 
-        def to_planes(queue, name, src, passes):
+        def to_planes(queue, name, src, passes, base, first):
             planes = keep.tile([P, passes, src.shape[1]], U8, name=name, align_bytes=64)
             for g in range(4):
                 queue.dma_start(
-                    out=planes[32 * g : 32 * g + 4].bitcast(I32),
-                    in_=src[4 * passes * g : 4 * passes * (g + 1), :].bitcast(I32),
+                    out=planes[32 * g + first : 32 * g + first + 4].bitcast(I32),
+                    in_=src[base + 4 * passes * g : base + 4 * passes * (g + 1), :].bitcast(I32),
                 )
             return planes
 
@@ -85,22 +89,22 @@ def tile_list_subcatchment_nitrate_loads_kernel(
         nc.vector.memset(rows[:], 0.0)
         nc.vector.memset(tab2_s[:].bitcast(I32), 0)
         nc.vector.memset(w4_s_raw[:].bitcast(I32), 0)
-        nc.vector.memset(tab_s[32:64, :].bitcast(I32), 0)
-        nc.vector.memset(tab_s[64:P, :].bitcast(I32), 0)
+        nc.vector.memset(tab_s[0:64, :].bitcast(I32), 0)
+        nc.vector.memset(tab_s[96:P, :].bitcast(I32), 0)
 
         offs_t = lists.tile([P, S // LIST_ROWS], U16, name="offs_t")
         pos_t = lists.tile([P, M // LIST_ROWS], U16, name="pos_t")
         offs2_t = lists.tile([P, M // LIST_ROWS], U16, name="offs2_t")
 
         nc.sync.dma_start(offs_t[:], offs)
-        load_scale_rows(tab_s, tab_scales)
+        load_scale_rows(tab_s, tab_scales, TAB_ROWS)
         w1_raw = {(0, 0): load_w1(0, 0)}
         nc.sync.dma_start(offs2_t[:], offs2)
         nc.sync.dma_start(pos_t[:], pos1)
         w1_raw[1, 0] = load_w1(1, 0)
         tab_w = [load_words("tab_w0", tab_words[0], AT_TAB[0])]
-        load_scale_rows(tab2_s, tab2_scales)
-        load_scale_rows(w4_s_raw, w4_scales)
+        load_scale_rows(tab2_s, tab2_scales, LATE_ROWS)
+        load_scale_rows(w4_s_raw, w4_scales, LATE_ROWS)
 
         b2_row, b3_row = n3, 2 * n3
         nc.gpsimd.dma_start(out=rows[0:b2_row, :], in_=kap.rearrange("(b c) -> b c", b=n3))
@@ -111,7 +115,7 @@ def tile_list_subcatchment_nitrate_loads_kernel(
 
         v_s_rows = keep.tile([P, S], U8, name="v_s_rows", align_bytes=64)
         nc.vector.tensor_copy(v_s_rows[:], tab_s[:].indirect(offs_t[:]))
-        v_s = to_planes(nc.sync, "v_s", v_s_rows, n1)
+        v_s = to_planes(nc.sync, "v_s", v_s_rows, n1, TAB_ROWS, V_PLANE)
         tab_w.append(load_words("tab_w1", tab_words[1], AT_TAB[1]))
 
         by_slot = bank(6)
@@ -121,6 +125,7 @@ def tile_list_subcatchment_nitrate_loads_kernel(
         nc.tensor.transpose(by_tile[:, 0:P], rows[:, 0:P], identity[:])
         slot_rows = by_slot[:].rearrange("p (t r) -> p t r", t=PACK)
         root = keep.tile([P, PACK, n3], F32, name="root")
+        inverse = keep.tile([P, PACK, n3], F32, name="inverse")
         b2_t = keep.tile([P, PACK, n3], F32, name="b2_t")
         b3_t = keep.tile([P, tiles_n], F32, name="b3_t")
 
@@ -153,7 +158,7 @@ def tile_list_subcatchment_nitrate_loads_kernel(
             run = slice(u * BANK, (u + 1) * BANK)
             nc.tensor.matmul_mx(
                 out=acc[blk, t, u][:], lhsT=w1_w[a, blk][:, cols].bitcast(FP8X4), lhsT_scale=w1_s[a, blk][:, cols],
-                rhs=v_w[a][:, run].bitcast(FP8X4), rhs_scale=v_s[:, a, run],
+                rhs=v_w[a][:, run].bitcast(FP8X4), rhs_scale=v_s[V_PLANE:P, a, run],
                 start=(a == 0), stop=(a == n1 - 1),
             )
 
@@ -163,20 +168,31 @@ def tile_list_subcatchment_nitrate_loads_kernel(
             nc.scalar.copy(out=h[blk, t][:, u * BANK : (u + 1) * BANK], in_=acc[blk, t, u][:])
 
         half = M // 2
-        picked = [keep.tile([P, PACK, M], F32, name="picked%d" % blk) for blk in range(n3)]
+        picked = {}
+        squared = [keep.tile([P, PACK, M], F32, name="squared%d" % blk) for blk in range(n3)]
 
         def pick(blk, t):
-            nc.vector.tensor_copy(picked[blk][:, t, :], h[blk, t][:].indirect(pos_t[:]))
+            name = "picked%d%d" % (blk, t)
+            if (blk, t) in AT_PICKED:
+                picked[blk, t] = stage.tile([P, M], F32, name=name, align_bytes=64, offset=AT_PICKED[blk, t])
+            else:
+                picked[blk, t] = keep.tile([P, M], F32, name=name)
+            nc.vector.tensor_copy(picked[blk, t][:], h[blk, t][:].indirect(pos_t[:]))
+            first_square(blk, t)
+
+        def first_square(blk, t):
+            x = picked[blk, t][:]
+            nc.gpsimd.tensor_tensor(out=squared[blk][:, t, :], in0=x, in1=x, op=ALU.mult)
 
         def square(blk, ts, m0, width):
             for t in ts:
-                x = picked[blk][:, t, m0 : m0 + width]
+                x = squared[blk][:, t, m0 : m0 + width]
                 nc.scalar.activation(x, x, ACT.Square, scale=root[:, t, blk : blk + 1])
 
         def inverse_root(blk, ts, m0, width):
             for t in ts:
-                x = picked[blk][:, t, m0 : m0 + width]
-                nc.scalar.activation(x, x, ACT.Abs_reciprocal_sqrt, bias=1.0)
+                x = squared[blk][:, t, m0 : m0 + width]
+                nc.scalar.activation(x, x, ACT.Abs_reciprocal_sqrt, bias=1.0, scale=inverse[:, t, blk : blk + 1])
 
         v2_w, own, tab2_w = {}, {}, {}
 
@@ -199,19 +215,26 @@ def tile_list_subcatchment_nitrate_loads_kernel(
 
         def ratio(blk, ts, m0, width):
             for t in ts:
-                x = picked[blk][:, t, m0 : m0 + width]
+                x = squared[blk][:, t, m0 : m0 + width]
                 nc.vector.scalar_tensor_tensor(
                     out=x, in0=own[blk, t][:, m0 : m0 + width], scalar=b2_t[:, t, blk : blk + 1], in1=x,
                     op0=ALU.add, op1=ALU.mult,
                 )
 
+        top = keep.tile([P, PACK, M], F32, name="top")
+
+        def numerator(ts):
+            for t in ts:
+                nc.scalar.activation(top[:, t, :], own[0, t][:], ACT.Relu, bias=b2_t[:, t, 0:1])
+
         def quantise_z(blk, m0, width):
             z_grouped = keep.tile([P, width, PACK], BF16, name="z_grouped%d_%d" % (blk, m0), align_bytes=64)
-            nc.vector.tensor_scalar_max(
-                out=z_grouped[:].rearrange("p (c i) t -> p c t i", i=4),
-                in0=picked[blk][:, :, m0 : m0 + width].rearrange("p t (c i) -> p c t i", i=4),
-                scalar1=0.0,
-            )
+            dst = z_grouped[:].rearrange("p (c i) t -> p c t i", i=4)
+            src = squared[blk][:, :, m0 : m0 + width].rearrange("p t (c i) -> p c t i", i=4)
+            if blk == 0:
+                nc.vector.tensor_tensor(out=dst, in0=src, in1=top[:].rearrange("p t (c i) -> p c t i", i=4), op=ALU.mult)
+            else:
+                nc.vector.tensor_scalar_max(out=dst, in0=src, scalar1=0.0)
             nc.vector.quantize_mx(
                 out=z_w[blk][:, m0 : m0 + width].bitcast(FP8X4), scales=z_s[blk][:, m0 : m0 + width],
                 in_=z_grouped[:].rearrange("p m t -> p (m t)"),
@@ -221,7 +244,7 @@ def tile_list_subcatchment_nitrate_loads_kernel(
             run = slice(m0, m0 + half)
             cols = slice(c * P, (c + 1) * P)
             nc.tensor.matmul_mx(
-                out=dst, lhsT=w8_w[:, blk, cols].bitcast(FP8X4), lhsT_scale=w8_s[:, blk, cols],
+                out=dst, lhsT=w8_w[:, blk, cols].bitcast(FP8X4), lhsT_scale=w8_s[W8_PLANE:P, blk, cols],
                 rhs=z_w[blk][:, run].bitcast(FP8X4), rhs_scale=z_s[blk][:, run], start=start, stop=stop,
             )
 
@@ -243,6 +266,7 @@ def tile_list_subcatchment_nitrate_loads_kernel(
         w1_raw[1, 1] = load_w1(1, 1)
         quantise_w1(1, 0)
         nc.scalar.activation(root[:], slot_rows[:, :, 0:b2_row], ACT.Abs_reciprocal_sqrt)
+        nc.scalar.activation(inverse[:], root[:], ACT.Square)
         nc.scalar.copy(out=b2_t[:], in_=slot_rows[:, :, b2_row:b3_row])
         nc.scalar.copy(out=b3_t[:], in_=by_tile[:, b3_row : b3_row + tiles_n])
         nc.vector.tensor_copy(v_w[0][:], tab_w[0][:].bitcast(U32).indirect(offs_t[:]))
@@ -254,14 +278,14 @@ def tile_list_subcatchment_nitrate_loads_kernel(
                 basin_pass(0, t, u, 0)
         v2_s_rows = keep.tile([P, M], U8, name="v2_s_rows", align_bytes=64)
         nc.vector.tensor_copy(v2_s_rows[:], tab2_s[:].indirect(offs2_t[:]))
-        v2_s = to_planes(nc.sync, "v2_s", v2_s_rows, n2)
+        v2_s = to_planes(nc.sync, "v2_s", v2_s_rows, n2, LATE_ROWS, 0)
         tab2_w[1] = load_words("tab2_w1", tab2_words[1], AT_TAB2[1])
         w4_s_rows = keep.tile([P, H], U8, name="w4_s_rows", align_bytes=64)
         nc.vector.tensor_copy(
             out=w4_s_rows[:].rearrange("p (b t c i) -> p b c t i", t=PACK, c=8, i=16),
             in_=w4_s_raw[:].rearrange("p (b c i t) -> p b c t i", t=PACK, c=8, i=16),
         )
-        w4_s = to_planes(nc.sync, "w4_s", w4_s_rows, n2)
+        w4_s = to_planes(nc.sync, "w4_s", w4_s_rows, n2, LATE_ROWS, 0)
         for u in range(2):
             entries = offs_t[:, u * BANK // LIST_ROWS : (u + 1) * BANK // LIST_ROWS]
             nc.vector.tensor_copy(v_w[1][:, u * BANK : (u + 1) * BANK], tab_w[1][:].bitcast(U32).indirect(entries))
@@ -277,14 +301,11 @@ def tile_list_subcatchment_nitrate_loads_kernel(
         w8_s = stage.tile([P, n3, N], U8, name="w8_s", align_bytes=64, offset=AT_W8 + 6 * KIB)
         for g in range(4):
             nc.sync.dma_start(
-                out=w8_s[32 * g : 32 * g + 4].bitcast(I32),
+                out=w8_s[32 * g + W8_PLANE : 32 * g + W8_PLANE + 4].bitcast(I32),
                 in_=w8_scales[:, 4 * g : 4 * g + 4, :].rearrange("a i n -> i a n").bitcast(I32),
             )
         pick(0, 0)
         quantise_w1(0, 1)
-        for t in range(PACK):
-            for u in range(2):
-                basin_pass(1, t, u, 0)
         pick(0, 1)
         cast_w1(1, 1, "scalar")
         pick(0, 2)
@@ -292,7 +313,8 @@ def tile_list_subcatchment_nitrate_loads_kernel(
         quantise_w1(1, 1)
         for t in range(PACK):
             for u in range(2):
-                basin_pass(1, t, u, 1)
+                for a in range(n1):
+                    basin_pass(1, t, u, a)
         gather_v2(0)
         w4_w = keep.tile([P, n2, 2 * H], U8, name="w4_w", align_bytes=64)
         nc.vector.tensor_copy(
@@ -305,14 +327,12 @@ def tile_list_subcatchment_nitrate_loads_kernel(
                 empty_basin(1, t, u)
             pick(1, t)
 
-        square(0, (0, 1), 0, M)
         inverse_root(0, (0, 1), 0, M)
-        empty_slot(0)
         gather_v2(1)
+        empty_slot(0)
+        gather_v2(2)
         square(0, (0, 1), 0, M)
         empty_slot(1)
-        gather_v2(2)
-        square(0, (2, 3), 0, M)
         empty_slot(2)
         for a in range(n2):
             for t in range(PACK):
@@ -323,7 +343,7 @@ def tile_list_subcatchment_nitrate_loads_kernel(
         for t in range(PACK):
             for a in range(n2):
                 own_pass(1, t, a)
-        ratio(0, range(PACK), 0, M)
+        numerator(range(PACK))
         quantise_z(0, 0, M)
 
         first = [bank(pair) for pair in range(tiles_n // 2)]
@@ -334,7 +354,6 @@ def tile_list_subcatchment_nitrate_loads_kernel(
         for c in range(tiles_n):
             score_pass(first_place(c), 0, c, 0, c % 2 == 0, False)
         for m0 in (0, half):
-            square(1, range(PACK), m0, half)
             inverse_root(1, range(PACK), m0, half)
             square(1, range(PACK), m0, half)
             ratio(1, range(PACK), m0, half)

@@ -178,7 +178,8 @@ def tile_list_subcatchment_nitrate_loads_kernel(
             else:
                 picked[blk, t] = keep.tile([P, M], F32, name=name)
             nc.vector.tensor_copy(picked[blk, t][:], h[blk, t][:].indirect(pos_t[:]))
-            first_square(blk, t)
+            if (blk, t) != (1, 3):
+                first_square(blk, t)
 
         def first_square(blk, t):
             x = picked[blk, t][:]
@@ -354,6 +355,8 @@ def tile_list_subcatchment_nitrate_loads_kernel(
         for c in range(tiles_n):
             score_pass(first_place(c), 0, c, 0, c % 2 == 0, False)
         for m0 in (0, half):
+            run = slice(m0, m0 + half)
+            nc.scalar.activation(squared[1][:, 3, run], picked[1, 3][:, run], ACT.Square)
             inverse_root(1, range(PACK), m0, half)
             square(1, range(PACK), m0, half)
             ratio(1, range(PACK), m0, half)

@@ -233,7 +233,8 @@ def tile_list_subcatchment_nitrate_loads_kernel(
             dst = z_grouped[:].rearrange("p (c i) t -> p c t i", i=4)
             src = squared[blk][:, :, m0 : m0 + width].rearrange("p t (c i) -> p c t i", i=4)
             if blk == 0:
-                nc.vector.tensor_tensor(out=dst, in0=src, in1=top[:].rearrange("p t (c i) -> p c t i", i=4), op=ALU.mult)
+                factor = top[:, :, m0 : m0 + width].rearrange("p t (c i) -> p c t i", i=4)
+                nc.vector.tensor_tensor(out=dst, in0=src, in1=factor, op=ALU.mult)
             else:
                 nc.vector.tensor_scalar_max(out=dst, in0=src, scalar1=0.0)
             nc.vector.quantize_mx(
@@ -345,7 +346,7 @@ def tile_list_subcatchment_nitrate_loads_kernel(
             for a in range(n2):
                 own_pass(1, t, a)
         numerator(range(PACK))
-        quantise_z(0, 0, M)
+        quantise_z(0, 0, half)
 
         first = [bank(pair) for pair in range(tiles_n // 2)]
 
@@ -364,6 +365,7 @@ def tile_list_subcatchment_nitrate_loads_kernel(
             if m0 == 0:
                 for c in range(tiles_n):
                     score_pass(first_place(c), 0, c, 1, False, c % 2 == 1)
+                quantise_z(0, half, half)
         for pair in range(tiles_n // 2):
             res = keep.tile([P, 2, half], F32, name="res_first%d" % pair)
             for j in range(2):

@@ -24,17 +24,16 @@ BANK = 512
 LIST_ROWS = 16
 SCALE_ROWS = 16
 KIB = 1024
-TAB_ROWS, LATE_ROWS = 64, 16
+HALF = M // 2
+TAB_ROWS, LATE_ROWS = 64, 40
 V_PLANE, W8_PLANE = 8, 4
 
-AT_W1 = {(0, 0): 0, (1, 0): 8 * KIB, (0, 1): 0, (1, 1): 8 * KIB}
+AT_W1 = (0, 8 * KIB)
 AT_TAB = (16 * KIB, 32 * KIB)
-AT_TAB_S = AT_TAB[1]
 AT_TAB2_S = 48 * KIB
 AT_TAB2 = (AT_TAB[0], AT_TAB2_S, AT_TAB[1])
 AT_W4_RAW = AT_TAB[0] + 8 * KIB
-AT_W8 = AT_W1[0, 1]
-AT_PICKED = {(1, 0): AT_TAB2[1], (1, 1): AT_TAB2[2], (1, 2): AT_TAB2[2] + 2 * KIB, (1, 3): AT_TAB2[2] + 4 * KIB}
+AT_LAST_SQUARE = 56 * KIB
 
 
 def tile_list_subcatchment_nitrate_loads_kernel(
@@ -53,8 +52,11 @@ def tile_list_subcatchment_nitrate_loads_kernel(
         def bank(i):
             return psum.tile([P, BANK], F32, name="bank%d" % i)
 
+        def placed(name, shape, dtype, offset):
+            return stage.tile(shape, dtype, name=name, align_bytes=64, offset=offset)
+
         def load_words(name, src, offset):
-            words = stage.tile([P, src.shape[1]], I32, name=name, align_bytes=64, offset=offset)
+            words = placed(name, [P, src.shape[1]], I32, offset)
             nc.sync.dma_start(out=words[:], in_=src.rearrange("p n t -> p (n t)").bitcast(I32))
             return words
 
@@ -65,25 +67,25 @@ def tile_list_subcatchment_nitrate_loads_kernel(
                 in_=src.rearrange("a q n -> q a n").bitcast(I32),
             )
 
-        def to_planes(queue, name, src, passes, base, first):
+        def to_planes(name, src, passes, base, first):
             planes = keep.tile([P, passes, src.shape[1]], U8, name=name, align_bytes=64)
-            for g in range(4):
-                queue.dma_start(
+            for g in (0, 2, 1, 3):
+                nc.sync.dma_start(
                     out=planes[32 * g + first : 32 * g + first + 4].bitcast(I32),
                     in_=src[base + 4 * passes * g : base + 4 * passes * (g + 1), :].bitcast(I32),
                 )
             return planes
 
         def load_w1(a, blk):
-            raw = stage.tile([P, PACK, PASS], F32, name="w1_raw%d%d" % (a, blk), align_bytes=64, offset=AT_W1[a, blk])
+            raw = placed("w1_raw%d%d" % (a, blk), [P, PACK, PASS], F32, AT_W1[a])
             nc.sync.dma_start(
                 out=raw[:],
                 in_=w1[a * PASS : (a + 1) * PASS, blk * PASS : (blk + 1) * PASS].rearrange("(p j) c -> p j c", j=PACK),
             )
             return raw
 
-        tab_s = stage.tile([P, T], U8, name="tab_s", align_bytes=64, offset=AT_TAB_S)
-        tab2_s = stage.tile([P, T2], U8, name="tab2_s", align_bytes=64, offset=AT_TAB2_S)
+        tab_s = placed("tab_s", [P, T], U8, AT_TAB[1])
+        tab2_s = placed("tab2_s", [P, T2], U8, AT_TAB2_S)
         w4_s_raw = keep.tile([P, H], U8, name="w4_s_raw", align_bytes=64)
         rows = keep.tile([P, PASS], F32, name="rows")
         nc.vector.memset(rows[:], 0.0)
@@ -115,7 +117,7 @@ def tile_list_subcatchment_nitrate_loads_kernel(
 
         v_s_rows = keep.tile([P, S], U8, name="v_s_rows", align_bytes=64)
         nc.vector.tensor_copy(v_s_rows[:], tab_s[:].indirect(offs_t[:]))
-        v_s = to_planes(nc.sync, "v_s", v_s_rows, n1, TAB_ROWS, V_PLANE)
+        v_s = to_planes("v_s", v_s_rows[:], n1, TAB_ROWS, V_PLANE)
         tab_w.append(load_words("tab_w1", tab_words[1], AT_TAB[1]))
 
         by_slot = bank(6)
@@ -124,18 +126,22 @@ def tile_list_subcatchment_nitrate_loads_kernel(
         by_tile = bank(7)
         nc.tensor.transpose(by_tile[:, 0:P], rows[:, 0:P], identity[:])
         slot_rows = by_slot[:].rearrange("p (t r) -> p t r", t=PACK)
-        root = keep.tile([P, PACK, n3], F32, name="root")
-        inverse = keep.tile([P, PACK, n3], F32, name="inverse")
-        b2_t = keep.tile([P, PACK, n3], F32, name="b2_t")
+        by_row = keep.tile([P, PACK, b3_row], F32, name="by_row")
         b3_t = keep.tile([P, tiles_n], F32, name="b3_t")
+
+        def kap_of(blk, t):
+            return by_row[:, t, blk : blk + 1]
+
+        def b2_of(blk, t):
+            return by_row[:, t, b2_row + blk : b2_row + blk + 1]
 
         grouped, w1_w, w1_s = {}, {}, {}
 
-        def cast_w1(a, blk, engine):
+        def cast_w1(a, blk, on_vector):
             grouped[a, blk] = keep.tile([P, PACK, P, PACK], BF16, name="w1_grouped%d%d" % (a, blk), align_bytes=64)
             src = w1_raw[a, blk][:].rearrange("p j (m t) -> p m j t", t=PACK)
             dst = grouped[a, blk][:].rearrange("p t m j -> p m j t")
-            if engine == "vector":
+            if on_vector:
                 nc.vector.tensor_copy(out=dst, in_=src)
             else:
                 nc.scalar.copy(out=dst, in_=src)
@@ -167,87 +173,115 @@ def tile_list_subcatchment_nitrate_loads_kernel(
                 h[blk, t] = keep.tile([P, S], F32, name="h%d%d" % (blk, t), align_bytes=64)
             nc.scalar.copy(out=h[blk, t][:, u * BANK : (u + 1) * BANK], in_=acc[blk, t, u][:])
 
-        half = M // 2
-        picked = {}
-        squared = [keep.tile([P, PACK, M], F32, name="squared%d" % blk) for blk in range(n3)]
+        def gpsimd_square(dst, src):
+            nc.gpsimd.tensor_tensor(out=dst, in0=src, in1=src, op=ALU.mult)
 
-        def pick(blk, t):
-            name = "picked%d%d" % (blk, t)
-            if (blk, t) in AT_PICKED:
-                picked[blk, t] = stage.tile([P, M], F32, name=name, align_bytes=64, offset=AT_PICKED[blk, t])
-            else:
-                picked[blk, t] = keep.tile([P, M], F32, name=name)
-            nc.vector.tensor_copy(picked[blk, t][:], h[blk, t][:].indirect(pos_t[:]))
-            if (blk, t) != (1, 3):
-                first_square(blk, t)
+        def inverse_root(dst, src, blk, t):
+            nc.scalar.activation(dst, src, ACT.Abs_reciprocal_sqrt, bias=kap_of(blk, t))
 
-        def first_square(blk, t):
-            x = picked[blk, t][:]
-            nc.gpsimd.tensor_tensor(out=squared[blk][:, t, :], in0=x, in1=x, op=ALU.mult)
+        squared0 = {}
 
-        def square(blk, ts, m0, width):
-            for t in ts:
-                x = squared[blk][:, t, m0 : m0 + width]
-                nc.scalar.activation(x, x, ACT.Square, scale=root[:, t, blk : blk + 1])
+        def pick0(t):
+            picked = keep.tile([P, M], F32, name="picked0%d" % t)
+            nc.vector.tensor_copy(picked[:], h[0, t][:].indirect(pos_t[:]))
+            squared0[t] = keep.tile([P, M], F32, name="squared0%d" % t)
+            gpsimd_square(squared0[t][:], picked[:])
 
-        def inverse_root(blk, ts, m0, width):
-            for t in ts:
-                x = squared[blk][:, t, m0 : m0 + width]
-                nc.scalar.activation(x, x, ACT.Abs_reciprocal_sqrt, bias=1.0, scale=inverse[:, t, blk : blk + 1])
+        picked1, squared1 = {}, {}
+
+        def pick1(half, t):
+            pair, j = divmod(t, 2)
+            name = "picked1_%d%d" % (half, pair)
+            if j == 0:
+                if half == 1:
+                    picked1[half, pair] = placed(name, [P, 2, HALF], F32, AT_TAB2[2] + 2 * KIB * pair)
+                elif pair == 0:
+                    picked1[half, pair] = placed(name, [P, 2, HALF], F32, AT_TAB2[1])
+                else:
+                    picked1[half, pair] = placed(name, [P, 2, HALF], F32, AT_TAB2[2] + 4 * KIB)
+            entries = pos_t[:, half * HALF // LIST_ROWS : (half + 1) * HALF // LIST_ROWS]
+            nc.vector.tensor_copy(picked1[half, pair][:, j, :], h[1, t][:].indirect(entries))
+            if j == 1:
+                if (half, pair) != (1, 1):
+                    squared1[half, pair] = keep.tile([P, 2, HALF], F32, name="squared1_%d%d" % (half, pair))
+                    gpsimd_square(squared1[half, pair][:], picked1[half, pair][:])
 
         v2_w, own, tab2_w = {}, {}, {}
 
         def gather_v2(a):
-            v2_w[a] = keep.tile([P, M], U32, name="v2_w%d" % a, align_bytes=64)
+            name = "v2_w%d" % a
+            v2_w[a] = placed(name, [P, M], U32, AT_W1[1]) if a == 0 else keep.tile([P, M], U32, name=name, align_bytes=64)
             nc.vector.tensor_copy(v2_w[a][:], tab2_w[a][:].bitcast(U32).indirect(offs2_t[:]))
 
-        def own_pass(blk, t, a):
-            if a == 0:
+        def own_pass(blk, t, a, order=(0, 1, 2)):
+            if a == order[0]:
                 own[blk, t] = bank(PACK * blk + t)
             c0 = blk * PASS + t * P
             nc.tensor.matmul_mx(
-                out=own[blk, t][:], lhsT=w4_w[:, a, 2 * c0 : 2 * (c0 + P)].bitcast(FP4X4), lhsT_scale=w4_s[:, a, c0 : c0 + P],
+                out=own[blk, t][:], lhsT=w4_w[:, a, 2 * c0 : 2 * (c0 + P)].bitcast(FP4X4),
+                lhsT_scale=w4_s[:, a, c0 : c0 + P],
                 rhs=v2_w[a][:].bitcast(FP8X4), rhs_scale=v2_s[:, a, :],
-                start=(a == 0), stop=(a == n2 - 1),
+                start=(a == order[0]), stop=(a == order[-1]),
             )
 
-        z_w = [keep.tile([P, M], U32, name="z_w%d" % blk, align_bytes=64) for blk in range(n3)]
-        z_s = [keep.tile([P, M], U8, name="z_s%d" % blk, align_bytes=64) for blk in range(n3)]
+        inverse1 = [keep.tile([P, PACK, HALF], F32, name="inverse1_%d" % half) for half in range(2)]
+        top = {unit: keep.tile([P, PACK, HALF], F32, name="top%d%d" % unit) for unit in ((0, 0), (0, 1))}
 
-        def ratio(blk, ts, m0, width):
+        root1 = {}
+
+        def inverse_roots1(half, pair):
+            name = "root1_%d%d" % (half, pair)
+            if (half, pair) == (0, 1):
+                root1[half, pair] = placed(name, [P, 2, HALF], F32, AT_LAST_SQUARE)
+            else:
+                root1[half, pair] = keep.tile([P, 2, HALF], F32, name=name)
+            for j in range(2):
+                inverse_root(root1[half, pair][:, j, :], squared1[half, pair][:, j, :], 1, 2 * pair + j)
+
+        def last_squares1(half, pair):
+            for j in range(2):
+                nc.scalar.activation(inverse1[half][:, 2 * pair + j, :], root1[half, pair][:, j, :], ACT.Square)
+
+        def numerator(blk, half, ts):
             for t in ts:
-                x = squared[blk][:, t, m0 : m0 + width]
+                src = own[blk, t][:, half * HALF : (half + 1) * HALF]
+                nc.scalar.activation(top[blk, half][:, t, :], src, ACT.Relu, bias=b2_of(blk, t))
+
+        def ratio(half, ts):
+            for t in ts:
+                x = inverse1[half][:, t, :]
                 nc.vector.scalar_tensor_tensor(
-                    out=x, in0=own[blk, t][:, m0 : m0 + width], scalar=b2_t[:, t, blk : blk + 1], in1=x,
+                    out=x, in0=own[1, t][:, half * HALF : (half + 1) * HALF], scalar=b2_of(1, t), in1=x,
                     op0=ALU.add, op1=ALU.mult,
                 )
 
-        top = keep.tile([P, PACK, M], F32, name="top")
+        z_grouped, z_w, z_s = {}, {}, {}
 
-        def numerator(ts):
-            for t in ts:
-                nc.scalar.activation(top[:, t, :], own[0, t][:], ACT.Relu, bias=b2_t[:, t, 0:1])
+        def by_lines(x):
+            return x.rearrange("p t (c i) -> p c t i", i=4)
 
-        def quantise_z(blk, m0, width):
-            z_grouped = keep.tile([P, width, PACK], BF16, name="z_grouped%d_%d" % (blk, m0), align_bytes=64)
-            dst = z_grouped[:].rearrange("p (c i) t -> p c t i", i=4)
-            src = squared[blk][:, :, m0 : m0 + width].rearrange("p t (c i) -> p c t i", i=4)
-            if blk == 0:
-                factor = top[:, :, m0 : m0 + width].rearrange("p t (c i) -> p c t i", i=4)
-                nc.vector.tensor_tensor(out=dst, in0=src, in1=factor, op=ALU.mult)
+        def group_z(blk, half):
+            z_grouped[blk, half] = keep.tile([P, HALF, PACK], BF16, name="z_grouped%d%d" % (blk, half), align_bytes=64)
+            dst = z_grouped[blk, half][:].rearrange("p (c i) t -> p c t i", i=4)
+            if (blk, half) in top:
+                src = inverse0[:, :, half * HALF : (half + 1) * HALF] if blk == 0 else inverse1[half][:]
+                nc.vector.tensor_tensor(out=dst, in0=by_lines(src), in1=by_lines(top[blk, half][:]), op=ALU.mult)
             else:
-                nc.vector.tensor_scalar_max(out=dst, in0=src, scalar1=0.0)
+                nc.vector.tensor_scalar_max(out=dst, in0=by_lines(inverse1[half][:]), scalar1=0.0)
+
+        def quantise_z(blk, half):
+            z_w[blk, half] = keep.tile([P, HALF], U32, name="z_w%d%d" % (blk, half), align_bytes=64)
+            z_s[blk, half] = keep.tile([P, HALF], U8, name="z_s%d%d" % (blk, half), align_bytes=64)
             nc.vector.quantize_mx(
-                out=z_w[blk][:, m0 : m0 + width].bitcast(FP8X4), scales=z_s[blk][:, m0 : m0 + width],
-                in_=z_grouped[:].rearrange("p m t -> p (m t)"),
+                out=z_w[blk, half][:].bitcast(FP8X4), scales=z_s[blk, half][:],
+                in_=z_grouped[blk, half][:].rearrange("p m t -> p (m t)"),
             )
 
-        def score_pass(dst, m0, c, blk, start, stop):
-            run = slice(m0, m0 + half)
+        def score_pass(dst, half, c, blk, start, stop):
             cols = slice(c * P, (c + 1) * P)
             nc.tensor.matmul_mx(
                 out=dst, lhsT=w8_w[:, blk, cols].bitcast(FP8X4), lhsT_scale=w8_s[W8_PLANE:P, blk, cols],
-                rhs=z_w[blk][:, run].bitcast(FP8X4), rhs_scale=z_s[blk][:, run], start=start, stop=stop,
+                rhs=z_w[blk, half][:].bitcast(FP8X4), rhs_scale=z_s[blk, half][:], start=start, stop=stop,
             )
 
         def add_bias(res, src, c, on_vector):
@@ -256,129 +290,146 @@ def tile_list_subcatchment_nitrate_loads_kernel(
             else:
                 nc.scalar.activation(res, src, ACT.Identity, bias=b3_t[:, c : c + 1])
 
-        def store_pair(res, pair, m0):
+        def store_pair(res, pair, half):
             nc.sync.dma_start(
-                out=out[2 * pair * P : 2 * (pair + 1) * P, m0 : m0 + half].rearrange("(j p) m -> p j m", p=P), in_=res[:]
+                out=out[2 * pair * P : 2 * (pair + 1) * P, half * HALF : (half + 1) * HALF].rearrange("(j p) m -> p j m", p=P),
+                in_=res[:],
             )
 
-        cast_w1(0, 0, "scalar")
+        cast_w1(0, 0, False)
         w1_raw[0, 1] = load_w1(0, 1)
         quantise_w1(0, 0)
-        cast_w1(1, 0, "scalar")
+        cast_w1(1, 0, False)
         w1_raw[1, 1] = load_w1(1, 1)
         quantise_w1(1, 0)
-        nc.scalar.activation(root[:], slot_rows[:, :, 0:b2_row], ACT.Abs_reciprocal_sqrt)
-        nc.scalar.activation(inverse[:], root[:], ACT.Square)
-        nc.scalar.copy(out=b2_t[:], in_=slot_rows[:, :, b2_row:b3_row])
+        nc.scalar.copy(out=by_row[:], in_=slot_rows[:, :, 0:b3_row])
         nc.scalar.copy(out=b3_t[:], in_=by_tile[:, b3_row : b3_row + tiles_n])
         nc.vector.tensor_copy(v_w[0][:], tab_w[0][:].bitcast(U32).indirect(offs_t[:]))
         tab2_w[0] = load_words("tab2_w0", tab2_words[0], AT_TAB2[0])
-        w4_raw = stage.tile([P, n2, H // 2], I32, name="w4_raw", align_bytes=64, offset=AT_W4_RAW)
+        w4_raw = placed("w4_raw", [P, n2, H // 2], I32, AT_W4_RAW)
         nc.sync.dma_start(out=w4_raw[:], in_=w4_words.rearrange("a p n -> p a n").bitcast(I32))
-        for u in range(2):
-            for t in range(PACK):
-                basin_pass(0, t, u, 0)
+        order0 = [(2 * pair + j, u) for pair in range(2) for u in range(2) for j in range(2)]
+        for t, u in order0:
+            basin_pass(0, t, u, 0)
         v2_s_rows = keep.tile([P, M], U8, name="v2_s_rows", align_bytes=64)
         nc.vector.tensor_copy(v2_s_rows[:], tab2_s[:].indirect(offs2_t[:]))
-        v2_s = to_planes(nc.sync, "v2_s", v2_s_rows, n2, LATE_ROWS, 0)
+        v2_s = to_planes("v2_s", v2_s_rows[:], n2, LATE_ROWS, 0)
         tab2_w[1] = load_words("tab2_w1", tab2_words[1], AT_TAB2[1])
         w4_s_rows = keep.tile([P, H], U8, name="w4_s_rows", align_bytes=64)
         nc.vector.tensor_copy(
             out=w4_s_rows[:].rearrange("p (b t c i) -> p b c t i", t=PACK, c=8, i=16),
             in_=w4_s_raw[:].rearrange("p (b c i t) -> p b c t i", t=PACK, c=8, i=16),
         )
-        w4_s = to_planes(nc.sync, "w4_s", w4_s_rows, n2, LATE_ROWS, 0)
+        w4_s = to_planes("w4_s", w4_s_rows[:], n2, LATE_ROWS, 0)
         for u in range(2):
             entries = offs_t[:, u * BANK // LIST_ROWS : (u + 1) * BANK // LIST_ROWS]
             nc.vector.tensor_copy(v_w[1][:, u * BANK : (u + 1) * BANK], tab_w[1][:].bitcast(U32).indirect(entries))
-            for t in range(PACK):
-                basin_pass(0, t, u, 1)
+        for t, u in order0:
+            basin_pass(0, t, u, 1)
         tab2_w[2] = load_words("tab2_w2", tab2_words[2], AT_TAB2[2])
-        for t, u in ((0, 0), (1, 0), (0, 1), (1, 1), (2, 0), (2, 1), (3, 0), (3, 1)):
+        for t, u in order0:
             empty_basin(0, t, u)
 
-        cast_w1(0, 1, "vector")
-        w8_w = stage.tile([P, n3, N], I32, name="w8_w", align_bytes=64, offset=AT_W8)
+        cast_w1(0, 1, True)
+        w8_w = placed("w8_w", [P, n3, N], I32, AT_W1[0])
         nc.sync.dma_start(out=w8_w[:], in_=w8_words.rearrange("a p n t -> p a (n t)").bitcast(I32))
-        w8_s = stage.tile([P, n3, N], U8, name="w8_s", align_bytes=64, offset=AT_W8 + 6 * KIB)
-        for g in range(4):
+        w8_s = placed("w8_s", [P, n3, N], U8, AT_W1[0] + 6 * KIB)
+        for g in (0, 2, 1, 3):
             nc.sync.dma_start(
                 out=w8_s[32 * g + W8_PLANE : 32 * g + W8_PLANE + 4].bitcast(I32),
                 in_=w8_scales[:, 4 * g : 4 * g + 4, :].rearrange("a i n -> i a n").bitcast(I32),
             )
-        pick(0, 0)
+        pick0(0)
         quantise_w1(0, 1)
-        pick(0, 1)
-        cast_w1(1, 1, "scalar")
-        pick(0, 2)
-        pick(0, 3)
+        pick0(1)
+        cast_w1(1, 1, False)
+        pick0(2)
+        pick0(3)
         quantise_w1(1, 1)
         for t in range(PACK):
             for u in range(2):
                 for a in range(n1):
                     basin_pass(1, t, u, a)
         gather_v2(0)
-        w4_w = keep.tile([P, n2, 2 * H], U8, name="w4_w", align_bytes=64)
+        w4_w = placed("w4_w", [P, n2, 2 * H], U8, AT_W1[1] + 2 * KIB)
         nc.vector.tensor_copy(
             out=w4_w[:].bitcast(U16).rearrange("p a (b t m) -> p (a b) m t", t=PACK, m=P),
             in_=w4_raw[:].bitcast(U16).rearrange("p a (b m t) -> p (a b) m t", t=PACK, m=P),
         )
 
-        def empty_slot(t):
+        root0 = keep.tile([P, PACK, M], F32, name="root0")
+        inverse0 = placed("inverse0", [P, PACK, M], F32, AT_W4_RAW)
+        for t in range(PACK):
+            inverse_root(root0[:, t, :], squared0[t][:], 0, t)
+        gpsimd_square(inverse0[:, 0:2, :], root0[:, 0:2, :])
+        for t in range(PACK):
             for u in range(2):
                 empty_basin(1, t, u)
-            pick(1, t)
+        nc.scalar.activation(inverse0[:, 3, :], root0[:, 3, :], ACT.Square)
 
-        inverse_root(0, (0, 1), 0, M)
         gather_v2(1)
-        empty_slot(0)
+        pick1(0, 0)
+        pick1(0, 1)
+        gpsimd_square(inverse0[:, 2, :], root0[:, 2, :])
         gather_v2(2)
-        square(0, (0, 1), 0, M)
-        empty_slot(1)
-        empty_slot(2)
+        pick1(0, 2)
+        pick1(0, 3)
+        for t in range(PACK):
+            pick1(1, t)
         for a in range(n2):
             for t in range(PACK):
                 own_pass(0, t, a)
-        inverse_root(0, (2, 3), 0, M)
-        empty_slot(3)
-        square(0, (2, 3), 0, M)
         for t in range(PACK):
-            for a in range(n2):
-                own_pass(1, t, a)
-        numerator(range(PACK))
-        quantise_z(0, 0, half)
+            order = (0, 1, 2) if t < 2 else (2, 0, 1)
+            for a in order:
+                own_pass(1, t, a, order)
 
+        inverse_roots1(0, 0)
+        numerator(0, 0, range(PACK))
+        last_squares1(0, 0)
+        inverse_roots1(0, 1)
+        numerator(0, 1, (0, 1))
+        last_squares1(0, 1)
+        numerator(0, 1, (2, 3))
+        squared1[1, 1] = placed("squared1_11", [P, 2, HALF], F32, AT_LAST_SQUARE)
+        nc.scalar.activation(squared1[1, 1][:], picked1[1, 1][:], ACT.Square)
+        inverse_roots1(1, 0)
+        inverse_roots1(1, 1)
+        last_squares1(1, 0)
+        last_squares1(1, 1)
+
+        group_z(0, 0)
+        ratio(0, range(PACK))
+        quantise_z(0, 0)
+        group_z(1, 0)
+        group_z(0, 1)
+        quantise_z(1, 0)
         first = [bank(pair) for pair in range(tiles_n // 2)]
 
         def first_place(c):
-            return first[c // 2][:, (c % 2) * half : (c % 2 + 1) * half]
+            return first[c // 2][:, (c % 2) * HALF : (c % 2 + 1) * HALF]
 
-        for c in range(tiles_n):
-            score_pass(first_place(c), 0, c, 0, c % 2 == 0, False)
-        for m0 in (0, half):
-            run = slice(m0, m0 + half)
-            nc.scalar.activation(squared[1][:, 3, run], picked[1, 3][:, run], ACT.Square)
-            inverse_root(1, range(PACK), m0, half)
-            square(1, range(PACK), m0, half)
-            ratio(1, range(PACK), m0, half)
-            quantise_z(1, m0, half)
-            if m0 == 0:
-                for c in range(tiles_n):
-                    score_pass(first_place(c), 0, c, 1, False, c % 2 == 1)
-                quantise_z(0, half, half)
         for pair in range(tiles_n // 2):
-            res = keep.tile([P, 2, half], F32, name="res_first%d" % pair)
+            for blk in range(n3):
+                for j in range(2):
+                    score_pass(first_place(2 * pair + j), 0, 2 * pair + j, blk, (blk, j) == (0, 0), (blk, j) == (1, 1))
+        ratio(1, range(PACK))
+        quantise_z(0, 1)
+        group_z(1, 1)
+        quantise_z(1, 1)
+        for pair in range(tiles_n // 2):
+            res = keep.tile([P, 2, HALF], F32, name="res_first%d" % pair)
             for j in range(2):
                 add_bias(res[:, j, :], first_place(2 * pair + j), 2 * pair + j, False)
             store_pair(res, pair, 0)
 
         second = [bank((3 + c) % 8) for c in range(tiles_n)]
         for c in range(tiles_n):
-            score_pass(second[c][:, 0:half], half, c, 0, True, False)
+            score_pass(second[c][:, 0:HALF], 1, c, 0, True, False)
         for pair in range(tiles_n // 2):
-            res = keep.tile([P, 2, half], F32, name="res_second%d" % pair)
+            res = keep.tile([P, 2, HALF], F32, name="res_second%d" % pair)
             for j in range(2):
                 c = 2 * pair + j
-                score_pass(second[c][:, 0:half], half, c, 1, False, True)
-                add_bias(res[:, j, :], second[c][:, 0:half], c, j == 0)
-            store_pair(res, pair, half)
+                score_pass(second[c][:, 0:HALF], 1, c, 1, False, True)
+                add_bias(res[:, j, :], second[c][:, 0:HALF], c, j == 0)
+            store_pair(res, pair, 1)

@@ -359,18 +359,20 @@ def tile_list_subcatchment_nitrate_loads_kernel(
 
         root0 = keep.tile([P, PACK, M], F32, name="root0")
         inverse0 = placed("inverse0", [P, PACK, M], F32, AT_W4_RAW)
-        for t in range(PACK):
+        for t in range(2):
             inverse_root(root0[:, t, :], squared0[t][:], 0, t)
         gpsimd_square(inverse0[:, 0:2, :], root0[:, 0:2, :])
         for t in range(PACK):
             for u in range(2):
                 empty_basin(1, t, u)
-        nc.scalar.activation(inverse0[:, 3, :], root0[:, 3, :], ACT.Square)
+        for t in range(2, PACK):
+            inverse_root(root0[:, t, :], squared0[t][:], 0, t)
+        for t in range(2, PACK):
+            nc.scalar.activation(inverse0[:, t, :], root0[:, t, :], ACT.Square)
 
         gather_v2(1)
         pick1(0, 0)
         pick1(0, 1)
-        gpsimd_square(inverse0[:, 2, :], root0[:, 2, :])
         gather_v2(2)
         pick1(0, 2)
         pick1(0, 3)

@@ -302,6 +302,10 @@ def tile_list_subcatchment_nitrate_loads_kernel(
         cast_w1(1, 0, False)
         w1_raw[1, 1] = load_w1(1, 1)
         quantise_w1(1, 0)
+        root_kap = keep.tile([P, 2], F32, name="root_kap")
+        inverse_kap = keep.tile([P, 2], F32, name="inverse_kap")
+        nc.scalar.activation(root_kap[:], slot_rows[:, 2:PACK, 0], ACT.Abs_reciprocal_sqrt)
+        nc.scalar.activation(inverse_kap[:], root_kap[:], ACT.Square)
         nc.scalar.copy(out=by_row[:], in_=slot_rows[:, :, 0:b3_row])
         nc.scalar.copy(out=b3_t[:], in_=by_tile[:, b3_row : b3_row + tiles_n])
         nc.vector.tensor_copy(v_w[0][:], tab_w[0][:].bitcast(U32).indirect(offs_t[:]))
@@ -358,17 +362,20 @@ def tile_list_subcatchment_nitrate_loads_kernel(
         )
 
         root0 = keep.tile([P, PACK, M], F32, name="root0")
-        inverse0 = placed("inverse0", [P, PACK, M], F32, AT_W4_RAW)
+        inverse0 = keep.tile([P, PACK, M], F32, name="inverse0")
         for t in range(2):
             inverse_root(root0[:, t, :], squared0[t][:], 0, t)
-        gpsimd_square(inverse0[:, 0:2, :], root0[:, 0:2, :])
         for t in range(PACK):
             for u in range(2):
                 empty_basin(1, t, u)
+            if t == 0:
+                nc.scalar.activation(inverse0[:, 0:2, :], root0[:, 0:2, :], ACT.Square)
         for t in range(2, PACK):
-            inverse_root(root0[:, t, :], squared0[t][:], 0, t)
+            nc.scalar.activation(
+                root0[:, t, :], squared0[t][:], ACT.Abs_reciprocal_sqrt, bias=1.0, scale=inverse_kap[:, t - 2 : t - 1]
+            )
         for t in range(2, PACK):
-            nc.scalar.activation(inverse0[:, t, :], root0[:, t, :], ACT.Square)
+            nc.scalar.activation(inverse0[:, t, :], root0[:, t, :], ACT.Square, scale=root_kap[:, t - 2 : t - 1])
 
         gather_v2(1)
         pick1(0, 0)

@@ -198,7 +198,7 @@ def tile_list_subcatchment_nitrate_loads_kernel(
                 elif pair == 0:
                     picked1[half, pair] = placed(name, [P, 2, HALF], F32, AT_TAB2[1])
                 else:
-                    picked1[half, pair] = placed(name, [P, 2, HALF], F32, AT_TAB2[2] + 4 * KIB)
+                    picked1[half, pair] = placed(name, [P, 2, HALF], F32, AT_TAB2[1] + 2 * KIB)
             entries = pos_t[:, half * HALF // LIST_ROWS : (half + 1) * HALF // LIST_ROWS]
             nc.vector.tensor_copy(picked1[half, pair][:, j, :], h[1, t][:].indirect(entries))
             if j == 1:
@@ -206,22 +206,29 @@ def tile_list_subcatchment_nitrate_loads_kernel(
                     squared1[half, pair] = keep.tile([P, 2, HALF], F32, name="squared1_%d%d" % (half, pair))
                     gpsimd_square(squared1[half, pair][:], picked1[half, pair][:])
 
-        v2_w, own, tab2_w = {}, {}, {}
+        v2_w, own, own_bank, tab2_w = {}, {}, {}, {}
 
         def gather_v2(a):
             name = "v2_w%d" % a
             v2_w[a] = placed(name, [P, M], U32, AT_W1[1]) if a == 0 else keep.tile([P, M], U32, name=name, align_bytes=64)
-            nc.vector.tensor_copy(v2_w[a][:], tab2_w[a][:].bitcast(U32).indirect(offs2_t[:]))
+            parts = 2 if a == n2 - 1 else 1
+            width = M // parts
+            for i in range(parts):
+                entries = offs2_t[:, i * width // LIST_ROWS : (i + 1) * width // LIST_ROWS]
+                nc.vector.tensor_copy(v2_w[a][:, i * width : (i + 1) * width], tab2_w[a][:].bitcast(U32).indirect(entries))
 
-        def own_pass(blk, t, a, order=(0, 1, 2)):
-            if a == order[0]:
-                own[blk, t] = bank(PACK * blk + t)
+        def own_pass(blk, half, t, a, order):
+            pair, j = divmod(t, 2)
+            if (a, j) == (order[0], 0):
+                own_bank[blk, half, pair] = bank(4 * half + 2 * blk + pair)
+            own[blk, half, t] = own_bank[blk, half, pair][:, j * HALF : (j + 1) * HALF]
             c0 = blk * PASS + t * P
+            run = slice(half * HALF, (half + 1) * HALF)
             nc.tensor.matmul_mx(
-                out=own[blk, t][:], lhsT=w4_w[:, a, 2 * c0 : 2 * (c0 + P)].bitcast(FP4X4),
+                out=own[blk, half, t], lhsT=w4_w[:, a, 2 * c0 : 2 * (c0 + P)].bitcast(FP4X4),
                 lhsT_scale=w4_s[:, a, c0 : c0 + P],
-                rhs=v2_w[a][:].bitcast(FP8X4), rhs_scale=v2_s[:, a, :],
-                start=(a == order[0]), stop=(a == order[-1]),
+                rhs=v2_w[a][:, run].bitcast(FP8X4), rhs_scale=v2_s[:, a, run],
+                start=(a, j) == (order[0], 0), stop=(a, j) == (order[-1], 1),
             )
 
         inverse1 = [keep.tile([P, PACK, HALF], F32, name="inverse1_%d" % half) for half in range(2)]
@@ -244,14 +251,14 @@ def tile_list_subcatchment_nitrate_loads_kernel(
 
         def numerator(blk, half, ts):
             for t in ts:
-                src = own[blk, t][:, half * HALF : (half + 1) * HALF]
+                src = own[blk, half, t]
                 nc.scalar.activation(top[blk, half][:, t, :], src, ACT.Relu, bias=b2_of(blk, t))
 
         def ratio(half, ts):
             for t in ts:
                 x = inverse1[half][:, t, :]
                 nc.vector.scalar_tensor_tensor(
-                    out=x, in0=own[1, t][:, half * HALF : (half + 1) * HALF], scalar=b2_of(1, t), in1=x,
+                    out=x, in0=own[1, half, t], scalar=b2_of(1, t), in1=x,
                     op0=ALU.add, op1=ALU.mult,
                 )
 
@@ -380,26 +387,24 @@ def tile_list_subcatchment_nitrate_loads_kernel(
         gather_v2(1)
         pick1(0, 0)
         pick1(0, 1)
-        gather_v2(2)
         pick1(0, 2)
         pick1(0, 3)
+        gather_v2(2)
         for t in range(PACK):
             pick1(1, t)
-        for a in range(n2):
-            for t in range(PACK):
-                own_pass(0, t, a)
-        for t in range(PACK):
-            order = (0, 1, 2) if t < 2 else (2, 0, 1)
-            for a in order:
-                own_pass(1, t, a, order)
+        for half in range(2):
+            for blk in range(n3):
+                order = (0, 2, 1) if half == 1 else (0, 1, 2)
+                for a in order:
+                    for t in range(PACK):
+                        own_pass(blk, half, t, a, order)
 
         inverse_roots1(0, 0)
-        numerator(0, 0, range(PACK))
-        last_squares1(0, 0)
         inverse_roots1(0, 1)
-        numerator(0, 1, (0, 1))
+        last_squares1(0, 0)
         last_squares1(0, 1)
-        numerator(0, 1, (2, 3))
+        numerator(0, 0, range(PACK))
+        numerator(0, 1, range(PACK))
         squared1[1, 1] = placed("squared1_11", [P, 2, HALF], F32, AT_LAST_SQUARE)
         nc.scalar.activation(squared1[1, 1][:], picked1[1, 1][:], ACT.Square)
         inverse_roots1(1, 0)
@@ -424,8 +429,17 @@ def tile_list_subcatchment_nitrate_loads_kernel(
                     score_pass(first_place(2 * pair + j), 0, 2 * pair + j, blk, (blk, j) == (0, 0), (blk, j) == (1, 1))
         ratio(1, range(PACK))
         quantise_z(0, 1)
-        group_z(1, 1)
-        quantise_z(1, 1)
+        z_w[1, 1] = keep.tile([P, HALF], U32, name="z_w11", align_bytes=64)
+        z_s[1, 1] = keep.tile([P, HALF], U8, name="z_s11", align_bytes=64)
+        last = [keep.tile([P, P, PACK], BF16, name="z_last%d" % i, align_bytes=64) for i in range(2)]
+        for i in range(2):
+            src = by_lines(inverse1[1][:, :, i * P : (i + 1) * P])
+            nc.vector.tensor_scalar_max(out=last[i][:].rearrange("p (c i) t -> p c t i", i=4), in0=src, scalar1=0.0)
+        for i in range(2):
+            nc.vector.quantize_mx(
+                out=z_w[1, 1][:, i * P : (i + 1) * P].bitcast(FP8X4), scales=z_s[1, 1][:, i * P : (i + 1) * P],
+                in_=last[i][:].rearrange("p m t -> p (m t)"),
+            )
         for pair in range(tiles_n // 2):
             res = keep.tile([P, 2, HALF], F32, name="res_first%d" % pair)
             for j in range(2):

@@ -198,7 +198,7 @@ def tile_list_subcatchment_nitrate_loads_kernel(
                 elif pair == 0:
                     picked1[half, pair] = placed(name, [P, 2, HALF], F32, AT_TAB2[1])
                 else:
-                    picked1[half, pair] = placed(name, [P, 2, HALF], F32, AT_TAB2[1] + 2 * KIB)
+                    picked1[half, pair] = placed(name, [P, 2, HALF], F32, AT_TAB2[2] + 4 * KIB)
             entries = pos_t[:, half * HALF // LIST_ROWS : (half + 1) * HALF // LIST_ROWS]
             nc.vector.tensor_copy(picked1[half, pair][:, j, :], h[1, t][:].indirect(entries))
             if j == 1:
@@ -225,7 +225,7 @@ def tile_list_subcatchment_nitrate_loads_kernel(
             c0 = blk * PASS + t * P
             run = slice(half * HALF, (half + 1) * HALF)
             nc.tensor.matmul_mx(
-                out=own[blk, half, t], lhsT=w4_w[:, a, 2 * c0 : 2 * (c0 + P)].bitcast(FP4X4),
+                out=own[blk, half, t], lhsT=w4_w[blk, a][:, 2 * t * P : 2 * (t + 1) * P].bitcast(FP4X4),
                 lhsT_scale=w4_s[:, a, c0 : c0 + P],
                 rhs=v2_w[a][:, run].bitcast(FP8X4), rhs_scale=v2_s[:, a, run],
                 start=(a, j) == (order[0], 0), stop=(a, j) == (order[-1], 1),
@@ -362,21 +362,33 @@ def tile_list_subcatchment_nitrate_loads_kernel(
                 for a in range(n1):
                     basin_pass(1, t, u, a)
         gather_v2(0)
-        w4_w = placed("w4_w", [P, n2, 2 * H], U8, AT_W1[1] + 2 * KIB)
+        w4_w0 = placed("w4_w0", [P, n2, 2 * PASS], U8, AT_W1[1] + 2 * KIB)
         nc.vector.tensor_copy(
-            out=w4_w[:].bitcast(U16).rearrange("p a (b t m) -> p (a b) m t", t=PACK, m=P),
-            in_=w4_raw[:].bitcast(U16).rearrange("p a (b m t) -> p (a b) m t", t=PACK, m=P),
+            out=w4_w0[:].bitcast(U16).rearrange("p a (t m) -> p a m t", t=PACK),
+            in_=w4_raw[:].bitcast(U16)[:, :, 0:PASS].rearrange("p a (m t) -> p a m t", t=PACK),
         )
+        w4_w = {(0, a): w4_w0[:, a, :] for a in range(n2)}
+
+        def deal_w4(a, offset):
+            words = placed("w4_w1%d" % a, [P, 2 * PASS], U8, offset)
+            nc.gpsimd.tensor_copy(
+                out=words[:].rearrange("p (t m e) -> p t m e", t=PACK, e=2),
+                in_=w4_raw[:].bitcast(U8)[:, a, 2 * PASS : 2 * H].rearrange("p (m t e) -> p t m e", t=PACK, e=2),
+            )
+            w4_w[1, a] = words[:]
+
+        deal_w4(0, AT_TAB2[0])
+        deal_w4(1, AT_TAB2[0] + KIB)
 
         root0 = keep.tile([P, PACK, M], F32, name="root0")
         inverse0 = keep.tile([P, PACK, M], F32, name="inverse0")
         for t in range(2):
             inverse_root(root0[:, t, :], squared0[t][:], 0, t)
+        nc.scalar.activation(inverse0[:, 0, :], root0[:, 0, :], ACT.Square)
         for t in range(PACK):
             for u in range(2):
                 empty_basin(1, t, u)
-            if t == 0:
-                nc.scalar.activation(inverse0[:, 0:2, :], root0[:, 0:2, :], ACT.Square)
+        nc.scalar.activation(inverse0[:, 1, :], root0[:, 1, :], ACT.Square)
         for t in range(2, PACK):
             nc.scalar.activation(
                 root0[:, t, :], squared0[t][:], ACT.Abs_reciprocal_sqrt, bias=1.0, scale=inverse_kap[:, t - 2 : t - 1]
@@ -387,9 +399,10 @@ def tile_list_subcatchment_nitrate_loads_kernel(
         gather_v2(1)
         pick1(0, 0)
         pick1(0, 1)
+        deal_w4(2, AT_TAB2[1])
+        gather_v2(2)
         pick1(0, 2)
         pick1(0, 3)
-        gather_v2(2)
         for t in range(PACK):
             pick1(1, t)
         for half in range(2):
@@ -400,10 +413,11 @@ def tile_list_subcatchment_nitrate_loads_kernel(
                         own_pass(blk, half, t, a, order)
 
         inverse_roots1(0, 0)
-        inverse_roots1(0, 1)
+        numerator(0, 0, (0, 1))
         last_squares1(0, 0)
+        inverse_roots1(0, 1)
+        numerator(0, 0, (2, 3))
         last_squares1(0, 1)
-        numerator(0, 0, range(PACK))
         numerator(0, 1, range(PACK))
         squared1[1, 1] = placed("squared1_11", [P, 2, HALF], F32, AT_LAST_SQUARE)
         nc.scalar.activation(squared1[1, 1][:], picked1[1, 1][:], ACT.Square)

@@ -179,13 +179,14 @@ def tile_list_subcatchment_nitrate_loads_kernel(
         def inverse_root(dst, src, blk, t):
             nc.scalar.activation(dst, src, ACT.Abs_reciprocal_sqrt, bias=kap_of(blk, t))
 
-        squared0 = {}
+        picked0, squared0 = {}, {}
 
         def pick0(t):
-            picked = keep.tile([P, M], F32, name="picked0%d" % t)
-            nc.vector.tensor_copy(picked[:], h[0, t][:].indirect(pos_t[:]))
-            squared0[t] = keep.tile([P, M], F32, name="squared0%d" % t)
-            gpsimd_square(squared0[t][:], picked[:])
+            picked0[t] = keep.tile([P, M], F32, name="picked0%d" % t)
+            nc.vector.tensor_copy(picked0[t][:], h[0, t][:].indirect(pos_t[:]))
+            if t < PACK - 1:
+                squared0[t] = keep.tile([P, M], F32, name="squared0%d" % t)
+                gpsimd_square(squared0[t][:], picked0[t][:])
 
         picked1, squared1 = {}, {}
 
@@ -362,23 +363,25 @@ def tile_list_subcatchment_nitrate_loads_kernel(
                 for a in range(n1):
                     basin_pass(1, t, u, a)
         gather_v2(0)
-        w4_w0 = placed("w4_w0", [P, n2, 2 * PASS], U8, AT_W1[1] + 2 * KIB)
+        w4_early = placed("w4_early", [P, n2 - 1, 2 * H], U8, AT_W1[1] + 2 * KIB)
         nc.vector.tensor_copy(
-            out=w4_w0[:].bitcast(U16).rearrange("p a (t m) -> p a m t", t=PACK),
-            in_=w4_raw[:].bitcast(U16)[:, :, 0:PASS].rearrange("p a (m t) -> p a m t", t=PACK),
+            out=w4_early[:].bitcast(U16).rearrange("p a (b t m) -> p (a b) m t", t=PACK, m=P),
+            in_=w4_raw[:, 0 : n2 - 1, :].bitcast(U16).rearrange("p a (b m t) -> p (a b) m t", t=PACK, m=P),
         )
-        w4_w = {(0, a): w4_w0[:, a, :] for a in range(n2)}
+        w4_w = {(blk, a): w4_early[:, a, 2 * blk * PASS : 2 * (blk + 1) * PASS] for blk in range(n3) for a in range(n2 - 1)}
 
-        def deal_w4(a, offset):
-            words = placed("w4_w1%d" % a, [P, 2 * PASS], U8, offset)
+        def deal_last_pass(blk, offset):
+            words = placed("w4_last%d" % blk, [P, 2 * PASS], U8, offset)
+            src = w4_raw[:].bitcast(U8)[:, n2 - 1, 2 * blk * PASS : 2 * (blk + 1) * PASS]
             nc.gpsimd.tensor_copy(
                 out=words[:].rearrange("p (t m e) -> p t m e", t=PACK, e=2),
-                in_=w4_raw[:].bitcast(U8)[:, a, 2 * PASS : 2 * H].rearrange("p (m t e) -> p t m e", t=PACK, e=2),
+                in_=src.rearrange("p (m t e) -> p t m e", t=PACK, e=2),
             )
-            w4_w[1, a] = words[:]
+            w4_w[blk, n2 - 1] = words[:]
 
-        deal_w4(0, AT_TAB2[0])
-        deal_w4(1, AT_TAB2[0] + KIB)
+        deal_last_pass(0, AT_TAB2[0])
+        squared0[PACK - 1] = placed("squared03", [P, M], F32, AT_TAB2[0] + 2 * KIB)
+        gpsimd_square(squared0[PACK - 1][:], picked0[PACK - 1][:])
 
         root0 = keep.tile([P, PACK, M], F32, name="root0")
         inverse0 = keep.tile([P, PACK, M], F32, name="inverse0")
@@ -399,7 +402,7 @@ def tile_list_subcatchment_nitrate_loads_kernel(
         gather_v2(1)
         pick1(0, 0)
         pick1(0, 1)
-        deal_w4(2, AT_TAB2[1])
+        deal_last_pass(1, AT_TAB2[1])
         gather_v2(2)
         pick1(0, 2)
         pick1(0, 3)
@@ -412,11 +415,10 @@ def tile_list_subcatchment_nitrate_loads_kernel(
                     for t in range(PACK):
                         own_pass(blk, half, t, a, order)
 
+        numerator(0, 0, range(PACK))
         inverse_roots1(0, 0)
-        numerator(0, 0, (0, 1))
-        last_squares1(0, 0)
         inverse_roots1(0, 1)
-        numerator(0, 0, (2, 3))
+        last_squares1(0, 0)
         last_squares1(0, 1)
         numerator(0, 1, range(PACK))
         squared1[1, 1] = placed("squared1_11", [P, 2, HALF], F32, AT_LAST_SQUARE)

@@ -34,6 +34,8 @@ AT_TAB2_S = 48 * KIB
 AT_TAB2 = (AT_TAB[0], AT_TAB2_S, AT_TAB[1])
 AT_W4_RAW = AT_TAB[0] + 8 * KIB
 AT_LAST_SQUARE = 56 * KIB
+AT_LAST_GROUPED = 60 * KIB
+AT_V2_S_ROWS = 64 * KIB
 
 
 def tile_list_subcatchment_nitrate_loads_kernel(
@@ -138,7 +140,11 @@ def tile_list_subcatchment_nitrate_loads_kernel(
         grouped, w1_w, w1_s = {}, {}, {}
 
         def cast_w1(a, blk, on_vector):
-            grouped[a, blk] = keep.tile([P, PACK, P, PACK], BF16, name="w1_grouped%d%d" % (a, blk), align_bytes=64)
+            name = "w1_grouped%d%d" % (a, blk)
+            if (a, blk) == (1, 1):
+                grouped[a, blk] = placed(name, [P, PACK, P, PACK], BF16, AT_LAST_GROUPED)
+            else:
+                grouped[a, blk] = keep.tile([P, PACK, P, PACK], BF16, name=name, align_bytes=64)
             src = w1_raw[a, blk][:].rearrange("p j (m t) -> p m j t", t=PACK)
             dst = grouped[a, blk][:].rearrange("p t m j -> p m j t")
             if on_vector:
@@ -197,7 +203,7 @@ def tile_list_subcatchment_nitrate_loads_kernel(
                 if half == 1:
                     picked1[half, pair] = placed(name, [P, 2, HALF], F32, AT_TAB2[2] + 2 * KIB * pair)
                 elif pair == 0:
-                    picked1[half, pair] = placed(name, [P, 2, HALF], F32, AT_TAB2[1])
+                    picked1[half, pair] = placed(name, [P, 2, HALF], F32, AT_V2_S_ROWS)
                 else:
                     picked1[half, pair] = placed(name, [P, 2, HALF], F32, AT_TAB2[2] + 4 * KIB)
             entries = pos_t[:, half * HALF // LIST_ROWS : (half + 1) * HALF // LIST_ROWS]
@@ -317,22 +323,22 @@ def tile_list_subcatchment_nitrate_loads_kernel(
         nc.scalar.copy(out=by_row[:], in_=slot_rows[:, :, 0:b3_row])
         nc.scalar.copy(out=b3_t[:], in_=by_tile[:, b3_row : b3_row + tiles_n])
         nc.vector.tensor_copy(v_w[0][:], tab_w[0][:].bitcast(U32).indirect(offs_t[:]))
-        tab2_w[0] = load_words("tab2_w0", tab2_words[0], AT_TAB2[0])
         w4_raw = placed("w4_raw", [P, n2, H // 2], I32, AT_W4_RAW)
         nc.sync.dma_start(out=w4_raw[:], in_=w4_words.rearrange("a p n -> p a n").bitcast(I32))
+        tab2_w[0] = load_words("tab2_w0", tab2_words[0], AT_TAB2[0])
         order0 = [(2 * pair + j, u) for pair in range(2) for u in range(2) for j in range(2)]
         for t, u in order0:
             basin_pass(0, t, u, 0)
-        v2_s_rows = keep.tile([P, M], U8, name="v2_s_rows", align_bytes=64)
-        nc.vector.tensor_copy(v2_s_rows[:], tab2_s[:].indirect(offs2_t[:]))
-        v2_s = to_planes("v2_s", v2_s_rows[:], n2, LATE_ROWS, 0)
-        tab2_w[1] = load_words("tab2_w1", tab2_words[1], AT_TAB2[1])
         w4_s_rows = keep.tile([P, H], U8, name="w4_s_rows", align_bytes=64)
         nc.vector.tensor_copy(
             out=w4_s_rows[:].rearrange("p (b t c i) -> p b c t i", t=PACK, c=8, i=16),
             in_=w4_s_raw[:].rearrange("p (b c i t) -> p b c t i", t=PACK, c=8, i=16),
         )
         w4_s = to_planes("w4_s", w4_s_rows[:], n2, LATE_ROWS, 0)
+        v2_s_rows = placed("v2_s_rows", [P, M], U8, AT_V2_S_ROWS)
+        nc.vector.tensor_copy(v2_s_rows[:], tab2_s[:].indirect(offs2_t[:]))
+        tab2_w[1] = load_words("tab2_w1", tab2_words[1], AT_TAB2[1])
+        v2_s = to_planes("v2_s", v2_s_rows[:], n2, LATE_ROWS, 0)
         for u in range(2):
             entries = offs_t[:, u * BANK // LIST_ROWS : (u + 1) * BANK // LIST_ROWS]
             nc.vector.tensor_copy(v_w[1][:, u * BANK : (u + 1) * BANK], tab_w[1][:].bitcast(U32).indirect(entries))
@@ -362,7 +368,6 @@ def tile_list_subcatchment_nitrate_loads_kernel(
             for u in range(2):
                 for a in range(n1):
                     basin_pass(1, t, u, a)
-        gather_v2(0)
         w4_early = placed("w4_early", [P, n2 - 1, 2 * H], U8, AT_W1[1] + 2 * KIB)
         nc.vector.tensor_copy(
             out=w4_early[:].bitcast(U16).rearrange("p a (b t m) -> p (a b) m t", t=PACK, m=P),
@@ -379,9 +384,11 @@ def tile_list_subcatchment_nitrate_loads_kernel(
             )
             w4_w[blk, n2 - 1] = words[:]
 
-        deal_last_pass(0, AT_TAB2[0])
-        squared0[PACK - 1] = placed("squared03", [P, M], F32, AT_TAB2[0] + 2 * KIB)
+        gather_v2(0)
+        squared0[PACK - 1] = placed("squared03", [P, M], F32, AT_LAST_GROUPED)
         gpsimd_square(squared0[PACK - 1][:], picked0[PACK - 1][:])
+        for blk in range(n3):
+            deal_last_pass(blk, AT_LAST_GROUPED + (2 + blk) * KIB)
 
         root0 = keep.tile([P, PACK, M], F32, name="root0")
         inverse0 = keep.tile([P, PACK, M], F32, name="inverse0")
@@ -402,7 +409,6 @@ def tile_list_subcatchment_nitrate_loads_kernel(
         gather_v2(1)
         pick1(0, 0)
         pick1(0, 1)
-        deal_last_pass(1, AT_TAB2[1])
         gather_v2(2)
         pick1(0, 2)
         pick1(0, 3)

@@ -36,6 +36,7 @@ AT_W4_RAW = AT_TAB[0] + 8 * KIB
 AT_LAST_SQUARE = 56 * KIB
 AT_LAST_GROUPED = 60 * KIB
 AT_V2_S_ROWS = 64 * KIB
+AT_Z = 68 * KIB
 
 
 def tile_list_subcatchment_nitrate_loads_kernel(
@@ -275,13 +276,14 @@ def tile_list_subcatchment_nitrate_loads_kernel(
             return x.rearrange("p t (c i) -> p c t i", i=4)
 
         def group_z(blk, half):
-            z_grouped[blk, half] = keep.tile([P, HALF, PACK], BF16, name="z_grouped%d%d" % (blk, half), align_bytes=64)
-            dst = z_grouped[blk, half][:].rearrange("p (c i) t -> p c t i", i=4)
-            if (blk, half) in top:
-                src = inverse0[:, :, half * HALF : (half + 1) * HALF] if blk == 0 else inverse1[half][:]
-                nc.vector.tensor_tensor(out=dst, in0=by_lines(src), in1=by_lines(top[blk, half][:]), op=ALU.mult)
+            name = "z_grouped%d%d" % (blk, half)
+            if half == 0:
+                z_grouped[blk, half] = keep.tile([P, HALF, PACK], BF16, name=name, align_bytes=64)
             else:
-                nc.vector.tensor_scalar_max(out=dst, in0=by_lines(inverse1[half][:]), scalar1=0.0)
+                z_grouped[blk, half] = placed(name, [P, HALF, PACK], BF16, AT_Z - KIB - KIB // 2)
+            dst = z_grouped[blk, half][:].rearrange("p (c i) t -> p c t i", i=4)
+            src = inverse0[:, :, half * HALF : (half + 1) * HALF]
+            nc.vector.tensor_tensor(out=dst, in0=by_lines(src), in1=by_lines(top[blk, half][:]), op=ALU.mult)
 
         def quantise_z(blk, half):
             z_w[blk, half] = keep.tile([P, HALF], U32, name="z_w%d%d" % (blk, half), align_bytes=64)
@@ -398,7 +400,7 @@ def tile_list_subcatchment_nitrate_loads_kernel(
         for t in range(PACK):
             for u in range(2):
                 empty_basin(1, t, u)
-        nc.scalar.activation(inverse0[:, 1, :], root0[:, 1, :], ACT.Square)
+        gpsimd_square(inverse0[:, 1, :], root0[:, 1, :])
         for t in range(2, PACK):
             nc.scalar.activation(
                 root0[:, t, :], squared0[t][:], ACT.Abs_reciprocal_sqrt, bias=1.0, scale=inverse_kap[:, t - 2 : t - 1]
@@ -434,12 +436,24 @@ def tile_list_subcatchment_nitrate_loads_kernel(
         last_squares1(1, 0)
         last_squares1(1, 1)
 
+        def finish_block1(half):
+            z_w[1, half] = keep.tile([P, HALF], U32, name="z_w1%d" % half, align_bytes=64)
+            z_s[1, half] = keep.tile([P, HALF], U8, name="z_s1%d" % half, align_bytes=64)
+            parts = [placed("z_part%d%d" % (half, i), [P, P, PACK], BF16, AT_Z + KIB * (2 * half + i)) for i in range(2)]
+            for i in range(2):
+                src = by_lines(inverse1[half][:, :, i * P : (i + 1) * P])
+                nc.vector.tensor_scalar_max(out=parts[i][:].rearrange("p (c i) t -> p c t i", i=4), in0=src, scalar1=0.0)
+            for i in range(2):
+                nc.vector.quantize_mx(
+                    out=z_w[1, half][:, i * P : (i + 1) * P].bitcast(FP8X4), scales=z_s[1, half][:, i * P : (i + 1) * P],
+                    in_=parts[i][:].rearrange("p m t -> p (m t)"),
+                )
+
         group_z(0, 0)
         ratio(0, range(PACK))
         quantise_z(0, 0)
-        group_z(1, 0)
+        finish_block1(0)
         group_z(0, 1)
-        quantise_z(1, 0)
         first = [bank(pair) for pair in range(tiles_n // 2)]
 
         def first_place(c):
@@ -451,17 +465,7 @@ def tile_list_subcatchment_nitrate_loads_kernel(
                     score_pass(first_place(2 * pair + j), 0, 2 * pair + j, blk, (blk, j) == (0, 0), (blk, j) == (1, 1))
         ratio(1, range(PACK))
         quantise_z(0, 1)
-        z_w[1, 1] = keep.tile([P, HALF], U32, name="z_w11", align_bytes=64)
-        z_s[1, 1] = keep.tile([P, HALF], U8, name="z_s11", align_bytes=64)
-        last = [keep.tile([P, P, PACK], BF16, name="z_last%d" % i, align_bytes=64) for i in range(2)]
-        for i in range(2):
-            src = by_lines(inverse1[1][:, :, i * P : (i + 1) * P])
-            nc.vector.tensor_scalar_max(out=last[i][:].rearrange("p (c i) t -> p c t i", i=4), in0=src, scalar1=0.0)
-        for i in range(2):
-            nc.vector.quantize_mx(
-                out=z_w[1, 1][:, i * P : (i + 1) * P].bitcast(FP8X4), scales=z_s[1, 1][:, i * P : (i + 1) * P],
-                in_=last[i][:].rearrange("p m t -> p (m t)"),
-            )
+        finish_block1(1)
         for pair in range(tiles_n // 2):
             res = keep.tile([P, 2, HALF], F32, name="res_first%d" % pair)
             for j in range(2):

@@ -193,7 +193,8 @@ def tile_list_subcatchment_nitrate_loads_kernel(
             nc.vector.tensor_copy(picked0[t][:], h[0, t][:].indirect(pos_t[:]))
             if t < PACK - 1:
                 squared0[t] = keep.tile([P, M], F32, name="squared0%d" % t)
-                gpsimd_square(squared0[t][:], picked0[t][:])
+                cols = slice(0, HALF if t == PACK - 2 else M)
+                gpsimd_square(squared0[t][:, cols], picked0[t][:, cols])
 
         picked1, squared1 = {}, {}
 
@@ -396,6 +397,7 @@ def tile_list_subcatchment_nitrate_loads_kernel(
         inverse0 = keep.tile([P, PACK, M], F32, name="inverse0")
         for t in range(2):
             inverse_root(root0[:, t, :], squared0[t][:], 0, t)
+        nc.scalar.activation(squared0[PACK - 2][:, HALF:M], picked0[PACK - 2][:, HALF:M], ACT.Square)
         nc.scalar.activation(inverse0[:, 0, :], root0[:, 0, :], ACT.Square)
         for t in range(PACK):
             for u in range(2):

@@ -25,7 +25,8 @@ LIST_ROWS = 16
 SCALE_ROWS = 16
 KIB = 1024
 HALF = M // 2
-TAB_ROWS, LATE_ROWS = 64, 40
+TAB_ROWS, LATE_ROWS = 32, 16
+ROW_STEP = 2
 V_PLANE, W8_PLANE = 8, 4
 
 AT_W1 = (0, 8 * KIB)
@@ -66,7 +67,7 @@ def tile_list_subcatchment_nitrate_loads_kernel(
         def load_scale_rows(dst, src, base):
             passes = src.shape[0]
             nc.sync.dma_start(
-                out=dst[base : base + SCALE_ROWS * passes, :].bitcast(I32),
+                out=dst[base : base + ROW_STEP * SCALE_ROWS * passes : ROW_STEP, :].bitcast(I32),
                 in_=src.rearrange("a q n -> q a n").bitcast(I32),
             )
 
@@ -75,7 +76,7 @@ def tile_list_subcatchment_nitrate_loads_kernel(
             for g in (0, 2, 1, 3):
                 nc.sync.dma_start(
                     out=planes[32 * g + first : 32 * g + first + 4].bitcast(I32),
-                    in_=src[base + 4 * passes * g : base + 4 * passes * (g + 1), :].bitcast(I32),
+                    in_=src[base + ROW_STEP * 4 * passes * g : base + ROW_STEP * 4 * passes * (g + 1) : ROW_STEP, :].bitcast(I32),
                 )
             return planes
 
@@ -91,19 +92,18 @@ def tile_list_subcatchment_nitrate_loads_kernel(
         tab2_s = placed("tab2_s", [P, T2], U8, AT_TAB2_S)
         w4_s_raw = keep.tile([P, H], U8, name="w4_s_raw", align_bytes=64)
         rows = keep.tile([P, PASS], F32, name="rows")
+        nc.vector.memset(tab_s[:].bitcast(I32), 0)
         nc.vector.memset(rows[:], 0.0)
         nc.vector.memset(tab2_s[:].bitcast(I32), 0)
         nc.vector.memset(w4_s_raw[:].bitcast(I32), 0)
-        nc.vector.memset(tab_s[0:64, :].bitcast(I32), 0)
-        nc.vector.memset(tab_s[96:P, :].bitcast(I32), 0)
 
         offs_t = lists.tile([P, S // LIST_ROWS], U16, name="offs_t")
         pos_t = lists.tile([P, M // LIST_ROWS], U16, name="pos_t")
         offs2_t = lists.tile([P, M // LIST_ROWS], U16, name="offs2_t")
 
+        w1_raw = {(0, 0): load_w1(0, 0)}
         nc.sync.dma_start(offs_t[:], offs)
         load_scale_rows(tab_s, tab_scales, TAB_ROWS)
-        w1_raw = {(0, 0): load_w1(0, 0)}
         nc.sync.dma_start(offs2_t[:], offs2)
         nc.sync.dma_start(pos_t[:], pos1)
         w1_raw[1, 0] = load_w1(1, 0)

@@ -38,6 +38,9 @@ AT_LAST_SQUARE = 56 * KIB
 AT_LAST_GROUPED = 60 * KIB
 AT_V2_S_ROWS = 64 * KIB
 AT_Z = 68 * KIB
+AT_LATE_PICKS = 72 * KIB
+AT_W8_S_ROWS = AT_LATE_PICKS + 2 * KIB - 256
+W8_ROWS = 32
 
 
 def tile_list_subcatchment_nitrate_loads_kernel(
@@ -71,14 +74,16 @@ def tile_list_subcatchment_nitrate_loads_kernel(
                 in_=src.rearrange("a q n -> q a n").bitcast(I32),
             )
 
-        def to_planes(name, src, passes, base, first):
-            planes = keep.tile([P, passes, src.shape[1]], U8, name=name, align_bytes=64)
-            for g in (0, 2, 1, 3):
+        def plane_tile(name, passes, width):
+            return keep.tile([P, passes, width], U8, name=name, align_bytes=64)
+
+        def to_planes(planes, src, base, first, quadrants=(0, 2, 1, 3)):
+            passes = planes.shape[1]
+            for g in quadrants:
                 nc.sync.dma_start(
                     out=planes[32 * g + first : 32 * g + first + 4].bitcast(I32),
                     in_=src[base + ROW_STEP * 4 * passes * g : base + ROW_STEP * 4 * passes * (g + 1) : ROW_STEP, :].bitcast(I32),
                 )
-            return planes
 
         def load_w1(a, blk):
             raw = placed("w1_raw%d%d" % (a, blk), [P, PACK, PASS], F32, AT_W1[a])
@@ -107,6 +112,8 @@ def tile_list_subcatchment_nitrate_loads_kernel(
         nc.sync.dma_start(offs2_t[:], offs2)
         nc.sync.dma_start(pos_t[:], pos1)
         w1_raw[1, 0] = load_w1(1, 0)
+        w8_s_rows = placed("w8_s_rows", [P, N], U8, AT_W8_S_ROWS)
+        load_scale_rows(w8_s_rows, w8_scales, W8_ROWS)
         tab_w = [load_words("tab_w0", tab_words[0], AT_TAB[0])]
         load_scale_rows(tab2_s, tab2_scales, LATE_ROWS)
         load_scale_rows(w4_s_raw, w4_scales, LATE_ROWS)
@@ -120,7 +127,8 @@ def tile_list_subcatchment_nitrate_loads_kernel(
 
         v_s_rows = keep.tile([P, S], U8, name="v_s_rows", align_bytes=64)
         nc.vector.tensor_copy(v_s_rows[:], tab_s[:].indirect(offs_t[:]))
-        v_s = to_planes("v_s", v_s_rows[:], n1, TAB_ROWS, V_PLANE)
+        v_s = plane_tile("v_s", n1, S)
+        to_planes(v_s, v_s_rows[:], TAB_ROWS, V_PLANE)
         tab_w.append(load_words("tab_w1", tab_words[1], AT_TAB[1]))
 
         by_slot = bank(6)
@@ -201,19 +209,18 @@ def tile_list_subcatchment_nitrate_loads_kernel(
         def pick1(half, t):
             pair, j = divmod(t, 2)
             name = "picked1_%d%d" % (half, pair)
-            if j == 0:
-                if half == 1:
-                    picked1[half, pair] = placed(name, [P, 2, HALF], F32, AT_TAB2[2] + 2 * KIB * pair)
-                elif pair == 0:
-                    picked1[half, pair] = placed(name, [P, 2, HALF], F32, AT_V2_S_ROWS)
-                else:
-                    picked1[half, pair] = placed(name, [P, 2, HALF], F32, AT_TAB2[2] + 4 * KIB)
+            if (half, t) == (1, 0):
+                second_half = placed("picked1_late", [P, PACK, HALF], F32, AT_LATE_PICKS + 2 * KIB)
+                for i in range(2):
+                    picked1[half, i] = second_half[:, 2 * i : 2 * i + 2, :]
+            elif (half, j) == (0, 0):
+                picked1[half, pair] = placed(name, [P, 2, HALF], F32, (AT_V2_S_ROWS, AT_LATE_PICKS)[pair])[:]
             entries = pos_t[:, half * HALF // LIST_ROWS : (half + 1) * HALF // LIST_ROWS]
             nc.vector.tensor_copy(picked1[half, pair][:, j, :], h[1, t][:].indirect(entries))
             if j == 1:
                 if (half, pair) != (1, 1):
                     squared1[half, pair] = keep.tile([P, 2, HALF], F32, name="squared1_%d%d" % (half, pair))
-                    gpsimd_square(squared1[half, pair][:], picked1[half, pair][:])
+                    gpsimd_square(squared1[half, pair][:], picked1[half, pair])
 
         v2_w, own, own_bank, tab2_w = {}, {}, {}, {}
 
@@ -326,9 +333,6 @@ def tile_list_subcatchment_nitrate_loads_kernel(
         nc.scalar.copy(out=by_row[:], in_=slot_rows[:, :, 0:b3_row])
         nc.scalar.copy(out=b3_t[:], in_=by_tile[:, b3_row : b3_row + tiles_n])
         nc.vector.tensor_copy(v_w[0][:], tab_w[0][:].bitcast(U32).indirect(offs_t[:]))
-        w4_raw = placed("w4_raw", [P, n2, H // 2], I32, AT_W4_RAW)
-        nc.sync.dma_start(out=w4_raw[:], in_=w4_words.rearrange("a p n -> p a n").bitcast(I32))
-        tab2_w[0] = load_words("tab2_w0", tab2_words[0], AT_TAB2[0])
         order0 = [(2 * pair + j, u) for pair in range(2) for u in range(2) for j in range(2)]
         for t, u in order0:
             basin_pass(0, t, u, 0)
@@ -337,29 +341,34 @@ def tile_list_subcatchment_nitrate_loads_kernel(
             out=w4_s_rows[:].rearrange("p (b t c i) -> p b c t i", t=PACK, c=8, i=16),
             in_=w4_s_raw[:].rearrange("p (b c i t) -> p b c t i", t=PACK, c=8, i=16),
         )
-        w4_s = to_planes("w4_s", w4_s_rows[:], n2, LATE_ROWS, 0)
         v2_s_rows = placed("v2_s_rows", [P, M], U8, AT_V2_S_ROWS)
         nc.vector.tensor_copy(v2_s_rows[:], tab2_s[:].indirect(offs2_t[:]))
+        v2_s = plane_tile("v2_s", n2, M)
+        w4_s = plane_tile("w4_s", n2, H)
+        w4_raw = placed("w4_raw", [P, n2, H // 2], I32, AT_W4_RAW)
+        nc.sync.dma_start(out=w4_raw[:], in_=w4_words.rearrange("a p n -> p a n").bitcast(I32))
+        to_planes(v2_s, v2_s_rows[:], LATE_ROWS, 0, (0, 2, 1))
+        to_planes(w4_s, w4_s_rows[:], LATE_ROWS, 0, (0, 2))
+        tab2_w[0] = load_words("tab2_w0", tab2_words[0], AT_TAB2[0])
+        to_planes(w4_s, w4_s_rows[:], LATE_ROWS, 0, (1,))
         tab2_w[1] = load_words("tab2_w1", tab2_words[1], AT_TAB2[1])
-        v2_s = to_planes("v2_s", v2_s_rows[:], n2, LATE_ROWS, 0)
+        to_planes(v2_s, v2_s_rows[:], LATE_ROWS, 0, (3,))
+        to_planes(w4_s, w4_s_rows[:], LATE_ROWS, 0, (3,))
+        w8_s = keep.tile([P, n3, N], U8, name="w8_s", align_bytes=64)
+        to_planes(w8_s, w8_s_rows[:], W8_ROWS, W8_PLANE, (0, 2, 1))
         for u in range(2):
             entries = offs_t[:, u * BANK // LIST_ROWS : (u + 1) * BANK // LIST_ROWS]
             nc.vector.tensor_copy(v_w[1][:, u * BANK : (u + 1) * BANK], tab_w[1][:].bitcast(U32).indirect(entries))
         for t, u in order0:
             basin_pass(0, t, u, 1)
         tab2_w[2] = load_words("tab2_w2", tab2_words[2], AT_TAB2[2])
+        to_planes(w8_s, w8_s_rows[:], W8_ROWS, W8_PLANE, (3,))
         for t, u in order0:
             empty_basin(0, t, u)
 
         cast_w1(0, 1, True)
         w8_w = placed("w8_w", [P, n3, N], I32, AT_W1[0])
         nc.sync.dma_start(out=w8_w[:], in_=w8_words.rearrange("a p n t -> p a (n t)").bitcast(I32))
-        w8_s = placed("w8_s", [P, n3, N], U8, AT_W1[0] + 6 * KIB)
-        for g in (0, 2, 1, 3):
-            nc.sync.dma_start(
-                out=w8_s[32 * g + W8_PLANE : 32 * g + W8_PLANE + 4].bitcast(I32),
-                in_=w8_scales[:, 4 * g : 4 * g + 4, :].rearrange("a i n -> i a n").bitcast(I32),
-            )
         pick0(0)
         quantise_w1(0, 1)
         pick0(1)
@@ -432,7 +441,7 @@ def tile_list_subcatchment_nitrate_loads_kernel(
         last_squares1(0, 1)
         numerator(0, 1, range(PACK))
         squared1[1, 1] = placed("squared1_11", [P, 2, HALF], F32, AT_LAST_SQUARE)
-        nc.scalar.activation(squared1[1, 1][:], picked1[1, 1][:], ACT.Square)
+        nc.scalar.activation(squared1[1, 1][:], picked1[1, 1], ACT.Square)
         inverse_roots1(1, 0)
         inverse_roots1(1, 1)
         last_squares1(1, 0)

from contextlib import ExitStack

import concourse.mybir as mybir
from concourse.masks import make_identity

K, K2, H, N, T, T2, S, M = 1024, 1536, 1024, 768, 4096, 2048, 1024, 512
FLOPS = 2 * (K * H * S + K2 * H * M + H * N * M)

F32 = mybir.dt.float32
BF16 = mybir.dt.bfloat16
I32 = mybir.dt.int32
U32 = mybir.dt.uint32
U16 = mybir.dt.uint16
U8 = mybir.dt.uint8
FP8X4 = mybir.dt.float8_e4m3fn_x4
FP4X4 = mybir.dt.float4_e2m1fn_x4
ACT = mybir.ActivationFunctionType
ALU = mybir.AluOpType

P = 128
PACK = 4
PASS = P * PACK
BANK = 512
LIST_ROWS = 16
SCALE_ROWS = 16
KIB = 1024
HALF = M // 2
TAB_ROWS, LATE_ROWS = 32, 16
ROW_STEP = 2
V_PLANE, W8_PLANE = 8, 4

AT_W1 = (0, 8 * KIB)
AT_TAB = (16 * KIB, 32 * KIB)
AT_TAB2_S = 48 * KIB
AT_TAB2 = (AT_TAB[0], AT_TAB2_S, AT_TAB[1])
AT_W4_RAW = AT_TAB[0] + 8 * KIB
AT_LAST_SQUARE = 56 * KIB
AT_LAST_GROUPED = 60 * KIB
AT_V2_S_ROWS = 64 * KIB
AT_Z = 68 * KIB
AT_LATE_PICKS = 72 * KIB
AT_W8_S_ROWS = AT_LATE_PICKS + 2 * KIB - 256
W8_ROWS = 32


def tile_list_subcatchment_nitrate_loads_kernel(
    tc, tab_words, tab_scales, offs, pos1, tab2_words, tab2_scales, offs2, w1,
    w4_words, w4_scales, w8_words, w8_scales, b2, kap, b3, out
):
    nc = tc.nc
    n1, n2, n3 = K // PASS, K2 // PASS, H // PASS
    tiles_n = N // P
    with ExitStack() as ctx:
        lists = ctx.enter_context(tc.tile_pool(name="lists", bufs=1))
        keep = ctx.enter_context(tc.tile_pool(name="keep", bufs=1))
        stage = ctx.enter_context(tc.tile_pool(name="stage", bufs=1))
        psum = ctx.enter_context(tc.psum_pool(name="psum", bufs=1))

        def bank(i):
            return psum.tile([P, BANK], F32, name="bank%d" % i)

        def placed(name, shape, dtype, offset):
            return stage.tile(shape, dtype, name=name, align_bytes=64, offset=offset)

        def load_words(name, src, offset):
            words = placed(name, [P, src.shape[1]], I32, offset)
            nc.sync.dma_start(out=words[:], in_=src.rearrange("p n t -> p (n t)").bitcast(I32))
            return words

        def load_scale_rows(dst, src, base):
            passes = src.shape[0]
            nc.sync.dma_start(
                out=dst[base : base + ROW_STEP * SCALE_ROWS * passes : ROW_STEP, :].bitcast(I32),
                in_=src.rearrange("a q n -> q a n").bitcast(I32),
            )

        def plane_tile(name, passes, width):
            return keep.tile([P, passes, width], U8, name=name, align_bytes=64)

        def to_planes(planes, src, base, first, quadrants=(0, 2, 1, 3)):
            passes = planes.shape[1]
            for g in quadrants:
                nc.sync.dma_start(
                    out=planes[32 * g + first : 32 * g + first + 4].bitcast(I32),
                    in_=src[base + ROW_STEP * 4 * passes * g : base + ROW_STEP * 4 * passes * (g + 1) : ROW_STEP, :].bitcast(I32),
                )

        def load_w1(a, blk):
            raw = placed("w1_raw%d%d" % (a, blk), [P, PACK, PASS], F32, AT_W1[a])
            nc.sync.dma_start(
                out=raw[:],
                in_=w1[a * PASS : (a + 1) * PASS, blk * PASS : (blk + 1) * PASS].rearrange("(p j) c -> p j c", j=PACK),
            )
            return raw

        tab_s = placed("tab_s", [P, T], U8, AT_TAB[1])
        tab2_s = placed("tab2_s", [P, T2], U8, AT_TAB2_S)
        w4_s_raw = keep.tile([P, H], U8, name="w4_s_raw", align_bytes=64)
        rows = keep.tile([P, PASS], F32, name="rows")
        nc.vector.memset(tab_s[:].bitcast(I32), 0)
        nc.vector.memset(rows[:], 0.0)
        nc.vector.memset(tab2_s[:].bitcast(I32), 0)
        nc.vector.memset(w4_s_raw[:].bitcast(I32), 0)

        offs_t = lists.tile([P, S // LIST_ROWS], U16, name="offs_t")
        pos_t = lists.tile([P, M // LIST_ROWS], U16, name="pos_t")
        offs2_t = lists.tile([P, M // LIST_ROWS], U16, name="offs2_t")

        w1_raw = {(0, 0): load_w1(0, 0)}
        nc.sync.dma_start(offs_t[:], offs)
        load_scale_rows(tab_s, tab_scales, TAB_ROWS)
        nc.sync.dma_start(offs2_t[:], offs2)
        nc.sync.dma_start(pos_t[:], pos1)
        w1_raw[1, 0] = load_w1(1, 0)
        w8_s_rows = placed("w8_s_rows", [P, N], U8, AT_W8_S_ROWS)
        load_scale_rows(w8_s_rows, w8_scales, W8_ROWS)
        tab_w = [load_words("tab_w0", tab_words[0], AT_TAB[0])]
        load_scale_rows(tab2_s, tab2_scales, LATE_ROWS)
        load_scale_rows(w4_s_raw, w4_scales, LATE_ROWS)

        b2_row, b3_row = n3, 2 * n3
        nc.gpsimd.dma_start(out=rows[0:b2_row, :], in_=kap.rearrange("(b c) -> b c", b=n3))
        nc.gpsimd.dma_start(out=rows[b2_row:b3_row, :], in_=b2.rearrange("(b c) -> b c", b=n3))
        nc.gpsimd.dma_start(out=rows[b3_row : b3_row + tiles_n, 0:P], in_=b3.rearrange("(c p) -> c p", p=P))
        identity = keep.tile([P, P], F32, name="identity")
        make_identity(nc, identity[:])

        v_s_rows = keep.tile([P, S], U8, name="v_s_rows", align_bytes=64)
        nc.vector.tensor_copy(v_s_rows[:], tab_s[:].indirect(offs_t[:]))
        v_s = plane_tile("v_s", n1, S)
        to_planes(v_s, v_s_rows[:], TAB_ROWS, V_PLANE)
        tab_w.append(load_words("tab_w1", tab_words[1], AT_TAB[1]))

        by_slot = bank(6)
        for t in range(PACK):
            nc.tensor.transpose(by_slot[:, t * P : (t + 1) * P], rows[:, t:PASS:PACK], identity[:])
        by_tile = bank(7)
        nc.tensor.transpose(by_tile[:, 0:P], rows[:, 0:P], identity[:])
        slot_rows = by_slot[:].rearrange("p (t r) -> p t r", t=PACK)
        by_row = keep.tile([P, PACK, b3_row], F32, name="by_row")
        b3_t = keep.tile([P, tiles_n], F32, name="b3_t")

        def kap_of(blk, t):
            return by_row[:, t, blk : blk + 1]

        def b2_of(blk, t):
            return by_row[:, t, b2_row + blk : b2_row + blk + 1]

        grouped, w1_w, w1_s = {}, {}, {}

        def cast_w1(a, blk, on_vector):
            name = "w1_grouped%d%d" % (a, blk)
            if (a, blk) == (1, 1):
                grouped[a, blk] = placed(name, [P, PACK, P, PACK], BF16, AT_LAST_GROUPED)
            else:
                grouped[a, blk] = keep.tile([P, PACK, P, PACK], BF16, name=name, align_bytes=64)
            src = w1_raw[a, blk][:].rearrange("p j (m t) -> p m j t", t=PACK)
            dst = grouped[a, blk][:].rearrange("p t m j -> p m j t")
            if on_vector:
                nc.vector.tensor_copy(out=dst, in_=src)
            else:
                nc.scalar.copy(out=dst, in_=src)

        def quantise_w1(a, blk):
            w1_w[a, blk] = keep.tile([P, PASS], U32, name="w1_w%d%d" % (a, blk), align_bytes=64)
            w1_s[a, blk] = keep.tile([P, PASS], U8, name="w1_s%d%d" % (a, blk), align_bytes=64)
            nc.vector.quantize_mx(
                out=w1_w[a, blk][:].bitcast(FP8X4), scales=w1_s[a, blk][:],
                in_=grouped[a, blk][:].rearrange("p t m j -> p (t m j)"),
            )

        v_w = [keep.tile([P, S], U32, name="v_w%d" % a, align_bytes=64) for a in range(n1)]
        h, acc = {}, {}

        def basin_pass(blk, t, u, a):
            if a == 0:
                acc[blk, t, u] = bank(2 * t + u)
            cols = slice(t * P, (t + 1) * P)
            run = slice(u * BANK, (u + 1) * BANK)
            nc.tensor.matmul_mx(
                out=acc[blk, t, u][:], lhsT=w1_w[a, blk][:, cols].bitcast(FP8X4), lhsT_scale=w1_s[a, blk][:, cols],
                rhs=v_w[a][:, run].bitcast(FP8X4), rhs_scale=v_s[V_PLANE:P, a, run],
                start=(a == 0), stop=(a == n1 - 1),
            )

        def empty_basin(blk, t, u):
            if u == 0:
                h[blk, t] = keep.tile([P, S], F32, name="h%d%d" % (blk, t), align_bytes=64)
            nc.scalar.copy(out=h[blk, t][:, u * BANK : (u + 1) * BANK], in_=acc[blk, t, u][:])

        def gpsimd_square(dst, src):
            nc.gpsimd.tensor_tensor(out=dst, in0=src, in1=src, op=ALU.mult)

        def inverse_root(dst, src, blk, t):
            nc.scalar.activation(dst, src, ACT.Abs_reciprocal_sqrt, bias=kap_of(blk, t))

        picked0, squared0 = {}, {}

        def pick0(t):
            picked0[t] = keep.tile([P, M], F32, name="picked0%d" % t)
            nc.vector.tensor_copy(picked0[t][:], h[0, t][:].indirect(pos_t[:]))
            if t < PACK - 1:
                squared0[t] = keep.tile([P, M], F32, name="squared0%d" % t)
                cols = slice(0, HALF if t == PACK - 2 else M)
                gpsimd_square(squared0[t][:, cols], picked0[t][:, cols])

        picked1, squared1 = {}, {}

        def pick1(half, t):
            pair, j = divmod(t, 2)
            name = "picked1_%d%d" % (half, pair)
            if (half, t) == (1, 0):
                second_half = placed("picked1_late", [P, PACK, HALF], F32, AT_LATE_PICKS + 2 * KIB)
                for i in range(2):
                    picked1[half, i] = second_half[:, 2 * i : 2 * i + 2, :]
            elif (half, j) == (0, 0):
                picked1[half, pair] = placed(name, [P, 2, HALF], F32, (AT_V2_S_ROWS, AT_LATE_PICKS)[pair])[:]
            entries = pos_t[:, half * HALF // LIST_ROWS : (half + 1) * HALF // LIST_ROWS]
            nc.vector.tensor_copy(picked1[half, pair][:, j, :], h[1, t][:].indirect(entries))
            if j == 1:
                if (half, pair) != (1, 1):
                    squared1[half, pair] = keep.tile([P, 2, HALF], F32, name="squared1_%d%d" % (half, pair))
                    gpsimd_square(squared1[half, pair][:], picked1[half, pair])

        v2_w, own, own_bank, tab2_w = {}, {}, {}, {}

        def gather_v2(a):
            name = "v2_w%d" % a
            v2_w[a] = placed(name, [P, M], U32, AT_W1[1]) if a == 0 else keep.tile([P, M], U32, name=name, align_bytes=64)
            parts = 2 if a == n2 - 1 else 1
            width = M // parts
            for i in range(parts):
                entries = offs2_t[:, i * width // LIST_ROWS : (i + 1) * width // LIST_ROWS]
                nc.vector.tensor_copy(v2_w[a][:, i * width : (i + 1) * width], tab2_w[a][:].bitcast(U32).indirect(entries))

        def own_pass(blk, half, t, a, order):
            pair, j = divmod(t, 2)
            if (a, j) == (order[0], 0):
                own_bank[blk, half, pair] = bank(4 * half + 2 * blk + pair)
            own[blk, half, t] = own_bank[blk, half, pair][:, j * HALF : (j + 1) * HALF]
            c0 = blk * PASS + t * P
            run = slice(half * HALF, (half + 1) * HALF)
            nc.tensor.matmul_mx(
                out=own[blk, half, t], lhsT=w4_w[blk, a][:, 2 * t * P : 2 * (t + 1) * P].bitcast(FP4X4),
                lhsT_scale=w4_s[:, a, c0 : c0 + P],
                rhs=v2_w[a][:, run].bitcast(FP8X4), rhs_scale=v2_s[:, a, run],
                start=(a, j) == (order[0], 0), stop=(a, j) == (order[-1], 1),
            )

        inverse1 = [keep.tile([P, PACK, HALF], F32, name="inverse1_%d" % half) for half in range(2)]
        top = {unit: keep.tile([P, PACK, HALF], F32, name="top%d%d" % unit) for unit in ((0, 0), (0, 1))}

        root1 = {}

        def inverse_roots1(half, pair):
            name = "root1_%d%d" % (half, pair)
            if (half, pair) == (0, 1):
                root1[half, pair] = placed(name, [P, 2, HALF], F32, AT_LAST_SQUARE)
            else:
                root1[half, pair] = keep.tile([P, 2, HALF], F32, name=name)
            for j in range(2):
                inverse_root(root1[half, pair][:, j, :], squared1[half, pair][:, j, :], 1, 2 * pair + j)

        def last_squares1(half, pair):
            for j in range(2):
                nc.scalar.activation(inverse1[half][:, 2 * pair + j, :], root1[half, pair][:, j, :], ACT.Square)

        def numerator(blk, half, ts):
            for t in ts:
                src = own[blk, half, t]
                nc.scalar.activation(top[blk, half][:, t, :], src, ACT.Relu, bias=b2_of(blk, t))

        def ratio(half, ts):
            for t in ts:
                x = inverse1[half][:, t, :]
                nc.vector.scalar_tensor_tensor(
                    out=x, in0=own[1, half, t], scalar=b2_of(1, t), in1=x,
                    op0=ALU.add, op1=ALU.mult,
                )

        z_grouped, z_w, z_s = {}, {}, {}

        def by_lines(x):
            return x.rearrange("p t (c i) -> p c t i", i=4)

        def group_z(blk, half):
            name = "z_grouped%d%d" % (blk, half)
            if half == 0:
                z_grouped[blk, half] = keep.tile([P, HALF, PACK], BF16, name=name, align_bytes=64)
            else:
                z_grouped[blk, half] = placed(name, [P, HALF, PACK], BF16, AT_Z - KIB - KIB // 2)
            dst = z_grouped[blk, half][:].rearrange("p (c i) t -> p c t i", i=4)
            src = inverse0[:, :, half * HALF : (half + 1) * HALF]
            nc.vector.tensor_tensor(out=dst, in0=by_lines(src), in1=by_lines(top[blk, half][:]), op=ALU.mult)

        def quantise_z(blk, half):
            z_w[blk, half] = keep.tile([P, HALF], U32, name="z_w%d%d" % (blk, half), align_bytes=64)
            z_s[blk, half] = keep.tile([P, HALF], U8, name="z_s%d%d" % (blk, half), align_bytes=64)
            nc.vector.quantize_mx(
                out=z_w[blk, half][:].bitcast(FP8X4), scales=z_s[blk, half][:],
                in_=z_grouped[blk, half][:].rearrange("p m t -> p (m t)"),
            )

        def score_pass(dst, half, c, blk, start, stop):
            cols = slice(c * P, (c + 1) * P)
            nc.tensor.matmul_mx(
                out=dst, lhsT=w8_w[:, blk, cols].bitcast(FP8X4), lhsT_scale=w8_s[W8_PLANE:P, blk, cols],
                rhs=z_w[blk, half][:].bitcast(FP8X4), rhs_scale=z_s[blk, half][:], start=start, stop=stop,
            )

        def add_bias(res, src, c, on_vector):
            if on_vector:
                nc.vector.tensor_scalar_add(out=res, in0=src, scalar1=b3_t[:, c : c + 1])
            else:
                nc.scalar.activation(res, src, ACT.Identity, bias=b3_t[:, c : c + 1])

        def store_pair(res, pair, half):
            nc.sync.dma_start(
                out=out[2 * pair * P : 2 * (pair + 1) * P, half * HALF : (half + 1) * HALF].rearrange("(j p) m -> p j m", p=P),
                in_=res[:],
            )

        cast_w1(0, 0, False)
        w1_raw[0, 1] = load_w1(0, 1)
        quantise_w1(0, 0)
        cast_w1(1, 0, False)
        w1_raw[1, 1] = load_w1(1, 1)
        quantise_w1(1, 0)
        root_kap = keep.tile([P, 2], F32, name="root_kap")
        inverse_kap = keep.tile([P, 2], F32, name="inverse_kap")
        nc.scalar.activation(root_kap[:], slot_rows[:, 2:PACK, 0], ACT.Abs_reciprocal_sqrt)
        nc.scalar.activation(inverse_kap[:], root_kap[:], ACT.Square)
        nc.scalar.copy(out=by_row[:], in_=slot_rows[:, :, 0:b3_row])
        nc.scalar.copy(out=b3_t[:], in_=by_tile[:, b3_row : b3_row + tiles_n])
        nc.vector.tensor_copy(v_w[0][:], tab_w[0][:].bitcast(U32).indirect(offs_t[:]))
        order0 = [(2 * pair + j, u) for pair in range(2) for u in range(2) for j in range(2)]
        for t, u in order0:
            basin_pass(0, t, u, 0)
        w4_s_rows = keep.tile([P, H], U8, name="w4_s_rows", align_bytes=64)
        nc.vector.tensor_copy(
            out=w4_s_rows[:].rearrange("p (b t c i) -> p b c t i", t=PACK, c=8, i=16),
            in_=w4_s_raw[:].rearrange("p (b c i t) -> p b c t i", t=PACK, c=8, i=16),
        )
        v2_s_rows = placed("v2_s_rows", [P, M], U8, AT_V2_S_ROWS)
        nc.vector.tensor_copy(v2_s_rows[:], tab2_s[:].indirect(offs2_t[:]))
        v2_s = plane_tile("v2_s", n2, M)
        w4_s = plane_tile("w4_s", n2, H)
        w4_raw = placed("w4_raw", [P, n2, H // 2], I32, AT_W4_RAW)
        nc.sync.dma_start(out=w4_raw[:], in_=w4_words.rearrange("a p n -> p a n").bitcast(I32))
        to_planes(v2_s, v2_s_rows[:], LATE_ROWS, 0, (0, 2, 1))
        to_planes(w4_s, w4_s_rows[:], LATE_ROWS, 0, (0, 2))
        tab2_w[0] = load_words("tab2_w0", tab2_words[0], AT_TAB2[0])
        to_planes(w4_s, w4_s_rows[:], LATE_ROWS, 0, (1,))
        tab2_w[1] = load_words("tab2_w1", tab2_words[1], AT_TAB2[1])
        to_planes(v2_s, v2_s_rows[:], LATE_ROWS, 0, (3,))
        to_planes(w4_s, w4_s_rows[:], LATE_ROWS, 0, (3,))
        w8_s = keep.tile([P, n3, N], U8, name="w8_s", align_bytes=64)
        to_planes(w8_s, w8_s_rows[:], W8_ROWS, W8_PLANE, (0, 2, 1))
        for u in range(2):
            entries = offs_t[:, u * BANK // LIST_ROWS : (u + 1) * BANK // LIST_ROWS]
            nc.vector.tensor_copy(v_w[1][:, u * BANK : (u + 1) * BANK], tab_w[1][:].bitcast(U32).indirect(entries))
        for t, u in order0:
            basin_pass(0, t, u, 1)
        tab2_w[2] = load_words("tab2_w2", tab2_words[2], AT_TAB2[2])
        to_planes(w8_s, w8_s_rows[:], W8_ROWS, W8_PLANE, (3,))
        for t, u in order0:
            empty_basin(0, t, u)

        cast_w1(0, 1, True)
        w8_w = placed("w8_w", [P, n3, N], I32, AT_W1[0])
        nc.sync.dma_start(out=w8_w[:], in_=w8_words.rearrange("a p n t -> p a (n t)").bitcast(I32))
        pick0(0)
        quantise_w1(0, 1)
        pick0(1)
        cast_w1(1, 1, False)
        pick0(2)
        pick0(3)
        quantise_w1(1, 1)
        for t in range(PACK):
            for u in range(2):
                for a in range(n1):
                    basin_pass(1, t, u, a)
        w4_early = placed("w4_early", [P, n2 - 1, 2 * H], U8, AT_W1[1] + 2 * KIB)
        nc.vector.tensor_copy(
            out=w4_early[:].bitcast(U16).rearrange("p a (b t m) -> p (a b) m t", t=PACK, m=P),
            in_=w4_raw[:, 0 : n2 - 1, :].bitcast(U16).rearrange("p a (b m t) -> p (a b) m t", t=PACK, m=P),
        )
        w4_w = {(blk, a): w4_early[:, a, 2 * blk * PASS : 2 * (blk + 1) * PASS] for blk in range(n3) for a in range(n2 - 1)}

        def deal_last_pass(blk, offset):
            words = placed("w4_last%d" % blk, [P, 2 * PASS], U8, offset)
            src = w4_raw[:].bitcast(U8)[:, n2 - 1, 2 * blk * PASS : 2 * (blk + 1) * PASS]
            nc.gpsimd.tensor_copy(
                out=words[:].rearrange("p (t m e) -> p t m e", t=PACK, e=2),
                in_=src.rearrange("p (m t e) -> p t m e", t=PACK, e=2),
            )
            w4_w[blk, n2 - 1] = words[:]

        gather_v2(0)
        squared0[PACK - 1] = placed("squared03", [P, M], F32, AT_LAST_GROUPED)
        gpsimd_square(squared0[PACK - 1][:], picked0[PACK - 1][:])
        for blk in range(n3):
            deal_last_pass(blk, AT_LAST_GROUPED + (2 + blk) * KIB)

        root0 = keep.tile([P, PACK, M], F32, name="root0")
        inverse0 = keep.tile([P, PACK, M], F32, name="inverse0")
        for t in range(2):
            inverse_root(root0[:, t, :], squared0[t][:], 0, t)
        nc.scalar.activation(squared0[PACK - 2][:, HALF:M], picked0[PACK - 2][:, HALF:M], ACT.Square)
        nc.scalar.activation(inverse0[:, 0, :], root0[:, 0, :], ACT.Square)
        for t in range(PACK):
            for u in range(2):
                empty_basin(1, t, u)
        gpsimd_square(inverse0[:, 1, :], root0[:, 1, :])
        for t in range(2, PACK):
            nc.scalar.activation(
                root0[:, t, :], squared0[t][:], ACT.Abs_reciprocal_sqrt, bias=1.0, scale=inverse_kap[:, t - 2 : t - 1]
            )
        for t in range(2, PACK):
            nc.scalar.activation(inverse0[:, t, :], root0[:, t, :], ACT.Square, scale=root_kap[:, t - 2 : t - 1])

        gather_v2(1)
        pick1(0, 0)
        pick1(0, 1)
        gather_v2(2)
        pick1(0, 2)
        pick1(0, 3)
        for t in range(PACK):
            pick1(1, t)
        for half in range(2):
            for blk in range(n3):
                order = (0, 2, 1) if half == 1 else (0, 1, 2)
                for a in order:
                    for t in range(PACK):
                        own_pass(blk, half, t, a, order)

        numerator(0, 0, range(PACK))
        inverse_roots1(0, 0)
        inverse_roots1(0, 1)
        last_squares1(0, 0)
        last_squares1(0, 1)
        numerator(0, 1, range(PACK))
        squared1[1, 1] = placed("squared1_11", [P, 2, HALF], F32, AT_LAST_SQUARE)
        nc.scalar.activation(squared1[1, 1][:], picked1[1, 1], ACT.Square)
        inverse_roots1(1, 0)
        inverse_roots1(1, 1)
        last_squares1(1, 0)
        last_squares1(1, 1)

        def finish_block1(half):
            z_w[1, half] = keep.tile([P, HALF], U32, name="z_w1%d" % half, align_bytes=64)
            z_s[1, half] = keep.tile([P, HALF], U8, name="z_s1%d" % half, align_bytes=64)
            parts = [placed("z_part%d%d" % (half, i), [P, P, PACK], BF16, AT_Z + KIB * (2 * half + i)) for i in range(2)]
            for i in range(2):
                src = by_lines(inverse1[half][:, :, i * P : (i + 1) * P])
                nc.vector.tensor_scalar_max(out=parts[i][:].rearrange("p (c i) t -> p c t i", i=4), in0=src, scalar1=0.0)
            for i in range(2):
                nc.vector.quantize_mx(
                    out=z_w[1, half][:, i * P : (i + 1) * P].bitcast(FP8X4), scales=z_s[1, half][:, i * P : (i + 1) * P],
                    in_=parts[i][:].rearrange("p m t -> p (m t)"),
                )

        group_z(0, 0)
        ratio(0, range(PACK))
        quantise_z(0, 0)
        finish_block1(0)
        group_z(0, 1)
        first = [bank(pair) for pair in range(tiles_n // 2)]

        def first_place(c):
            return first[c // 2][:, (c % 2) * HALF : (c % 2 + 1) * HALF]

        for pair in range(tiles_n // 2):
            for blk in range(n3):
                for j in range(2):
                    score_pass(first_place(2 * pair + j), 0, 2 * pair + j, blk, (blk, j) == (0, 0), (blk, j) == (1, 1))
        ratio(1, range(PACK))
        quantise_z(0, 1)
        finish_block1(1)
        for pair in range(tiles_n // 2):
            res = keep.tile([P, 2, HALF], F32, name="res_first%d" % pair)
            for j in range(2):
                add_bias(res[:, j, :], first_place(2 * pair + j), 2 * pair + j, False)
            store_pair(res, pair, 0)

        second = [bank((3 + c) % 8) for c in range(tiles_n)]
        for c in range(tiles_n):
            score_pass(second[c][:, 0:HALF], 1, c, 0, True, False)
        for pair in range(tiles_n // 2):
            res = keep.tile([P, 2, HALF], F32, name="res_second%d" % pair)
            for j in range(2):
                c = 2 * pair + j
                score_pass(second[c][:, 0:HALF], 1, c, 1, False, True)
                add_bias(res[:, j, :], second[c][:, 0:HALF], c, j == 0)
            store_pair(res, pair, 1)
